import numpy as np
import ml_dtypes


def mxq(x, axis, fmt="e4m3"):
    dtype, down = {"e4m3": (ml_dtypes.float8_e4m3fn, 7), "e5m2": (ml_dtypes.float8_e5m2, 14)}[fmt]
    v = np.moveaxis(np.asarray(x, np.float32).astype(ml_dtypes.bfloat16).astype(np.float64), axis, -1)
    blocks = v.reshape(v.shape[:-1] + (-1, 32))
    amax = np.abs(blocks).max(-1, keepdims=True)
    byte = np.maximum(np.where(amax > 0, np.frexp(amax)[1] - 1 + 127, 0) - down, 1)
    scale = np.exp2(byte - 127.0)
    codes = (blocks / scale).astype(np.float32).astype(dtype).astype(np.float64)
    return np.moveaxis((codes * scale).reshape(v.shape), -1, axis)


WIDE = False


def mx_kscale(k):
    if not WIDE:
        return np.ones(k)
    levels = np.array([10, -10, 5, -5, 0])
    if k % 512:
        return np.exp2(np.random.permutation(np.resize(levels, k // 32))).repeat(32)
    a = np.empty((k // 512, 16))
    for p in range(k // 512):
        a[p, :8] = np.random.permutation(np.resize(levels, 8))
        for g in range(8):
            far = levels[np.abs(levels - a[p, g]) >= 10]
            a[p, g + 8] = far[np.random.randint(len(far))]
    return np.exp2(a.ravel()).repeat(32)


def f64(x):
    return np.asarray(x).astype(np.float64)


def striped(idx):
    return np.tile(idx.reshape(-1, 16).T, (8, 1)).astype(np.uint16)


def unstriped(offs):
    return offs[:16].T.reshape(-1).astype(np.int64)


def pack_weight(w):
    k, n = w.shape
    w = f64(np.asarray(w, np.float32).astype(ml_dtypes.bfloat16)).reshape(k // 32, 32, n)
    amax = np.abs(w).max(1)
    byte = np.clip(np.where(amax > 0, np.frexp(amax)[1] - 1 + 127 - 7, 1), 1, 254)
    scaled = (w * np.exp2(127.0 - byte)[:, None, :]).reshape(k, n).astype(np.float32)
    words = np.ascontiguousarray(scaled.reshape(k // 512, 128, 4, n).transpose(0, 1, 3, 2)).astype(ml_dtypes.float8_e4m3fn).view(np.uint8)
    return words, np.ascontiguousarray(byte.astype(np.uint8).reshape(k // 512, 16, n))


def unpack_weight(words, scales):
    g, p, n, _ = words.shape
    vals = np.ascontiguousarray(words).view(ml_dtypes.float8_e4m3fn).astype(np.float64) * np.repeat(np.exp2(scales.astype(np.float64) - 127.0), 8, axis=1)[..., None]
    return vals.transpose(0, 1, 3, 2).reshape(g * 512, n)


def relu2(v):
    return np.maximum(v, 0.0) ** 2


K, T, S, H, D, W, U = 1024, 2048, 512, 512, 8, 2048, 1024


def setup_inputs():
    n = np.random.standard_normal
    s = mx_kscale(K)[:, None]
    u = mx_kscale(H)
    packed_xT = pack_weight(n((K, T)) * s)
    packed_eT = pack_weight(n((H, W)) / np.sqrt(H) / u[:, None])
    return {
        "x_words": packed_xT[0],
        "x_scales": packed_xT[1],
        "w1": (n((K, H)) / np.sqrt(K) / s * u).astype(np.float32),
        "e_words": packed_eT[0],
        "e_scales": packed_eT[1],
        "offs": striped(np.random.permutation(T)[:S]),
        "pos": striped(np.random.permutation(W)[:U]),
        "neg": striped(np.random.permutation(W)[:U]),
    }


def reference(x_words, x_scales, w1, e_words, e_scales, offs, pos, neg):
    xq = unpack_weight(x_words, x_scales)[:, unstriped(offs)]
    h = mxq(f64(w1), 0, "e4m3").T @ xq
    hq = mxq(h, 0, "e4m3")
    e_neg = unpack_weight(e_words, e_scales)[:, unstriped(neg)]
    z = hq.T @ e_neg
    ee = np.exp(z + 0.5)
    l = np.log(ee.reshape(len(ee), -1, D).sum(axis=2))
    e_pos = unpack_weight(e_words, e_scales)[:, unstriped(pos)]
    y = hq.T @ e_pos
    mean = y.reshape(len(y), -1, D).mean(axis=2)
    return relu2(l - mean - 2.5)

@@ -1,0 +1,211 @@
+from contextlib import ExitStack
+
+import concourse.mybir as mybir
+from concourse.masks import make_identity
+
+K, T, S, H, D, W, U = 1024, 2048, 512, 512, 8, 2048, 1024
+V = U // D
+FLOPS = 2 * K * H * S + 2 * 2 * H * S * U
+
+F32 = mybir.dt.float32
+BF16 = mybir.dt.bfloat16
+I32 = mybir.dt.int32
+U32 = mybir.dt.uint32
+U16 = mybir.dt.uint16
+U8 = mybir.dt.uint8
+FP8X4 = mybir.dt.float8_e4m3fn_x4
+ACT = mybir.ActivationFunctionType
+ALU = mybir.AluOpType
+
+P = 128
+PACK = 4
+PASSES = K // (P * PACK)
+TILES = S // P
+HALF = 512
+
+
+def tile_picked_ylift_lift_p_kernel(tc, x_words, x_scales, w1, e_words, e_scales, offs, pos, neg, out):
+    nc = tc.nc
+    with ExitStack() as ctx:
+        lists = ctx.enter_context(tc.tile_pool(name="lists", bufs=1))
+        keep = ctx.enter_context(tc.tile_pool(name="keep", bufs=1))
+        psum = ctx.enter_context(tc.psum_pool(name="psum", bufs=1))
+
+        offs_t = lists.tile([P, S // 16], U16, name="offs_t")
+        pos_t = lists.tile([P, U // 16], U16, name="pos_t")
+        neg_t = lists.tile([P, U // 16], U16, name="neg_t")
+
+        e_sc = keep.tile([P, W], U8, name="e_sc", align_bytes=64)
+        x_sc = keep.tile([P, T], U8, name="x_sc", align_bytes=64)
+        e_wd = keep.tile([P, W], I32, name="e_wd", align_bytes=64)
+        x_wd = [keep.tile([P, T], I32, name=f"x_wd{g}", tag=f"x_wd{g}", align_bytes=64) for g in range(PASSES)]
+        w_pieces = [(0, 0, H), (1, 0, H)]
+        w_raw = [keep.tile([P, PACK, c1 - c0], F32, name=f"w_raw{i}", align_bytes=64) for i, (g, c0, c1) in enumerate(w_pieces)]
+        ident = keep.tile([P, P], F32, name="ident")
+
+        nc.vector.memset(e_sc[:, 0:W // 2].bitcast(I32), 0)
+        nc.gpsimd.memset(e_sc[:, W // 2:W].bitcast(I32), 0)
+        nc.vector.memset(x_sc[:].bitcast(I32), 0)
+        make_identity(nc, ident[:])
+
+        def load_w(i):
+            g, c0, c1 = w_pieces[i]
+            nc.sync.dma_start(out=w_raw[i][:], in_=w1[g * 512:(g + 1) * 512, c0:c1].rearrange("(p j) c -> p j c", j=PACK))
+
+        def load_words(tile, words):
+            nc.sync.dma_start(out=tile[:], in_=words.rearrange("p n t -> p (n t)").bitcast(I32))
+
+        nc.sync.dma_start(neg_t[:], neg)
+        nc.sync.dma_start(pos_t[:], pos)
+        nc.sync.dma_start(offs_t[:], offs)
+        for q in range(4):
+            nc.sync.dma_start(out=e_sc[32 * q:32 * q + 4, :].bitcast(I32), in_=e_scales[0, 4 * q:4 * q + 4, :].bitcast(I32))
+        load_w(0)
+        for q in range(4):
+            nc.sync.dma_start(out=x_sc[32 * q:32 * q + 8, :].bitcast(I32), in_=x_scales[:, 4 * q:4 * q + 4, :].bitcast(I32))
+        load_w(1)
+        load_words(x_wd[0], x_words[0])
+        load_words(x_wd[1], x_words[1])
+        load_words(e_wd, e_words[0])
+
+        w_bf = [keep.tile([P, PACK * H], BF16, name=f"w_bf{g}", tag=f"w_bf{g}", align_bytes=64) for g in range(PASSES)]
+        wq = [keep.tile([P, H], U32, name="wq0", align_bytes=64)]
+        ws = [keep.tile([P, H], U8, name=f"ws{g}", align_bytes=64) for g in range(PASSES)]
+        for i, (g, c0, c1) in enumerate(w_pieces):
+            nc.scalar.copy(
+                out=w_bf[g][:].rearrange("p (t m j) -> p m j t", t=PACK, j=PACK)[:, c0 // PACK:c1 // PACK],
+                in_=w_raw[i][:].rearrange("p j (m t) -> p m j t", t=PACK),
+            )
+
+        neg_sc = keep.tile([P, U], U8, name="neg_sc", align_bytes=64)
+        pos_sc_listed = keep.tile([P, U], U8, name="pos_sc_listed", align_bytes=64)
+        xg_sc = keep.tile([P, S], U8, name="xg_sc", align_bytes=64)
+        xg0 = keep.tile([P, S], U32, name="xg0", align_bytes=64)
+        neg_wd = [keep.tile([P, HALF], U32, name=f"neg_wd{i}", align_bytes=64) for i in range(2)]
+
+        nc.vector.tensor_copy(neg_sc[:], e_sc[:].indirect(neg_t[:]))
+        nc.vector.tensor_copy(pos_sc_listed[:], e_sc[:].indirect(pos_t[:]))
+        nc.vector.tensor_copy(xg_sc[:], x_sc[:].indirect(offs_t[:]))
+        nc.vector.tensor_copy(xg0[:], x_wd[0][:].bitcast(U32).indirect(offs_t[:]))
+        nc.vector.quantize_mx(out=wq[0][:].bitcast(FP8X4), scales=ws[0][:], in_=w_bf[0][:])
+        wq.append(keep.tile([P, H], U32, name="wq1", tag="x_wd0", align_bytes=64))
+        nc.vector.quantize_mx(out=wq[1][:].bitcast(FP8X4), scales=ws[1][:], in_=w_bf[1][:])
+        xg1 = [keep.tile([P, S // 2], U32, name=f"xg1_{i}", tag=("w_bf1", "xg1_1")[i], align_bytes=64) for i in range(2)]
+        warm_ps = psum.tile([P, S], F32, name="warm_ps", tag="bank7")
+        for t in range(3):
+            nc.tensor.matmul_mx(out=warm_ps[:], lhsT=wq[0][:, 0:P].bitcast(FP8X4), lhsT_scale=ws[0][:, 0:P],
+                                rhs=xg0[:].bitcast(FP8X4), rhs_scale=xg_sc[:], start=True, stop=True)
+        for i in range(2):
+            nc.vector.tensor_copy(xg1[i][:], x_wd[1][:].bitcast(U32).indirect(offs_t[:, 16 * i:16 * (i + 1)]))
+        pos_sc = keep.tile([P, U], U8, name="pos_sc", tag="x_wd1", align_bytes=64)
+        nc.vector.tensor_copy(
+            out=pos_sc[:].rearrange("p (d v) -> p d v", d=D),
+            in_=pos_sc_listed[:].rearrange("p (v d) -> p d v", d=D),
+        )
+
+        for i in range(2):
+            nc.vector.tensor_copy(neg_wd[i][:], e_wd[:].bitcast(U32).indirect(neg_t[:, 32 * i:32 * (i + 1)]))
+
+        shift = [keep.tile([P, 1], F32, name=f"shift{i}", tag=f"late{i}", align_bytes=64) for i in range(2)]
+        for i in range(2):
+            nc.gpsimd.memset(shift[i][:], -2.0)
+        hq = [keep.tile([P, P], U32, name=f"hq{a}", align_bytes=64) for a in range(2)]
+        h_bf = []
+        hs = [keep.tile([P, P], U8, name=f"hs{a}", align_bytes=64) for a in range(TILES)]
+        for a in range(TILES):
+            cols = slice(a * P, (a + 1) * P)
+            h_ps = psum.tile([P, PACK * P], F32, name="h_ps", tag=f"bank{a}")
+            x_codes = [xg0[:, cols], xg1[a // 2][:, (a % 2) * P:(a % 2 + 1) * P]]
+            for t in range(PACK):
+                for g in range(PASSES):
+                    nc.tensor.matmul_mx(
+                        out=h_ps[:, t * P:(t + 1) * P],
+                        lhsT=wq[g][:, t * P:(t + 1) * P].bitcast(FP8X4),
+                        lhsT_scale=ws[g][:, t * P:(t + 1) * P],
+                        rhs=x_codes[g].bitcast(FP8X4),
+                        rhs_scale=xg_sc[4 * g:P, cols],
+                        start=(g == 0),
+                        stop=(g == PASSES - 1),
+                    )
+            h_bf.append(keep.tile([P, PACK * P], BF16, name=f"h_bf{a}", tag=f"h_bf{a}", align_bytes=64))
+            nc.scalar.copy(
+                out=h_bf[a][:].rearrange("p (n t) -> p n t", t=PACK),
+                in_=h_ps[:].rearrange("p (t n) -> p n t", t=PACK),
+            )
+            if a < 2:
+                nc.vector.quantize_mx(out=hq[a][:].bitcast(FP8X4), scales=hs[a][:], in_=h_bf[a][:])
+
+
+        ee = [keep.tile([P, U], F32, name=f"ee{a}") for a in range(TILES)]
+
+        def exp_scores(a, i, bank, bias):
+            z_ps = psum.tile([P, HALF], F32, name="z_ps", tag=f"bank{bank}")
+            nc.tensor.matmul_mx(
+                out=z_ps[:],
+                lhsT=hq[a][:].bitcast(FP8X4),
+                lhsT_scale=hs[a][:],
+                rhs=neg_wd[i][:].bitcast(FP8X4),
+                rhs_scale=neg_sc[:, i * HALF:(i + 1) * HALF],
+                start=True,
+                stop=True,
+            )
+            if a < TILES - 1:
+                nc.scalar.activation(
+                    out=ee[a][:].rearrange("p (d v) -> p d v", d=D)[:, :, i * 64:(i + 1) * 64],
+                    in_=z_ps[:].rearrange("p (v d) -> p d v", d=D),
+                    func=ACT.Exp,
+                    bias=bias,
+                )
+            else:
+                nc.scalar.activation(out=ee[a][:, i * HALF:(i + 1) * HALF], in_=z_ps[:], func=ACT.Exp, bias=bias)
+
+        st_ps = psum.tile([P, 3 * P], F32, name="st_ps", tag="bank0")
+
+        def sum_groups(a):
+            for d in range(D):
+                nc.tensor.matmul(st_ps[:, a * P:(a + 1) * P], ee[a][:, d * V:(d + 1) * V], ident[:], start=(d == 0), stop=(d == D - 1), is_transpose=True)
+
+        for n, (a, i) in enumerate([(0, 0), (1, 0), (0, 1), (1, 1), (2, 0), (2, 1), (3, 0), (3, 1)]):
+            exp_scores(a, i, 4 + n % 3, shift[n][:] if n < 2 else -2.0)
+            if n < 2:
+                hq.append(keep.tile([P, P], U32, name=f"hq{2 + n}", tag=f"late{n}", align_bytes=64))
+                nc.vector.quantize_mx(out=hq[2 + n][:].bitcast(FP8X4), scales=hs[2 + n][:], in_=h_bf[2 + n][:])
+        pos_wd = keep.tile([P, U], U32, name="pos_wd", tag=f"h_bf{TILES - 1}", align_bytes=64)
+        nc.vector.tensor_copy(pos_wd[:].rearrange("p (d v) -> p v d", d=D), e_wd[:].bitcast(U32).indirect(pos_t[:]))
+        ln_warm = keep.tile([P, 1], F32, name="ln_warm")
+        nc.scalar.activation(out=ln_warm[:], in_=ee[3][:, U - 1:U], func=ACT.Ln, scale=ee[3][:, 0:1], bias=ee[2][:, U - 1:U])
+        sum_groups(0)
+        sum_groups(1)
+        sum_groups(2)
+
+        st = keep.tile([P, 3 * P], F32, name="st")
+        nc.vector.tensor_copy(st[:], st_ps[:])
+        s_ps = psum.tile([P, 3 * V], F32, name="s_ps", tag="bank1")
+        for a in range(3):
+            nc.tensor.transpose(s_ps[:, a * V:(a + 1) * V], st[:, a * P:(a + 1) * P], ident[:])
+        s_last = keep.tile([P, V], F32, name="s_last")
+        nc.vector.tensor_reduce(out=s_last[:], in_=ee[3][:].rearrange("p (v d) -> p v d", d=D), axis=mybir.AxisListType.X, op=ALU.add)
+
+        y_ps = [psum.tile([P, 2 * V], F32, name=f"y_ps{b}", tag=("bank6", "bank4")[b]) for b in range(2)]
+        for a in range(TILES):
+            for d in range(D):
+                nc.tensor.matmul_mx(
+                    out=y_ps[a // 2][:, (a % 2) * V:(a % 2 + 1) * V],
+                    lhsT=hq[a][:].bitcast(FP8X4),
+                    lhsT_scale=hs[a][:],
+                    rhs=pos_wd[:, d * V:(d + 1) * V].bitcast(FP8X4),
+                    rhs_scale=pos_sc[:, d * V:(d + 1) * V],
+                    start=(d == 0),
+                    stop=(d == D - 1),
+                )
+
+        logs = keep.tile([P, S], F32, name="logs")
+        nc.scalar.activation(out=logs[:, 0:3 * V], in_=s_ps[:], func=ACT.Ln)
+        nc.scalar.activation(out=logs[:, 3 * V:4 * V], in_=s_last[:], func=ACT.Ln)
+        for b in range(2):
+            cols = slice(2 * b * V, 2 * (b + 1) * V)
+            margin = keep.tile([P, 2 * V], F32, name=f"margin{b}")
+            result = keep.tile([P, 2 * V], F32, name=f"result{b}")
+            nc.vector.scalar_tensor_tensor(out=margin[:], in0=y_ps[b][:], scalar=-1.0 / D, in1=logs[:, cols], op0=ALU.mult, op1=ALU.add)
+            nc.vector.scalar_tensor_tensor(out=result[:], in0=margin[:], scalar=0.0, in1=margin[:], op0=ALU.max, op1=ALU.mult)
+            nc.sync.dma_start(out=out[2 * b * P:2 * (b + 1) * P, :].rearrange("(a t) v -> t a v", t=P), in_=result[:].rearrange("p (a v) -> p a v", v=V))

@@ -73,15 +73,14 @@ def tile_picked_ylift_lift_p_kernel(tc, x_words, x_scales, w1, e_words, e_scales
         ws = [keep.tile([P, H], U8, name=f"ws{g}", align_bytes=64) for g in range(PASSES)]
         for i, (g, c0, c1) in enumerate(w_pieces):
             nc.scalar.copy(
-                out=w_bf[g][:].rearrange("p (t m j) -> p m j t", t=PACK, j=PACK)[:, c0 // PACK:c1 // PACK],
-                in_=w_raw[i][:].rearrange("p j (m t) -> p m j t", t=PACK),
+                out=w_bf[g][:].rearrange("p (t m j) -> p m t j", t=PACK, j=PACK)[:, c0 // PACK:c1 // PACK],
+                in_=w_raw[i][:].rearrange("p j (m t) -> p m t j", t=PACK),
             )
 
         neg_sc = keep.tile([P, U], U8, name="neg_sc", align_bytes=64)
         pos_sc_listed = keep.tile([P, U], U8, name="pos_sc_listed", align_bytes=64)
         xg_sc = keep.tile([P, S], U8, name="xg_sc", align_bytes=64)
         xg0 = keep.tile([P, S], U32, name="xg0", align_bytes=64)
-        neg_wd = [keep.tile([P, HALF], U32, name=f"neg_wd{i}", align_bytes=64) for i in range(2)]
 
         nc.vector.tensor_copy(neg_sc[:], e_sc[:].indirect(neg_t[:]))
         nc.vector.tensor_copy(pos_sc_listed[:], e_sc[:].indirect(pos_t[:]))
@@ -103,15 +102,21 @@ def tile_picked_ylift_lift_p_kernel(tc, x_words, x_scales, w1, e_words, e_scales
             in_=pos_sc_listed[:].rearrange("p (v d) -> p d v", d=D),
         )
 
-        for i in range(2):
-            nc.vector.tensor_copy(neg_wd[i][:], e_wd[:].bitcast(U32).indirect(neg_t[:, 32 * i:32 * (i + 1)]))
+        QUART = 256
+        neg_first = keep.tile([P, QUART], U32, name="neg_first", tag="neg_first", align_bytes=64)
+        neg_q = [keep.tile([P, QUART], U32, name=f"neg_q{i}", align_bytes=64) for i in range(2)]
+        nc.vector.tensor_copy(neg_first[:], e_wd[:].bitcast(U32).indirect(neg_t[:, 0:16]))
+        nc.vector.tensor_copy(neg_q[1][:], e_wd[:].bitcast(U32).indirect(neg_t[:, 16:32]))
+        nc.vector.tensor_copy(neg_q[0][:].bitcast(I32), neg_first[:].bitcast(I32))
 
-        shift = [keep.tile([P, 1], F32, name=f"shift{i}", tag=f"late{i}", align_bytes=64) for i in range(2)]
-        for i in range(2):
-            nc.gpsimd.memset(shift[i][:], -2.0)
-        hq = [keep.tile([P, P], U32, name=f"hq{a}", align_bytes=64) for a in range(2)]
-        h_bf = []
-        hs = [keep.tile([P, P], U8, name=f"hs{a}", align_bytes=64) for a in range(TILES)]
+        shift_first = keep.tile([P, 1], F32, name="shift_first", tag="shift_first", align_bytes=64)
+        shift_rest = keep.tile([P, 1], F32, name="shift_rest", tag="shift_rest", align_bytes=64)
+        nc.gpsimd.memset(shift_first[:], -2.0)
+        nc.gpsimd.memset(shift_rest[:], -2.0)
+        h_bf0 = keep.tile([P, PACK * P], BF16, name="h_bf0", tag="h_bf0", align_bytes=64)
+        h_bf1 = keep.tile([P, PACK * P], BF16, name="h_bf1", tag="h_bf1", align_bytes=64)
+        h_bf23 = keep.tile([P, 2 * PACK * P], BF16, name="h_bf23", tag="h_bf23", align_bytes=64)
+        h_bf = [h_bf0[:], h_bf1[:], h_bf23[:, 0:PACK * P], h_bf23[:, PACK * P:2 * PACK * P]]
         for a in range(TILES):
             cols = slice(a * P, (a + 1) * P)
             h_ps = psum.tile([P, PACK * P], F32, name="h_ps", tag=f"bank{a}")
@@ -127,85 +132,97 @@ def tile_picked_ylift_lift_p_kernel(tc, x_words, x_scales, w1, e_words, e_scales
                         start=(g == 0),
                         stop=(g == PASSES - 1),
                     )
-            h_bf.append(keep.tile([P, PACK * P], BF16, name=f"h_bf{a}", tag=f"h_bf{a}", align_bytes=64))
             nc.scalar.copy(
-                out=h_bf[a][:].rearrange("p (n t) -> p n t", t=PACK),
+                out=h_bf[a].rearrange("p (n t) -> p n t", t=PACK),
                 in_=h_ps[:].rearrange("p (t n) -> p n t", t=PACK),
             )
-            if a < 2:
-                nc.vector.quantize_mx(out=hq[a][:].bitcast(FP8X4), scales=hs[a][:], in_=h_bf[a][:])
 
+        hq0 = keep.tile([P, P], U32, name="hq0", tag="neg_first", align_bytes=64)
+        hs0 = keep.tile([P, P], U8, name="hs0", align_bytes=64)
+        nc.vector.quantize_mx(out=hq0[:].bitcast(FP8X4), scales=hs0[:], in_=h_bf0[:])
+        hq1 = keep.tile([P, P], U32, name="hq1", tag="h_bf0", align_bytes=64)
+        hs1 = keep.tile([P, P], U8, name="hs1", align_bytes=64)
+        nc.vector.quantize_mx(out=hq1[:].bitcast(FP8X4), scales=hs1[:], in_=h_bf1[:])
+        neg_second = keep.tile([P, HALF], U32, name="neg_second", tag="h_bf1", align_bytes=64)
+        nc.vector.tensor_copy(neg_second[:], e_wd[:].bitcast(U32).indirect(neg_t[:, 32:64]))
+        hq = [hq0[:], hq1[:]]
+        hs = [hs0[:], hs1[:]]
+        neg_parts = [[(neg_q[0], 0, QUART), (neg_q[1], QUART, HALF)], [(neg_second, 0, HALF)]]
 
         ee = [keep.tile([P, U], F32, name=f"ee{a}") for a in range(TILES)]
 
-        def exp_scores(a, i, bank, bias):
+        def exp_scores(a, i, bank, shift):
             z_ps = psum.tile([P, HALF], F32, name="z_ps", tag=f"bank{bank}")
-            nc.tensor.matmul_mx(
-                out=z_ps[:],
-                lhsT=hq[a][:].bitcast(FP8X4),
-                lhsT_scale=hs[a][:],
-                rhs=neg_wd[i][:].bitcast(FP8X4),
-                rhs_scale=neg_sc[:, i * HALF:(i + 1) * HALF],
-                start=True,
-                stop=True,
-            )
-            if a < TILES - 1:
+            for codes, c0, c1 in neg_parts[i]:
+                nc.tensor.matmul_mx(
+                    out=z_ps[:, c0:c1],
+                    lhsT=hq[a].bitcast(FP8X4),
+                    lhsT_scale=hs[a],
+                    rhs=codes[:].bitcast(FP8X4),
+                    rhs_scale=neg_sc[:, i * HALF + c0:i * HALF + c1],
+                    start=True,
+                    stop=True,
+                )
+            if a < 2:
                 nc.scalar.activation(
                     out=ee[a][:].rearrange("p (d v) -> p d v", d=D)[:, :, i * 64:(i + 1) * 64],
                     in_=z_ps[:].rearrange("p (v d) -> p d v", d=D),
                     func=ACT.Exp,
-                    bias=bias,
+                    bias=shift[:],
                 )
             else:
-                nc.scalar.activation(out=ee[a][:, i * HALF:(i + 1) * HALF], in_=z_ps[:], func=ACT.Exp, bias=bias)
+                nc.scalar.activation(out=ee[a][:, i * HALF:(i + 1) * HALF], in_=z_ps[:], func=ACT.Exp, bias=shift[:])
 
-        st_ps = psum.tile([P, 3 * P], F32, name="st_ps", tag="bank0")
+        exp_scores(0, 0, 4, shift_first)
+        hq23 = keep.tile([P, 2 * P], U32, name="hq23", tag="shift_first", align_bytes=64)
+        hs23 = keep.tile([P, 2 * P], U8, name="hs23", align_bytes=64)
+        nc.vector.quantize_mx(out=hq23[:].bitcast(FP8X4), scales=hs23[:], in_=h_bf23[:])
+        hq.extend([hq23[:, 0:P], hq23[:, P:2 * P]])
+        hs.extend([hs23[:, 0:P], hs23[:, P:2 * P]])
+        for n, (a, i) in enumerate([(1, 0), (0, 1), (1, 1), (2, 0), (2, 1), (3, 0), (3, 1)]):
+            exp_scores(a, i, 4 + (n + 1) % 3, shift_rest)
 
-        def sum_groups(a):
+        pos_wd_listed = keep.tile([P, U], U32, name="pos_wd_listed", tag="h_bf23", align_bytes=64)
+        nc.vector.tensor_copy(pos_wd_listed[:], e_wd[:].bitcast(U32).indirect(pos_t[:]))
+        pos_wd = keep.tile([P, U], U32, name="pos_wd", align_bytes=64)
+        nc.vector.tensor_copy(
+            out=pos_wd[:].bitcast(I32).rearrange("p (d u w) -> p u d w", d=D, w=4),
+            in_=pos_wd_listed[:].bitcast(I32).rearrange("p (u w d) -> p u d w", d=D, w=4),
+        )
+
+        st_ps = psum.tile([P, 2 * P], F32, name="st_ps", tag="bank0")
+        for a in range(2):
             for d in range(D):
                 nc.tensor.matmul(st_ps[:, a * P:(a + 1) * P], ee[a][:, d * V:(d + 1) * V], ident[:], start=(d == 0), stop=(d == D - 1), is_transpose=True)
-
-        for n, (a, i) in enumerate([(0, 0), (1, 0), (0, 1), (1, 1), (2, 0), (2, 1), (3, 0), (3, 1)]):
-            exp_scores(a, i, 4 + n % 3, shift[n][:] if n < 2 else -2.0)
-            if n < 2:
-                hq.append(keep.tile([P, P], U32, name=f"hq{2 + n}", tag=f"late{n}", align_bytes=64))
-                nc.vector.quantize_mx(out=hq[2 + n][:].bitcast(FP8X4), scales=hs[2 + n][:], in_=h_bf[2 + n][:])
-        pos_wd = keep.tile([P, U], U32, name="pos_wd", tag=f"h_bf{TILES - 1}", align_bytes=64)
-        nc.vector.tensor_copy(pos_wd[:].rearrange("p (d v) -> p v d", d=D), e_wd[:].bitcast(U32).indirect(pos_t[:]))
-        ln_warm = keep.tile([P, 1], F32, name="ln_warm")
-        nc.scalar.activation(out=ln_warm[:], in_=ee[3][:, U - 1:U], func=ACT.Ln, scale=ee[3][:, 0:1], bias=ee[2][:, U - 1:U])
-        sum_groups(0)
-        sum_groups(1)
-        sum_groups(2)
-
-        st = keep.tile([P, 3 * P], F32, name="st")
-        nc.vector.tensor_copy(st[:], st_ps[:])
-        s_ps = psum.tile([P, 3 * V], F32, name="s_ps", tag="bank1")
-        for a in range(3):
+        st = keep.tile([P, 2 * P], F32, name="st")
+        nc.scalar.copy(st[:], st_ps[:])
+        s_ps = psum.tile([P, 2 * V], F32, name="s_ps", tag="bank1")
+        for a in range(2):
             nc.tensor.transpose(s_ps[:, a * V:(a + 1) * V], st[:, a * P:(a + 1) * P], ident[:])
-        s_last = keep.tile([P, V], F32, name="s_last")
-        nc.vector.tensor_reduce(out=s_last[:], in_=ee[3][:].rearrange("p (v d) -> p v d", d=D), axis=mybir.AxisListType.X, op=ALU.add)
+        s_last = keep.tile([P, 2 * V], F32, name="s_last")
+        for a in range(2, TILES):
+            nc.vector.tensor_reduce(out=s_last[:, (a - 2) * V:(a - 1) * V], in_=ee[a][:].rearrange("p (v d) -> p v d", d=D), axis=mybir.AxisListType.X, op=ALU.add)
 
-        y_ps = [psum.tile([P, 2 * V], F32, name=f"y_ps{b}", tag=("bank6", "bank4")[b]) for b in range(2)]
+        y_ps = [psum.tile([P, 2 * V], F32, name=f"y_ps{b}", tag=("bank4", "bank5")[b]) for b in range(2)]
         for a in range(TILES):
             for d in range(D):
                 nc.tensor.matmul_mx(
                     out=y_ps[a // 2][:, (a % 2) * V:(a % 2 + 1) * V],
-                    lhsT=hq[a][:].bitcast(FP8X4),
-                    lhsT_scale=hs[a][:],
+                    lhsT=hq[a].bitcast(FP8X4),
+                    lhsT_scale=hs[a],
                     rhs=pos_wd[:, d * V:(d + 1) * V].bitcast(FP8X4),
                     rhs_scale=pos_sc[:, d * V:(d + 1) * V],
                     start=(d == 0),
                     stop=(d == D - 1),
                 )
 
-        logs = keep.tile([P, S], F32, name="logs")
-        nc.scalar.activation(out=logs[:, 0:3 * V], in_=s_ps[:], func=ACT.Ln)
-        nc.scalar.activation(out=logs[:, 3 * V:4 * V], in_=s_last[:], func=ACT.Ln)
+        logs = [keep.tile([P, 2 * V], F32, name=f"logs{b}", tag=("shift_rest", "logs1")[b], align_bytes=64) for b in range(2)]
+        sums = [s_ps, s_last]
         for b in range(2):
-            cols = slice(2 * b * V, 2 * (b + 1) * V)
+            nc.scalar.activation(out=logs[b][:], in_=sums[b][:], func=ACT.Ln)
+        for b in range(2):
             margin = keep.tile([P, 2 * V], F32, name=f"margin{b}")
             result = keep.tile([P, 2 * V], F32, name=f"result{b}")
-            nc.vector.scalar_tensor_tensor(out=margin[:], in0=y_ps[b][:], scalar=-1.0 / D, in1=logs[:, cols], op0=ALU.mult, op1=ALU.add)
+            nc.vector.scalar_tensor_tensor(out=margin[:], in0=y_ps[b][:], scalar=-1.0 / D, in1=logs[b][:], op0=ALU.mult, op1=ALU.add)
             nc.vector.scalar_tensor_tensor(out=result[:], in0=margin[:], scalar=0.0, in1=margin[:], op0=ALU.max, op1=ALU.mult)
             nc.sync.dma_start(out=out[2 * b * P:2 * (b + 1) * P, :].rearrange("(a t) v -> t a v", t=P), in_=result[:].rearrange("p (a v) -> p a v", v=V))

@@ -4,7 +4,6 @@ import concourse.mybir as mybir
 from concourse.masks import make_identity
 
 K, T, S, H, D, W, U = 1024, 2048, 512, 512, 8, 2048, 1024
-V = U // D
 FLOPS = 2 * K * H * S + 2 * 2 * H * S * U
 
 F32 = mybir.dt.float32
@@ -19,9 +18,17 @@ ALU = mybir.AluOpType
 
 P = 128
 PACK = 4
+QUADRANT = 32
 PASSES = K // (P * PACK)
 TILES = S // P
-HALF = 512
+V = U // D
+HALF = U // 2
+QUARTER = U // 4
+LIST_ROWS = 16
+LINE = 4
+TURNED = 2
+SHIFT = 0.5 - 2.5
+SCORE_BANKS = ("bank4", "bank5", "bank6")
 
 
 def tile_picked_ylift_lift_p_kernel(tc, x_words, x_scales, w1, e_words, e_scales, offs, pos, neg, out):
@@ -31,16 +38,29 @@ def tile_picked_ylift_lift_p_kernel(tc, x_words, x_scales, w1, e_words, e_scales
         keep = ctx.enter_context(tc.tile_pool(name="keep", bufs=1))
         psum = ctx.enter_context(tc.psum_pool(name="psum", bufs=1))
 
-        offs_t = lists.tile([P, S // 16], U16, name="offs_t")
-        pos_t = lists.tile([P, U // 16], U16, name="pos_t")
-        neg_t = lists.tile([P, U // 16], U16, name="neg_t")
+        def entries(list_tile, first, end):
+            return list_tile[:, first // LIST_ROWS:end // LIST_ROWS]
+
+        def product(acc, stationary, stationary_scales, moving, moving_scales, start, stop):
+            nc.tensor.matmul_mx(
+                out=acc,
+                lhsT=stationary.bitcast(FP8X4),
+                lhsT_scale=stationary_scales,
+                rhs=moving.bitcast(FP8X4),
+                rhs_scale=moving_scales,
+                start=start,
+                stop=stop,
+            )
+
+        offs_t = lists.tile([P, S // LIST_ROWS], U16, name="offs_t")
+        pos_t = lists.tile([P, U // LIST_ROWS], U16, name="pos_t")
+        neg_t = lists.tile([P, U // LIST_ROWS], U16, name="neg_t")
 
         e_sc = keep.tile([P, W], U8, name="e_sc", align_bytes=64)
         x_sc = keep.tile([P, T], U8, name="x_sc", align_bytes=64)
         e_wd = keep.tile([P, W], I32, name="e_wd", align_bytes=64)
         x_wd = [keep.tile([P, T], I32, name=f"x_wd{g}", tag=f"x_wd{g}", align_bytes=64) for g in range(PASSES)]
-        w_pieces = [(0, 0, H), (1, 0, H)]
-        w_raw = [keep.tile([P, PACK, c1 - c0], F32, name=f"w_raw{i}", align_bytes=64) for i, (g, c0, c1) in enumerate(w_pieces)]
+        w_raw = [keep.tile([P, PACK, H], F32, name=f"w_raw{g}", align_bytes=64) for g in range(PASSES)]
         ident = keep.tile([P, P], F32, name="ident")
 
         nc.vector.memset(e_sc[:, 0:W // 2].bitcast(I32), 0)
@@ -48,90 +68,85 @@ def tile_picked_ylift_lift_p_kernel(tc, x_words, x_scales, w1, e_words, e_scales
         nc.vector.memset(x_sc[:].bitcast(I32), 0)
         make_identity(nc, ident[:])
 
-        def load_w(i):
-            g, c0, c1 = w_pieces[i]
-            nc.sync.dma_start(out=w_raw[i][:], in_=w1[g * 512:(g + 1) * 512, c0:c1].rearrange("(p j) c -> p j c", j=PACK))
+        def load_w(g):
+            rows = w1[g * P * PACK:(g + 1) * P * PACK, :]
+            nc.sync.dma_start(out=w_raw[g][:], in_=rows.rearrange("(p j) c -> p j c", j=PACK))
 
         def load_words(tile, words):
             nc.sync.dma_start(out=tile[:], in_=words.rearrange("p n t -> p (n t)").bitcast(I32))
 
+        def load_scales(tile, scales, g):
+            for q in range(P // QUADRANT):
+                first = QUADRANT * q + PACK * g
+                nc.sync.dma_start(out=tile[first:first + PACK, :].bitcast(I32), in_=scales[g, PACK * q:PACK * (q + 1), :].bitcast(I32))
+
         nc.sync.dma_start(neg_t[:], neg)
         nc.sync.dma_start(pos_t[:], pos)
         nc.sync.dma_start(offs_t[:], offs)
-        for q in range(4):
-            nc.sync.dma_start(out=e_sc[32 * q:32 * q + 4, :].bitcast(I32), in_=e_scales[0, 4 * q:4 * q + 4, :].bitcast(I32))
+        load_scales(e_sc, e_scales, 0)
         load_w(0)
-        for q in range(4):
-            nc.sync.dma_start(out=x_sc[32 * q:32 * q + 8, :].bitcast(I32), in_=x_scales[:, 4 * q:4 * q + 4, :].bitcast(I32))
+        load_scales(x_sc, x_scales, 0)
         load_w(1)
+        load_scales(x_sc, x_scales, 1)
         load_words(x_wd[0], x_words[0])
         load_words(x_wd[1], x_words[1])
         load_words(e_wd, e_words[0])
 
         w_bf = [keep.tile([P, PACK * H], BF16, name=f"w_bf{g}", tag=f"w_bf{g}", align_bytes=64) for g in range(PASSES)]
-        wq = [keep.tile([P, H], U32, name="wq0", align_bytes=64)]
+        wq0 = keep.tile([P, H], U32, name="wq0", align_bytes=64)
         ws = [keep.tile([P, H], U8, name=f"ws{g}", align_bytes=64) for g in range(PASSES)]
-        for i, (g, c0, c1) in enumerate(w_pieces):
+        for g in range(PASSES):
             nc.scalar.copy(
-                out=w_bf[g][:].rearrange("p (t m j) -> p m t j", t=PACK, j=PACK)[:, c0 // PACK:c1 // PACK],
-                in_=w_raw[i][:].rearrange("p j (m t) -> p m t j", t=PACK),
+                out=w_bf[g][:].rearrange("p (t m j) -> p m t j", t=PACK, j=PACK),
+                in_=w_raw[g][:].rearrange("p j (m t) -> p m t j", t=PACK),
             )
 
         neg_sc = keep.tile([P, U], U8, name="neg_sc", align_bytes=64)
         pos_sc_listed = keep.tile([P, U], U8, name="pos_sc_listed", align_bytes=64)
         xg_sc = keep.tile([P, S], U8, name="xg_sc", align_bytes=64)
         xg0 = keep.tile([P, S], U32, name="xg0", align_bytes=64)
-
         nc.vector.tensor_copy(neg_sc[:], e_sc[:].indirect(neg_t[:]))
         nc.vector.tensor_copy(pos_sc_listed[:], e_sc[:].indirect(pos_t[:]))
         nc.vector.tensor_copy(xg_sc[:], x_sc[:].indirect(offs_t[:]))
         nc.vector.tensor_copy(xg0[:], x_wd[0][:].bitcast(U32).indirect(offs_t[:]))
-        nc.vector.quantize_mx(out=wq[0][:].bitcast(FP8X4), scales=ws[0][:], in_=w_bf[0][:])
-        wq.append(keep.tile([P, H], U32, name="wq1", tag="x_wd0", align_bytes=64))
-        nc.vector.quantize_mx(out=wq[1][:].bitcast(FP8X4), scales=ws[1][:], in_=w_bf[1][:])
+        nc.vector.quantize_mx(out=wq0[:].bitcast(FP8X4), scales=ws[0][:], in_=w_bf[0][:])
+        wq1 = keep.tile([P, H], U32, name="wq1", tag="x_wd0", align_bytes=64)
+        nc.vector.quantize_mx(out=wq1[:].bitcast(FP8X4), scales=ws[1][:], in_=w_bf[1][:])
+        wq = [wq0, wq1]
         xg1 = [keep.tile([P, S // 2], U32, name=f"xg1_{i}", tag=("w_bf1", "xg1_1")[i], align_bytes=64) for i in range(2)]
-        warm_ps = psum.tile([P, S], F32, name="warm_ps", tag="bank7")
-        for t in range(3):
-            nc.tensor.matmul_mx(out=warm_ps[:], lhsT=wq[0][:, 0:P].bitcast(FP8X4), lhsT_scale=ws[0][:, 0:P],
-                                rhs=xg0[:].bitcast(FP8X4), rhs_scale=xg_sc[:], start=True, stop=True)
         for i in range(2):
-            nc.vector.tensor_copy(xg1[i][:], x_wd[1][:].bitcast(U32).indirect(offs_t[:, 16 * i:16 * (i + 1)]))
+            picked = entries(offs_t, i * S // 2, (i + 1) * S // 2)
+            nc.vector.tensor_copy(xg1[i][:], x_wd[1][:].bitcast(U32).indirect(picked))
         pos_sc = keep.tile([P, U], U8, name="pos_sc", tag="x_wd1", align_bytes=64)
         nc.vector.tensor_copy(
             out=pos_sc[:].rearrange("p (d v) -> p d v", d=D),
             in_=pos_sc_listed[:].rearrange("p (v d) -> p d v", d=D),
         )
 
-        QUART = 256
-        neg_first = keep.tile([P, QUART], U32, name="neg_first", tag="neg_first", align_bytes=64)
-        neg_q = [keep.tile([P, QUART], U32, name=f"neg_q{i}", align_bytes=64) for i in range(2)]
-        nc.vector.tensor_copy(neg_first[:], e_wd[:].bitcast(U32).indirect(neg_t[:, 0:16]))
-        nc.vector.tensor_copy(neg_q[1][:], e_wd[:].bitcast(U32).indirect(neg_t[:, 16:32]))
+        neg_first = keep.tile([P, QUARTER], U32, name="neg_first", tag="neg_first", align_bytes=64)
+        neg_q = [keep.tile([P, QUARTER], U32, name=f"neg_q{i}", align_bytes=64) for i in range(2)]
+        nc.vector.tensor_copy(neg_first[:], e_wd[:].bitcast(U32).indirect(entries(neg_t, 0, QUARTER)))
+        nc.vector.tensor_copy(neg_q[1][:], e_wd[:].bitcast(U32).indirect(entries(neg_t, QUARTER, HALF)))
         nc.vector.tensor_copy(neg_q[0][:].bitcast(I32), neg_first[:].bitcast(I32))
 
         shift_first = keep.tile([P, 1], F32, name="shift_first", tag="shift_first", align_bytes=64)
         shift_rest = keep.tile([P, 1], F32, name="shift_rest", tag="shift_rest", align_bytes=64)
-        nc.gpsimd.memset(shift_first[:], -2.0)
-        nc.gpsimd.memset(shift_rest[:], -2.0)
+        nc.gpsimd.memset(shift_first[:], SHIFT)
+        nc.gpsimd.memset(shift_rest[:], SHIFT)
+
         h_bf0 = keep.tile([P, PACK * P], BF16, name="h_bf0", tag="h_bf0", align_bytes=64)
         h_bf1 = keep.tile([P, PACK * P], BF16, name="h_bf1", tag="h_bf1", align_bytes=64)
         h_bf23 = keep.tile([P, 2 * PACK * P], BF16, name="h_bf23", tag="h_bf23", align_bytes=64)
         h_bf = [h_bf0[:], h_bf1[:], h_bf23[:, 0:PACK * P], h_bf23[:, PACK * P:2 * PACK * P]]
         for a in range(TILES):
-            cols = slice(a * P, (a + 1) * P)
+            anchors = slice(a * P, (a + 1) * P)
             h_ps = psum.tile([P, PACK * P], F32, name="h_ps", tag=f"bank{a}")
-            x_codes = [xg0[:, cols], xg1[a // 2][:, (a % 2) * P:(a % 2 + 1) * P]]
+            x_codes = [xg0[:, anchors], xg1[a // 2][:, (a % 2) * P:(a % 2 + 1) * P]]
             for t in range(PACK):
+                channels = slice(t * P, (t + 1) * P)
                 for g in range(PASSES):
-                    nc.tensor.matmul_mx(
-                        out=h_ps[:, t * P:(t + 1) * P],
-                        lhsT=wq[g][:, t * P:(t + 1) * P].bitcast(FP8X4),
-                        lhsT_scale=ws[g][:, t * P:(t + 1) * P],
-                        rhs=x_codes[g].bitcast(FP8X4),
-                        rhs_scale=xg_sc[4 * g:P, cols],
-                        start=(g == 0),
-                        stop=(g == PASSES - 1),
-                    )
+                    product(h_ps[:, channels], wq[g][:, channels], ws[g][:, channels], x_codes[g], xg_sc[PACK * g:P, anchors],
+                            g == 0, g == PASSES - 1)
             nc.scalar.copy(
                 out=h_bf[a].rearrange("p (n t) -> p n t", t=PACK),
                 in_=h_ps[:].rearrange("p (t n) -> p n t", t=PACK),
@@ -144,28 +159,20 @@ def tile_picked_ylift_lift_p_kernel(tc, x_words, x_scales, w1, e_words, e_scales
         hs1 = keep.tile([P, P], U8, name="hs1", align_bytes=64)
         nc.vector.quantize_mx(out=hq1[:].bitcast(FP8X4), scales=hs1[:], in_=h_bf1[:])
         neg_second = keep.tile([P, HALF], U32, name="neg_second", tag="h_bf1", align_bytes=64)
-        nc.vector.tensor_copy(neg_second[:], e_wd[:].bitcast(U32).indirect(neg_t[:, 32:64]))
+        nc.vector.tensor_copy(neg_second[:], e_wd[:].bitcast(U32).indirect(entries(neg_t, HALF, U)))
         hq = [hq0[:], hq1[:]]
         hs = [hs0[:], hs1[:]]
-        neg_parts = [[(neg_q[0], 0, QUART), (neg_q[1], QUART, HALF)], [(neg_second, 0, HALF)]]
+        neg_parts = [[(neg_q[0], 0, QUARTER), (neg_q[1], QUARTER, HALF)], [(neg_second, 0, HALF)]]
 
         ee = [keep.tile([P, U], F32, name=f"ee{a}") for a in range(TILES)]
 
         def exp_scores(a, i, bank, shift):
-            z_ps = psum.tile([P, HALF], F32, name="z_ps", tag=f"bank{bank}")
+            z_ps = psum.tile([P, HALF], F32, name="z_ps", tag=bank)
             for codes, c0, c1 in neg_parts[i]:
-                nc.tensor.matmul_mx(
-                    out=z_ps[:, c0:c1],
-                    lhsT=hq[a].bitcast(FP8X4),
-                    lhsT_scale=hs[a],
-                    rhs=codes[:].bitcast(FP8X4),
-                    rhs_scale=neg_sc[:, i * HALF + c0:i * HALF + c1],
-                    start=True,
-                    stop=True,
-                )
-            if a < 2:
+                product(z_ps[:, c0:c1], hq[a], hs[a], codes[:], neg_sc[:, i * HALF + c0:i * HALF + c1], True, True)
+            if a < TURNED:
                 nc.scalar.activation(
-                    out=ee[a][:].rearrange("p (d v) -> p d v", d=D)[:, :, i * 64:(i + 1) * 64],
+                    out=ee[a][:].rearrange("p (d v) -> p d v", d=D)[:, :, i * V // 2:(i + 1) * V // 2],
                     in_=z_ps[:].rearrange("p (v d) -> p d v", d=D),
                     func=ACT.Exp,
                     bias=shift[:],
@@ -173,56 +180,59 @@ def tile_picked_ylift_lift_p_kernel(tc, x_words, x_scales, w1, e_words, e_scales
             else:
                 nc.scalar.activation(out=ee[a][:, i * HALF:(i + 1) * HALF], in_=z_ps[:], func=ACT.Exp, bias=shift[:])
 
-        exp_scores(0, 0, 4, shift_first)
+        exp_scores(0, 0, SCORE_BANKS[0], shift_first)
         hq23 = keep.tile([P, 2 * P], U32, name="hq23", tag="shift_first", align_bytes=64)
         hs23 = keep.tile([P, 2 * P], U8, name="hs23", align_bytes=64)
         nc.vector.quantize_mx(out=hq23[:].bitcast(FP8X4), scales=hs23[:], in_=h_bf23[:])
         hq.extend([hq23[:, 0:P], hq23[:, P:2 * P]])
         hs.extend([hs23[:, 0:P], hs23[:, P:2 * P]])
-        for n, (a, i) in enumerate([(1, 0), (0, 1), (1, 1), (2, 0), (2, 1), (3, 0), (3, 1)]):
-            exp_scores(a, i, 4 + (n + 1) % 3, shift_rest)
+        steps = [(a, i) for i in range(2) for a in range(2)] + [(a, i) for a in range(2, TILES) for i in range(2)]
+        for n in range(1, len(steps)):
+            exp_scores(steps[n][0], steps[n][1], SCORE_BANKS[n % len(SCORE_BANKS)], shift_rest)
 
         pos_wd_listed = keep.tile([P, U], U32, name="pos_wd_listed", tag="h_bf23", align_bytes=64)
         nc.vector.tensor_copy(pos_wd_listed[:], e_wd[:].bitcast(U32).indirect(pos_t[:]))
         pos_wd = keep.tile([P, U], U32, name="pos_wd", align_bytes=64)
         nc.vector.tensor_copy(
-            out=pos_wd[:].bitcast(I32).rearrange("p (d u w) -> p u d w", d=D, w=4),
-            in_=pos_wd_listed[:].bitcast(I32).rearrange("p (u w d) -> p u d w", d=D, w=4),
+            out=pos_wd[:].bitcast(I32).rearrange("p (d u w) -> p u d w", d=D, w=LINE),
+            in_=pos_wd_listed[:].bitcast(I32).rearrange("p (u w d) -> p u d w", d=D, w=LINE),
         )
 
-        st_ps = psum.tile([P, 2 * P], F32, name="st_ps", tag="bank0")
-        for a in range(2):
+        turned_ps = psum.tile([P, TURNED * P], F32, name="turned_ps", tag="bank0")
+        for a in range(TURNED):
             for d in range(D):
-                nc.tensor.matmul(st_ps[:, a * P:(a + 1) * P], ee[a][:, d * V:(d + 1) * V], ident[:], start=(d == 0), stop=(d == D - 1), is_transpose=True)
-        st = keep.tile([P, 2 * P], F32, name="st")
-        nc.scalar.copy(st[:], st_ps[:])
-        s_ps = psum.tile([P, 2 * V], F32, name="s_ps", tag="bank1")
-        for a in range(2):
-            nc.tensor.transpose(s_ps[:, a * V:(a + 1) * V], st[:, a * P:(a + 1) * P], ident[:])
-        s_last = keep.tile([P, 2 * V], F32, name="s_last")
-        for a in range(2, TILES):
-            nc.vector.tensor_reduce(out=s_last[:, (a - 2) * V:(a - 1) * V], in_=ee[a][:].rearrange("p (v d) -> p v d", d=D), axis=mybir.AxisListType.X, op=ALU.add)
+                nc.tensor.matmul(turned_ps[:, a * P:(a + 1) * P], ee[a][:, d * V:(d + 1) * V], ident[:],
+                                 start=(d == 0), stop=(d == D - 1), is_transpose=True)
+        turned = keep.tile([P, TURNED * P], F32, name="turned")
+        nc.scalar.copy(turned[:], turned_ps[:])
+        sums_ps = psum.tile([P, TURNED * V], F32, name="sums_ps", tag="bank1")
+        for a in range(TURNED):
+            nc.tensor.transpose(sums_ps[:, a * V:(a + 1) * V], turned[:, a * P:(a + 1) * P], ident[:])
+        sums_sb = keep.tile([P, (TILES - TURNED) * V], F32, name="sums_sb")
+        for a in range(TURNED, TILES):
+            nc.vector.tensor_reduce(out=sums_sb[:, (a - TURNED) * V:(a - TURNED + 1) * V], in_=ee[a][:].rearrange("p (v d) -> p v d", d=D),
+                                    axis=mybir.AxisListType.X, op=ALU.add)
 
-        y_ps = [psum.tile([P, 2 * V], F32, name=f"y_ps{b}", tag=("bank4", "bank5")[b]) for b in range(2)]
+        y_ps = [psum.tile([P, 2 * V], F32, name=f"y_ps{b}", tag=(SCORE_BANKS[2], SCORE_BANKS[0])[b]) for b in range(2)]
         for a in range(TILES):
             for d in range(D):
-                nc.tensor.matmul_mx(
-                    out=y_ps[a // 2][:, (a % 2) * V:(a % 2 + 1) * V],
-                    lhsT=hq[a].bitcast(FP8X4),
-                    lhsT_scale=hs[a],
-                    rhs=pos_wd[:, d * V:(d + 1) * V].bitcast(FP8X4),
-                    rhs_scale=pos_sc[:, d * V:(d + 1) * V],
-                    start=(d == 0),
-                    stop=(d == D - 1),
-                )
+                members = slice(d * V, (d + 1) * V)
+                product(y_ps[a // 2][:, (a % 2) * V:(a % 2 + 1) * V], hq[a], hs[a], pos_wd[:, members], pos_sc[:, members],
+                        d == 0, d == D - 1)
 
         logs = [keep.tile([P, 2 * V], F32, name=f"logs{b}", tag=("shift_rest", "logs1")[b], align_bytes=64) for b in range(2)]
-        sums = [s_ps, s_last]
+        sums = [sums_ps, sums_sb]
         for b in range(2):
             nc.scalar.activation(out=logs[b][:], in_=sums[b][:], func=ACT.Ln)
         for b in range(2):
             margin = keep.tile([P, 2 * V], F32, name=f"margin{b}")
             result = keep.tile([P, 2 * V], F32, name=f"result{b}")
             nc.vector.scalar_tensor_tensor(out=margin[:], in0=y_ps[b][:], scalar=-1.0 / D, in1=logs[b][:], op0=ALU.mult, op1=ALU.add)
-            nc.vector.scalar_tensor_tensor(out=result[:], in0=margin[:], scalar=0.0, in1=margin[:], op0=ALU.max, op1=ALU.mult)
-            nc.sync.dma_start(out=out[2 * b * P:2 * (b + 1) * P, :].rearrange("(a t) v -> t a v", t=P), in_=result[:].rearrange("p (a v) -> p a v", v=V))
+            if b == 0:
+                positive = keep.tile([P, 2 * V], F32, name="positive")
+                nc.scalar.activation(out=positive[:], in_=margin[:], func=ACT.Relu)
+                nc.scalar.activation(out=result[:], in_=positive[:], func=ACT.Square)
+            else:
+                nc.vector.scalar_tensor_tensor(out=result[:], in0=margin[:], scalar=0.0, in1=margin[:], op0=ALU.max, op1=ALU.mult)
+            rows = out[2 * b * P:2 * (b + 1) * P, :]
+            nc.sync.dma_start(out=rows.rearrange("(a t) v -> t a v", t=P), in_=result[:].rearrange("p (a v) -> p a v", v=V))

@@ -28,7 +28,7 @@ LIST_ROWS = 16
 LINE = 4
 TURNED = 2
 SHIFT = 0.5 - 2.5
-SCORE_BANKS = ("bank4", "bank5", "bank6")
+SCORE_BANKS = tuple(f"bank{(n + 4) % 8}" for n in range(8))
 
 
 def tile_picked_ylift_lift_p_kernel(tc, x_words, x_scales, w1, e_words, e_scales, offs, pos, neg, out):
@@ -138,19 +138,20 @@ def tile_picked_ylift_lift_p_kernel(tc, x_words, x_scales, w1, e_words, e_scales
         h_bf1 = keep.tile([P, PACK * P], BF16, name="h_bf1", tag="h_bf1", align_bytes=64)
         h_bf23 = keep.tile([P, 2 * PACK * P], BF16, name="h_bf23", tag="h_bf23", align_bytes=64)
         h_bf = [h_bf0[:], h_bf1[:], h_bf23[:, 0:PACK * P], h_bf23[:, PACK * P:2 * PACK * P]]
-        for a in range(TILES):
-            anchors = slice(a * P, (a + 1) * P)
-            h_ps = psum.tile([P, PACK * P], F32, name="h_ps", tag=f"bank{a}")
-            x_codes = [xg0[:, anchors], xg1[a // 2][:, (a % 2) * P:(a % 2 + 1) * P]]
-            for t in range(PACK):
-                channels = slice(t * P, (t + 1) * P)
-                for g in range(PASSES):
-                    product(h_ps[:, channels], wq[g][:, channels], ws[g][:, channels], x_codes[g], xg_sc[PACK * g:P, anchors],
-                            g == 0, g == PASSES - 1)
-            nc.scalar.copy(
-                out=h_bf[a].rearrange("p (n t) -> p n t", t=PACK),
-                in_=h_ps[:].rearrange("p (t n) -> p n t", t=PACK),
-            )
+        h_ps = [psum.tile([P, PACK * P], F32, name=f"h_ps{a}", tag=f"bank{a}") for a in range(TILES)]
+        for g in range(PASSES):
+            for a in range(TILES):
+                anchors = slice(a * P, (a + 1) * P)
+                x_codes = [xg0[:, anchors], xg1[a // 2][:, (a % 2) * P:(a % 2 + 1) * P]]
+                for t in range(PACK):
+                    channels = slice(t * P, (t + 1) * P)
+                    product(h_ps[a][:, channels], wq[g][:, channels], ws[g][:, channels], x_codes[g], xg_sc[PACK * g:P, anchors],
+                            g == 0 and t == 0, g == PASSES - 1 and t == PACK - 1)
+                if g == PASSES - 1:
+                    nc.scalar.copy(
+                        out=h_bf[a].rearrange("p (n t) -> p n t", t=PACK),
+                        in_=h_ps[a][:].rearrange("p (t n) -> p n t", t=PACK),
+                    )
 
         hq0 = keep.tile([P, P], U32, name="hq0", tag="neg_first", align_bytes=64)
         hs0 = keep.tile([P, P], U8, name="hs0", align_bytes=64)
@@ -198,14 +199,14 @@ def tile_picked_ylift_lift_p_kernel(tc, x_words, x_scales, w1, e_words, e_scales
             in_=pos_wd_listed[:].bitcast(I32).rearrange("p (u w d) -> p u d w", d=D, w=LINE),
         )
 
-        turned_ps = psum.tile([P, TURNED * P], F32, name="turned_ps", tag="bank0")
+        turned_ps = psum.tile([P, TURNED * P], F32, name="turned_ps", tag="bank4")
         for a in range(TURNED):
             for d in range(D):
                 nc.tensor.matmul(turned_ps[:, a * P:(a + 1) * P], ee[a][:, d * V:(d + 1) * V], ident[:],
                                  start=(d == 0), stop=(d == D - 1), is_transpose=True)
         turned = keep.tile([P, TURNED * P], F32, name="turned")
         nc.scalar.copy(turned[:], turned_ps[:])
-        sums_ps = psum.tile([P, TURNED * V], F32, name="sums_ps", tag="bank1")
+        sums_ps = psum.tile([P, TURNED * V], F32, name="sums_ps", tag="bank5")
         for a in range(TURNED):
             nc.tensor.transpose(sums_ps[:, a * V:(a + 1) * V], turned[:, a * P:(a + 1) * P], ident[:])
         sums_sb = keep.tile([P, (TILES - TURNED) * V], F32, name="sums_sb")
@@ -213,7 +214,7 @@ def tile_picked_ylift_lift_p_kernel(tc, x_words, x_scales, w1, e_words, e_scales
             nc.vector.tensor_reduce(out=sums_sb[:, (a - TURNED) * V:(a - TURNED + 1) * V], in_=ee[a][:].rearrange("p (v d) -> p v d", d=D),
                                     axis=mybir.AxisListType.X, op=ALU.add)
 
-        y_ps = [psum.tile([P, 2 * V], F32, name=f"y_ps{b}", tag=(SCORE_BANKS[2], SCORE_BANKS[0])[b]) for b in range(2)]
+        y_ps = [psum.tile([P, 2 * V], F32, name=f"y_ps{b}", tag=("bank4", "bank6")[b]) for b in range(2)]
         for a in range(TILES):
             for d in range(D):
                 members = slice(d * V, (d + 1) * V)

@@ -28,7 +28,7 @@ LIST_ROWS = 16
 LINE = 4
 TURNED = 2
 SHIFT = 0.5 - 2.5
-SCORE_BANKS = tuple(f"bank{(n + 4) % 8}" for n in range(8))
+SCORE_BANKS = ("bank4", "bank5", "bank6", "bank7", "bank0", "bank1", "bank7", "bank0")
 
 
 def tile_picked_ylift_lift_p_kernel(tc, x_words, x_scales, w1, e_words, e_scales, offs, pos, neg, out):
@@ -75,19 +75,18 @@ def tile_picked_ylift_lift_p_kernel(tc, x_words, x_scales, w1, e_words, e_scales
         def load_words(tile, words):
             nc.sync.dma_start(out=tile[:], in_=words.rearrange("p n t -> p (n t)").bitcast(I32))
 
-        def load_scales(tile, scales, g):
+        def load_scales(tile, scales, passes):
             for q in range(P // QUADRANT):
-                first = QUADRANT * q + PACK * g
-                nc.sync.dma_start(out=tile[first:first + PACK, :].bitcast(I32), in_=scales[g, PACK * q:PACK * (q + 1), :].bitcast(I32))
+                first = QUADRANT * q
+                nc.sync.dma_start(out=tile[first:first + PACK * passes, :].bitcast(I32), in_=scales[:, PACK * q:PACK * (q + 1), :].bitcast(I32))
 
         nc.sync.dma_start(neg_t[:], neg)
         nc.sync.dma_start(pos_t[:], pos)
         nc.sync.dma_start(offs_t[:], offs)
-        load_scales(e_sc, e_scales, 0)
+        load_scales(e_sc, e_scales, 1)
         load_w(0)
-        load_scales(x_sc, x_scales, 0)
+        load_scales(x_sc, x_scales, PASSES)
         load_w(1)
-        load_scales(x_sc, x_scales, 1)
         load_words(x_wd[0], x_words[0])
         load_words(x_wd[1], x_words[1])
         load_words(e_wd, e_words[0])
@@ -97,19 +96,30 @@ def tile_picked_ylift_lift_p_kernel(tc, x_words, x_scales, w1, e_words, e_scales
         ws = [keep.tile([P, H], U8, name=f"ws{g}", align_bytes=64) for g in range(PASSES)]
         for g in range(PASSES):
             nc.scalar.copy(
-                out=w_bf[g][:].rearrange("p (t m j) -> p m t j", t=PACK, j=PACK),
-                in_=w_raw[g][:].rearrange("p j (m t) -> p m t j", t=PACK),
+                out=w_bf[g][:].rearrange("p (t m j) -> p m j t", t=PACK, j=PACK),
+                in_=w_raw[g][:].rearrange("p j (m t) -> p m j t", t=PACK),
             )
 
         neg_sc = keep.tile([P, U], U8, name="neg_sc", align_bytes=64)
         pos_sc_listed = keep.tile([P, U], U8, name="pos_sc_listed", align_bytes=64)
         xg_sc = keep.tile([P, S], U8, name="xg_sc", align_bytes=64)
-        xg0 = keep.tile([P, S], U32, name="xg0", align_bytes=64)
         nc.vector.tensor_copy(neg_sc[:], e_sc[:].indirect(neg_t[:]))
         nc.vector.tensor_copy(pos_sc_listed[:], e_sc[:].indirect(pos_t[:]))
         nc.vector.tensor_copy(xg_sc[:], x_sc[:].indirect(offs_t[:]))
-        nc.vector.tensor_copy(xg0[:], x_wd[0][:].bitcast(U32).indirect(offs_t[:]))
+        pos_sc = [keep.tile([P, HALF], U8, name=f"pos_sc{i}", tag=("pos_sc0", "x_wd1")[i], align_bytes=64) for i in range(2)]
+
+        def weave_scales(i):
+            nc.vector.tensor_copy(
+                out=pos_sc[i][:].rearrange("p (d v) -> p d v", d=D // 2),
+                in_=pos_sc_listed[:].rearrange("p (v d) -> p d v", d=D)[:, i * D // 2:(i + 1) * D // 2, :],
+            )
+
+        weave_scales(0)
         nc.vector.quantize_mx(out=wq0[:].bitcast(FP8X4), scales=ws[0][:], in_=w_bf[0][:])
+        xg0 = [keep.tile([P, S // 2], U32, name=f"xg0_{i}", tag=("w_bf0", "xg0_1")[i], align_bytes=64) for i in range(2)]
+        for i in range(2):
+            picked = entries(offs_t, i * S // 2, (i + 1) * S // 2)
+            nc.vector.tensor_copy(xg0[i][:], x_wd[0][:].bitcast(U32).indirect(picked))
         wq1 = keep.tile([P, H], U32, name="wq1", tag="x_wd0", align_bytes=64)
         nc.vector.quantize_mx(out=wq1[:].bitcast(FP8X4), scales=ws[1][:], in_=w_bf[1][:])
         wq = [wq0, wq1]
@@ -117,32 +127,25 @@ def tile_picked_ylift_lift_p_kernel(tc, x_words, x_scales, w1, e_words, e_scales
         for i in range(2):
             picked = entries(offs_t, i * S // 2, (i + 1) * S // 2)
             nc.vector.tensor_copy(xg1[i][:], x_wd[1][:].bitcast(U32).indirect(picked))
-        pos_sc = keep.tile([P, U], U8, name="pos_sc", tag="x_wd1", align_bytes=64)
-        nc.vector.tensor_copy(
-            out=pos_sc[:].rearrange("p (d v) -> p d v", d=D),
-            in_=pos_sc_listed[:].rearrange("p (v d) -> p d v", d=D),
-        )
-
+        weave_scales(1)
         neg_first = keep.tile([P, QUARTER], U32, name="neg_first", tag="neg_first", align_bytes=64)
-        neg_q = [keep.tile([P, QUARTER], U32, name=f"neg_q{i}", align_bytes=64) for i in range(2)]
+        neg_q1 = keep.tile([P, QUARTER], U32, name="neg_q1", align_bytes=64)
         nc.vector.tensor_copy(neg_first[:], e_wd[:].bitcast(U32).indirect(entries(neg_t, 0, QUARTER)))
-        nc.vector.tensor_copy(neg_q[1][:], e_wd[:].bitcast(U32).indirect(entries(neg_t, QUARTER, HALF)))
-        nc.vector.tensor_copy(neg_q[0][:].bitcast(I32), neg_first[:].bitcast(I32))
-
-        shift_first = keep.tile([P, 1], F32, name="shift_first", tag="shift_first", align_bytes=64)
+        nc.vector.tensor_copy(neg_q1[:], e_wd[:].bitcast(U32).indirect(entries(neg_t, QUARTER, HALF)))
         shift_rest = keep.tile([P, 1], F32, name="shift_rest", tag="shift_rest", align_bytes=64)
-        nc.gpsimd.memset(shift_first[:], SHIFT)
+        shift_last = keep.tile([P, 1], F32, name="shift_last", tag="shift_last", align_bytes=64)
         nc.gpsimd.memset(shift_rest[:], SHIFT)
+        nc.gpsimd.memset(shift_last[:], SHIFT)
 
         h_bf0 = keep.tile([P, PACK * P], BF16, name="h_bf0", tag="h_bf0", align_bytes=64)
-        h_bf1 = keep.tile([P, PACK * P], BF16, name="h_bf1", tag="h_bf1", align_bytes=64)
-        h_bf23 = keep.tile([P, 2 * PACK * P], BF16, name="h_bf23", tag="h_bf23", align_bytes=64)
-        h_bf = [h_bf0[:], h_bf1[:], h_bf23[:, 0:PACK * P], h_bf23[:, PACK * P:2 * PACK * P]]
+        h_bf12 = keep.tile([P, 2 * PACK * P], BF16, name="h_bf12", tag="h_bf12", align_bytes=64)
+        h_bf3 = keep.tile([P, PACK * P], BF16, name="h_bf3", tag="h_bf3", align_bytes=64)
+        h_bf = [h_bf0[:], h_bf12[:, 0:PACK * P], h_bf12[:, PACK * P:2 * PACK * P], h_bf3[:]]
         h_ps = [psum.tile([P, PACK * P], F32, name=f"h_ps{a}", tag=f"bank{a}") for a in range(TILES)]
         for g in range(PASSES):
             for a in range(TILES):
                 anchors = slice(a * P, (a + 1) * P)
-                x_codes = [xg0[:, anchors], xg1[a // 2][:, (a % 2) * P:(a % 2 + 1) * P]]
+                x_codes = [xg0[a // 2][:, (a % 2) * P:(a % 2 + 1) * P], xg1[a // 2][:, (a % 2) * P:(a % 2 + 1) * P]]
                 for t in range(PACK):
                     channels = slice(t * P, (t + 1) * P)
                     product(h_ps[a][:, channels], wq[g][:, channels], ws[g][:, channels], x_codes[g], xg_sc[PACK * g:P, anchors],
@@ -153,82 +156,103 @@ def tile_picked_ylift_lift_p_kernel(tc, x_words, x_scales, w1, e_words, e_scales
                         in_=h_ps[a][:].rearrange("p (t n) -> p n t", t=PACK),
                     )
 
+        neg_q0 = keep.tile([P, QUARTER], U32, name="neg_q0", align_bytes=64)
+        nc.vector.tensor_copy(neg_q0[:].bitcast(I32), neg_first[:].bitcast(I32))
         hq0 = keep.tile([P, P], U32, name="hq0", tag="neg_first", align_bytes=64)
         hs0 = keep.tile([P, P], U8, name="hs0", align_bytes=64)
         nc.vector.quantize_mx(out=hq0[:].bitcast(FP8X4), scales=hs0[:], in_=h_bf0[:])
-        hq1 = keep.tile([P, P], U32, name="hq1", tag="h_bf0", align_bytes=64)
-        hs1 = keep.tile([P, P], U8, name="hs1", align_bytes=64)
-        nc.vector.quantize_mx(out=hq1[:].bitcast(FP8X4), scales=hs1[:], in_=h_bf1[:])
-        neg_second = keep.tile([P, HALF], U32, name="neg_second", tag="h_bf1", align_bytes=64)
-        nc.vector.tensor_copy(neg_second[:], e_wd[:].bitcast(U32).indirect(entries(neg_t, HALF, U)))
-        hq = [hq0[:], hq1[:]]
-        hs = [hs0[:], hs1[:]]
-        neg_parts = [[(neg_q[0], 0, QUARTER), (neg_q[1], QUARTER, HALF)], [(neg_second, 0, HALF)]]
+        hq12 = keep.tile([P, 2 * P], U32, name="hq12", tag="h_bf0", align_bytes=64)
+        hs12 = keep.tile([P, 2 * P], U8, name="hs12", align_bytes=64)
+        nc.vector.quantize_mx(out=hq12[:].bitcast(FP8X4), scales=hs12[:], in_=h_bf12[:])
+        hq3 = keep.tile([P, P], U32, name="hq3", tag="h_bf12", align_bytes=64)
+        hs3 = keep.tile([P, P], U8, name="hs3", align_bytes=64)
+        nc.vector.quantize_mx(out=hq3[:].bitcast(FP8X4), scales=hs3[:], in_=h_bf3[:])
+        late = keep.tile([P, HALF + U], U32, name="late", tag="h_bf3", align_bytes=64)
+        neg_second = late[:, 0:HALF]
+        pos_wd_listed = late[:, HALF:HALF + U]
+        nc.vector.tensor_copy(neg_second, e_wd[:].bitcast(U32).indirect(entries(neg_t, HALF, U)))
+        nc.vector.tensor_copy(pos_wd_listed, e_wd[:].bitcast(U32).indirect(pos_t[:]))
+        hq = [hq0[:], hq12[:, 0:P], hq12[:, P:2 * P], hq3[:]]
+        hs = [hs0[:], hs12[:, 0:P], hs12[:, P:2 * P], hs3[:]]
+        neg_parts = [[(neg_q0[:], 0, QUARTER), (neg_q1[:], QUARTER, HALF)], [(neg_second, 0, HALF)]]
 
-        ee = [keep.tile([P, U], F32, name=f"ee{a}") for a in range(TILES)]
+        pos_wd = [keep.tile([P, HALF], U32, name=f"pos_wd{i}", align_bytes=64) for i in range(2)]
+        for i in range(2):
+            nc.vector.tensor_copy(
+                out=pos_wd[i][:].bitcast(I32).rearrange("p (d u w) -> p u d w", d=D // 2, w=LINE),
+                in_=pos_wd_listed.bitcast(I32).rearrange("p (u w d) -> p u d w", d=D, w=LINE)[:, :, i * D // 2:(i + 1) * D // 2, :],
+            )
 
-        def exp_scores(a, i, bank, shift):
-            z_ps = psum.tile([P, HALF], F32, name="z_ps", tag=bank)
+        steps = [(a, i) for i in range(2) for a in range(TILES)]
+        z_ps = []
+        y_ps = []
+
+        def scores(n):
+            a, i = steps[n]
+            z_ps.append(psum.tile([P, HALF], F32, name=f"z_ps{n}", tag=SCORE_BANKS[n]))
             for codes, c0, c1 in neg_parts[i]:
-                product(z_ps[:, c0:c1], hq[a], hs[a], codes[:], neg_sc[:, i * HALF + c0:i * HALF + c1], True, True)
-            if a < TURNED:
+                product(z_ps[n][:, c0:c1], hq[a], hs[a], codes, neg_sc[:, i * HALF + c0:i * HALF + c1], True, True)
+
+        ee_first = [keep.tile([P, U], F32, name=f"ee_first{b}") for b in range(2)]
+        ee_second = [keep.tile([P, HALF], F32, name=f"ee_second{a}") for a in range(TILES)]
+
+        def exponentials(n, shift):
+            a, i = steps[n]
+            if i == 0:
                 nc.scalar.activation(
-                    out=ee[a][:].rearrange("p (d v) -> p d v", d=D)[:, :, i * V // 2:(i + 1) * V // 2],
-                    in_=z_ps[:].rearrange("p (v d) -> p d v", d=D),
+                    out=ee_first[a // 2][:].rearrange("p (d v) -> p d v", d=D)[:, :, (a % 2) * V // 2:(a % 2 + 1) * V // 2],
+                    in_=z_ps[n][:].rearrange("p (v d) -> p d v", d=D),
                     func=ACT.Exp,
                     bias=shift[:],
                 )
             else:
-                nc.scalar.activation(out=ee[a][:, i * HALF:(i + 1) * HALF], in_=z_ps[:], func=ACT.Exp, bias=shift[:])
+                nc.scalar.activation(out=ee_second[a][:], in_=z_ps[n][:], func=ACT.Exp, bias=shift[:])
 
-        exp_scores(0, 0, SCORE_BANKS[0], shift_first)
-        hq23 = keep.tile([P, 2 * P], U32, name="hq23", tag="shift_first", align_bytes=64)
-        hs23 = keep.tile([P, 2 * P], U8, name="hs23", align_bytes=64)
-        nc.vector.quantize_mx(out=hq23[:].bitcast(FP8X4), scales=hs23[:], in_=h_bf23[:])
-        hq.extend([hq23[:, 0:P], hq23[:, P:2 * P]])
-        hs.extend([hs23[:, 0:P], hs23[:, P:2 * P]])
-        steps = [(a, i) for i in range(2) for a in range(2)] + [(a, i) for a in range(2, TILES) for i in range(2)]
-        for n in range(1, len(steps)):
-            exp_scores(steps[n][0], steps[n][1], SCORE_BANKS[n % len(SCORE_BANKS)], shift_rest)
+        for n in range(6):
+            scores(n)
+        for n in range(4):
+            exponentials(n, shift_rest)
+        scores(6)
+        exponentials(4, shift_rest)
+        scores(7)
+        exponentials(5, shift_rest)
+        exponentials(6, shift_rest)
 
-        pos_wd_listed = keep.tile([P, U], U32, name="pos_wd_listed", tag="h_bf23", align_bytes=64)
-        nc.vector.tensor_copy(pos_wd_listed[:], e_wd[:].bitcast(U32).indirect(pos_t[:]))
-        pos_wd = keep.tile([P, U], U32, name="pos_wd", align_bytes=64)
-        nc.vector.tensor_copy(
-            out=pos_wd[:].bitcast(I32).rearrange("p (d u w) -> p u d w", d=D, w=LINE),
-            in_=pos_wd_listed[:].bitcast(I32).rearrange("p (u w d) -> p u d w", d=D, w=LINE),
-        )
-
-        turned_ps = psum.tile([P, TURNED * P], F32, name="turned_ps", tag="bank4")
-        for a in range(TURNED):
-            for d in range(D):
-                nc.tensor.matmul(turned_ps[:, a * P:(a + 1) * P], ee[a][:, d * V:(d + 1) * V], ident[:],
-                                 start=(d == 0), stop=(d == D - 1), is_transpose=True)
-        turned = keep.tile([P, TURNED * P], F32, name="turned")
-        nc.scalar.copy(turned[:], turned_ps[:])
-        sums_ps = psum.tile([P, TURNED * V], F32, name="sums_ps", tag="bank5")
-        for a in range(TURNED):
-            nc.tensor.transpose(sums_ps[:, a * V:(a + 1) * V], turned[:, a * P:(a + 1) * P], ident[:])
-        sums_sb = keep.tile([P, (TILES - TURNED) * V], F32, name="sums_sb")
-        for a in range(TURNED, TILES):
-            nc.vector.tensor_reduce(out=sums_sb[:, (a - TURNED) * V:(a - TURNED + 1) * V], in_=ee[a][:].rearrange("p (v d) -> p v d", d=D),
-                                    axis=mybir.AxisListType.X, op=ALU.add)
-
-        y_ps = [psum.tile([P, 2 * V], F32, name=f"y_ps{b}", tag=("bank4", "bank6")[b]) for b in range(2)]
-        for a in range(TILES):
-            for d in range(D):
-                members = slice(d * V, (d + 1) * V)
-                product(y_ps[a // 2][:, (a % 2) * V:(a % 2 + 1) * V], hq[a], hs[a], pos_wd[:, members], pos_sc[:, members],
-                        d == 0, d == D - 1)
-
-        logs = [keep.tile([P, 2 * V], F32, name=f"logs{b}", tag=("shift_rest", "logs1")[b], align_bytes=64) for b in range(2)]
-        sums = [sums_ps, sums_sb]
+        turned_ps = [psum.tile([P, P], F32, name=f"turned_ps{b}", tag=f"bank{4 + b}") for b in range(2)]
         for b in range(2):
-            nc.scalar.activation(out=logs[b][:], in_=sums[b][:], func=ACT.Ln)
+            for d in range(D):
+                nc.tensor.matmul(turned_ps[b][:], ee_first[b][:, d * V:(d + 1) * V], ident[:],
+                                 start=(d == 0), stop=(d == D - 1), is_transpose=True)
+        turned = [keep.tile([P, P], F32, name=f"turned{b}", tag=("shift_rest", "shift_last")[b], align_bytes=64) for b in range(2)]
+        sums_ps = [psum.tile([P, V], F32, name=f"sums_ps{b}", tag=("bank6", "bank2")[b]) for b in range(2)]
+        for b in range(2):
+            nc.scalar.copy(turned[b][:], turned_ps[b][:])
+            nc.tensor.transpose(sums_ps[b][:], turned[b][:], ident[:])
+            if b == 0:
+                exponentials(len(steps) - 1, shift_last)
+            y_ps.append(psum.tile([P, 2 * V], F32, name=f"y_ps{b}", tag=("bank4", "bank0")[b]))
+            for i in range(2):
+                for a in range(2 * b, 2 * b + 2):
+                    for d in range(D // 2):
+                        members = slice(d * V, (d + 1) * V)
+                        product(y_ps[b][:, (a % 2) * V:(a % 2 + 1) * V], hq[a], hs[a], pos_wd[i][:, members], pos_sc[i][:, members],
+                                (i, a % 2, d) == (0, 0, 0), (i, a % 2, d) == (1, 1, D // 2 - 1))
+
+        sums_sb = [keep.tile([P, V], F32, name=f"sums_sb{b}") for b in range(2)]
+        for a in range(TILES):
+            nc.vector.tensor_reduce(out=sums_sb[a // 2][:, (a % 2) * V // 2:(a % 2 + 1) * V // 2],
+                                    in_=ee_second[a][:].rearrange("p (v d) -> p v d", d=D), axis=mybir.AxisListType.X, op=ALU.add)
+
+        logs_all = keep.tile([P, TILES * V], F32, name="logs_all", tag="shift_rest", align_bytes=64)
+        logs = [logs_all[:, 2 * b * V:2 * (b + 1) * V] for b in range(2)]
+        for b in range(2):
+            for i, sums in enumerate((sums_ps[b][:], sums_sb[b][:])):
+                nc.scalar.activation(out=logs[b].rearrange("p (a i v) -> p a i v", a=2, i=2)[:, :, i, :],
+                                     in_=sums.rearrange("p (a v) -> p a v", a=2), func=ACT.Ln)
         for b in range(2):
             margin = keep.tile([P, 2 * V], F32, name=f"margin{b}")
             result = keep.tile([P, 2 * V], F32, name=f"result{b}")
-            nc.vector.scalar_tensor_tensor(out=margin[:], in0=y_ps[b][:], scalar=-1.0 / D, in1=logs[b][:], op0=ALU.mult, op1=ALU.add)
+            nc.vector.scalar_tensor_tensor(out=margin[:], in0=y_ps[b][:], scalar=-1.0 / D, in1=logs[b], op0=ALU.mult, op1=ALU.add)
             if b == 0:
                 positive = keep.tile([P, 2 * V], F32, name="positive")
                 nc.scalar.activation(out=positive[:], in_=margin[:], func=ACT.Relu)

@@ -28,7 +28,7 @@ LIST_ROWS = 16
 LINE = 4
 TURNED = 2
 SHIFT = 0.5 - 2.5
-SCORE_BANKS = ("bank4", "bank5", "bank6", "bank7", "bank0", "bank1", "bank7", "bank0")
+SCORE_BANKS = ("bank4", "bank5", "bank6", "bank7", "bank0", "bank1", "bank7", "bank6")
 
 
 def tile_picked_ylift_lift_p_kernel(tc, x_words, x_scales, w1, e_words, e_scales, offs, pos, neg, out):
@@ -75,18 +75,19 @@ def tile_picked_ylift_lift_p_kernel(tc, x_words, x_scales, w1, e_words, e_scales
         def load_words(tile, words):
             nc.sync.dma_start(out=tile[:], in_=words.rearrange("p n t -> p (n t)").bitcast(I32))
 
-        def load_scales(tile, scales, passes):
+        def load_scales(tile, scales, g):
             for q in range(P // QUADRANT):
-                first = QUADRANT * q
-                nc.sync.dma_start(out=tile[first:first + PACK * passes, :].bitcast(I32), in_=scales[:, PACK * q:PACK * (q + 1), :].bitcast(I32))
+                first = QUADRANT * q + PACK * g
+                nc.sync.dma_start(out=tile[first:first + PACK, :].bitcast(I32), in_=scales[g, PACK * q:PACK * (q + 1), :].bitcast(I32))
 
         nc.sync.dma_start(neg_t[:], neg)
         nc.sync.dma_start(pos_t[:], pos)
         nc.sync.dma_start(offs_t[:], offs)
-        load_scales(e_sc, e_scales, 1)
+        load_scales(e_sc, e_scales, 0)
         load_w(0)
-        load_scales(x_sc, x_scales, PASSES)
+        load_scales(x_sc, x_scales, 0)
         load_w(1)
+        load_scales(x_sc, x_scales, 1)
         load_words(x_wd[0], x_words[0])
         load_words(x_wd[1], x_words[1])
         load_words(e_wd, e_words[0])
@@ -106,15 +107,6 @@ def tile_picked_ylift_lift_p_kernel(tc, x_words, x_scales, w1, e_words, e_scales
         nc.vector.tensor_copy(neg_sc[:], e_sc[:].indirect(neg_t[:]))
         nc.vector.tensor_copy(pos_sc_listed[:], e_sc[:].indirect(pos_t[:]))
         nc.vector.tensor_copy(xg_sc[:], x_sc[:].indirect(offs_t[:]))
-        pos_sc = [keep.tile([P, HALF], U8, name=f"pos_sc{i}", tag=("pos_sc0", "x_wd1")[i], align_bytes=64) for i in range(2)]
-
-        def weave_scales(i):
-            nc.vector.tensor_copy(
-                out=pos_sc[i][:].rearrange("p (d v) -> p d v", d=D // 2),
-                in_=pos_sc_listed[:].rearrange("p (v d) -> p d v", d=D)[:, i * D // 2:(i + 1) * D // 2, :],
-            )
-
-        weave_scales(0)
         nc.vector.quantize_mx(out=wq0[:].bitcast(FP8X4), scales=ws[0][:], in_=w_bf[0][:])
         xg0 = [keep.tile([P, S // 2], U32, name=f"xg0_{i}", tag=("w_bf0", "xg0_1")[i], align_bytes=64) for i in range(2)]
         for i in range(2):
@@ -127,7 +119,11 @@ def tile_picked_ylift_lift_p_kernel(tc, x_words, x_scales, w1, e_words, e_scales
         for i in range(2):
             picked = entries(offs_t, i * S // 2, (i + 1) * S // 2)
             nc.vector.tensor_copy(xg1[i][:], x_wd[1][:].bitcast(U32).indirect(picked))
-        weave_scales(1)
+        pos_sc = keep.tile([P, U], U8, name="pos_sc", tag="x_wd1", align_bytes=64)
+        nc.vector.tensor_copy(
+            out=pos_sc[:].rearrange("p (d v) -> p d v", d=D),
+            in_=pos_sc_listed[:].rearrange("p (v d) -> p d v", d=D),
+        )
         neg_first = keep.tile([P, QUARTER], U32, name="neg_first", tag="neg_first", align_bytes=64)
         neg_q1 = keep.tile([P, QUARTER], U32, name="neg_q1", align_bytes=64)
         nc.vector.tensor_copy(neg_first[:], e_wd[:].bitcast(U32).indirect(entries(neg_t, 0, QUARTER)))
@@ -194,7 +190,7 @@ def tile_picked_ylift_lift_p_kernel(tc, x_words, x_scales, w1, e_words, e_scales
                 product(z_ps[n][:, c0:c1], hq[a], hs[a], codes, neg_sc[:, i * HALF + c0:i * HALF + c1], True, True)
 
         ee_first = [keep.tile([P, U], F32, name=f"ee_first{b}") for b in range(2)]
-        ee_second = [keep.tile([P, HALF], F32, name=f"ee_second{a}") for a in range(TILES)]
+        ee_second = [keep.tile([P, U], F32, name=f"ee_second{b}") for b in range(2)]
 
         def exponentials(n, shift):
             a, i = steps[n]
@@ -206,42 +202,50 @@ def tile_picked_ylift_lift_p_kernel(tc, x_words, x_scales, w1, e_words, e_scales
                     bias=shift[:],
                 )
             else:
-                nc.scalar.activation(out=ee_second[a][:], in_=z_ps[n][:], func=ACT.Exp, bias=shift[:])
+                nc.scalar.activation(out=ee_second[a // 2][:, (a % 2) * HALF:(a % 2 + 1) * HALF], in_=z_ps[n][:], func=ACT.Exp, bias=shift[:])
 
         for n in range(6):
             scores(n)
         for n in range(4):
             exponentials(n, shift_rest)
-        scores(6)
-        exponentials(4, shift_rest)
-        scores(7)
-        exponentials(5, shift_rest)
-        exponentials(6, shift_rest)
 
         turned_ps = [psum.tile([P, P], F32, name=f"turned_ps{b}", tag=f"bank{4 + b}") for b in range(2)]
         for b in range(2):
             for d in range(D):
                 nc.tensor.matmul(turned_ps[b][:], ee_first[b][:, d * V:(d + 1) * V], ident[:],
                                  start=(d == 0), stop=(d == D - 1), is_transpose=True)
+            if b == 0:
+                scores(6)
+                scores(7)
+        for n in range(4, 7):
+            exponentials(n, shift_rest)
         turned = [keep.tile([P, P], F32, name=f"turned{b}", tag=("shift_rest", "shift_last")[b], align_bytes=64) for b in range(2)]
-        sums_ps = [psum.tile([P, V], F32, name=f"sums_ps{b}", tag=("bank6", "bank2")[b]) for b in range(2)]
+        sums_ps = [psum.tile([P, V], F32, name=f"sums_ps{b}", tag=("bank3", "bank2")[b]) for b in range(2)]
         for b in range(2):
             nc.scalar.copy(turned[b][:], turned_ps[b][:])
             nc.tensor.transpose(sums_ps[b][:], turned[b][:], ident[:])
             if b == 0:
                 exponentials(len(steps) - 1, shift_last)
-            y_ps.append(psum.tile([P, 2 * V], F32, name=f"y_ps{b}", tag=("bank4", "bank0")[b]))
-            for i in range(2):
-                for a in range(2 * b, 2 * b + 2):
-                    for d in range(D // 2):
-                        members = slice(d * V, (d + 1) * V)
-                        product(y_ps[b][:, (a % 2) * V:(a % 2 + 1) * V], hq[a], hs[a], pos_wd[i][:, members], pos_sc[i][:, members],
-                                (i, a % 2, d) == (0, 0, 0), (i, a % 2, d) == (1, 1, D // 2 - 1))
+            if b == 0:
+                y_pair = psum.tile([P, 2 * V], F32, name="y_pair", tag="bank4")
+                for i in range(2):
+                    for a in range(2):
+                        for d in range(D // 2):
+                            members = slice(d * V, (d + 1) * V)
+                            product(y_pair[:, a * V:(a + 1) * V], hq[a], hs[a], pos_wd[i][:, members],
+                                    pos_sc[:, i * HALF + d * V:i * HALF + (d + 1) * V],
+                                    (i, a, d) == (0, 0, 0), (i, a, d) == (1, 1, D // 2 - 1))
+                y_ps.append(y_pair)
+        for a in range(2, TILES):
+            y_ps.append(psum.tile([P, V], F32, name=f"y_ps{a}", tag=("bank6", "bank5")[a - 2]))
+            for d in range(D):
+                product(y_ps[-1][:], hq[a], hs[a], pos_wd[d // 4][:, (d % 4) * V:(d % 4 + 1) * V], pos_sc[:, d * V:(d + 1) * V],
+                        d == 0, d == D - 1)
 
         sums_sb = [keep.tile([P, V], F32, name=f"sums_sb{b}") for b in range(2)]
-        for a in range(TILES):
-            nc.vector.tensor_reduce(out=sums_sb[a // 2][:, (a % 2) * V // 2:(a % 2 + 1) * V // 2],
-                                    in_=ee_second[a][:].rearrange("p (v d) -> p v d", d=D), axis=mybir.AxisListType.X, op=ALU.add)
+        for b in range(2):
+            nc.vector.tensor_reduce(out=sums_sb[b][:], in_=ee_second[b][:].rearrange("p (v d) -> p v d", d=D),
+                                    axis=mybir.AxisListType.X, op=ALU.add)
 
         logs_all = keep.tile([P, TILES * V], F32, name="logs_all", tag="shift_rest", align_bytes=64)
         logs = [logs_all[:, 2 * b * V:2 * (b + 1) * V] for b in range(2)]
@@ -249,15 +253,17 @@ def tile_picked_ylift_lift_p_kernel(tc, x_words, x_scales, w1, e_words, e_scales
             for i, sums in enumerate((sums_ps[b][:], sums_sb[b][:])):
                 nc.scalar.activation(out=logs[b].rearrange("p (a i v) -> p a i v", a=2, i=2)[:, :, i, :],
                                      in_=sums.rearrange("p (a v) -> p a v", a=2), func=ACT.Ln)
-        for b in range(2):
-            margin = keep.tile([P, 2 * V], F32, name=f"margin{b}")
-            result = keep.tile([P, 2 * V], F32, name=f"result{b}")
-            nc.vector.scalar_tensor_tensor(out=margin[:], in0=y_ps[b][:], scalar=-1.0 / D, in1=logs[b], op0=ALU.mult, op1=ALU.add)
-            if b == 0:
-                positive = keep.tile([P, 2 * V], F32, name="positive")
+        for n, (a0, a1) in enumerate(((0, 2), (2, 3), (3, 4))):
+            width = (a1 - a0) * V
+            margin = keep.tile([P, width], F32, name=f"margin{n}")
+            result = keep.tile([P, width], F32, name=f"result{n}")
+            nc.vector.scalar_tensor_tensor(out=margin[:], in0=y_ps[n][:], scalar=-1.0 / D, in1=logs_all[:, a0 * V:a1 * V],
+                                           op0=ALU.mult, op1=ALU.add)
+            if n == 0:
+                positive = keep.tile([P, width], F32, name="positive")
                 nc.scalar.activation(out=positive[:], in_=margin[:], func=ACT.Relu)
                 nc.scalar.activation(out=result[:], in_=positive[:], func=ACT.Square)
             else:
                 nc.vector.scalar_tensor_tensor(out=result[:], in0=margin[:], scalar=0.0, in1=margin[:], op0=ALU.max, op1=ALU.mult)
-            rows = out[2 * b * P:2 * (b + 1) * P, :]
+            rows = out[a0 * P:a1 * P, :]
             nc.sync.dma_start(out=rows.rearrange("(a t) v -> t a v", t=P), in_=result[:].rearrange("p (a v) -> p a v", v=V))

@@ -167,7 +167,9 @@ def tile_picked_ylift_lift_p_kernel(tc, x_words, x_scales, w1, e_words, e_scales
         neg_second = late[:, 0:HALF]
         pos_wd_listed = late[:, HALF:HALF + U]
         nc.vector.tensor_copy(neg_second, e_wd[:].bitcast(U32).indirect(entries(neg_t, HALF, U)))
-        nc.vector.tensor_copy(pos_wd_listed, e_wd[:].bitcast(U32).indirect(pos_t[:]))
+        for i in range(2):
+            nc.vector.tensor_copy(pos_wd_listed[:, i * HALF:(i + 1) * HALF],
+                                  e_wd[:].bitcast(U32).indirect(entries(pos_t, i * HALF, (i + 1) * HALF)))
         hq = [hq0[:], hq12[:, 0:P], hq12[:, P:2 * P], hq3[:]]
         hs = [hs0[:], hs12[:, 0:P], hs12[:, P:2 * P], hs3[:]]
         neg_parts = [[(neg_q0[:], 0, QUARTER), (neg_q1[:], QUARTER, HALF)], [(neg_second, 0, HALF)]]
@@ -219,6 +221,9 @@ def tile_picked_ylift_lift_p_kernel(tc, x_words, x_scales, w1, e_words, e_scales
                 scores(7)
         for n in range(4, 7):
             exponentials(n, shift_rest)
+        warm_ps = psum.tile([P, HALF], F32, name="warm_ps", tag="bank1")
+        for n in range(3):
+            product(warm_ps[:], hq[0], hs[0], pos_wd_listed[:, 0:HALF], pos_sc_listed[:, 0:HALF], True, True)
         turned = [keep.tile([P, P], F32, name=f"turned{b}", tag=("shift_rest", "shift_last")[b], align_bytes=64) for b in range(2)]
         sums_ps = [psum.tile([P, V], F32, name=f"sums_ps{b}", tag=("bank3", "bank2")[b]) for b in range(2)]
         for b in range(2):

@@ -63,8 +63,6 @@ def tile_picked_ylift_lift_p_kernel(tc, x_words, x_scales, w1, e_words, e_scales
         w_raw = [keep.tile([P, PACK, H], F32, name=f"w_raw{g}", align_bytes=64) for g in range(PASSES)]
         ident = keep.tile([P, P], F32, name="ident")
 
-        nc.vector.memset(e_sc[:, 0:W // 2].bitcast(I32), 0)
-        nc.gpsimd.memset(e_sc[:, W // 2:W].bitcast(I32), 0)
         nc.vector.memset(x_sc[:].bitcast(I32), 0)
         make_identity(nc, ident[:])
 
@@ -75,19 +73,20 @@ def tile_picked_ylift_lift_p_kernel(tc, x_words, x_scales, w1, e_words, e_scales
         def load_words(tile, words):
             nc.sync.dma_start(out=tile[:], in_=words.rearrange("p n t -> p (n t)").bitcast(I32))
 
-        def load_scales(tile, scales, g):
+        def load_scales(tile, scales, passes):
             for q in range(P // QUADRANT):
-                first = QUADRANT * q + PACK * g
-                nc.sync.dma_start(out=tile[first:first + PACK, :].bitcast(I32), in_=scales[g, PACK * q:PACK * (q + 1), :].bitcast(I32))
+                first = QUADRANT * q
+                nc.sync.dma_start(out=tile[first:first + PACK * passes, :].bitcast(I32), in_=scales[:, PACK * q:PACK * (q + 1), :].bitcast(I32))
 
         nc.sync.dma_start(neg_t[:], neg)
+        for q in range(P // QUADRANT):
+            rows = e_scales[0, PACK * q:PACK * (q + 1), :].bitcast(I32)
+            nc.sync.dma_start(out=e_sc[QUADRANT * q:QUADRANT * (q + 1), :].bitcast(I32), in_=rows.partition_broadcast(QUADRANT // PACK))
         nc.sync.dma_start(pos_t[:], pos)
         nc.sync.dma_start(offs_t[:], offs)
-        load_scales(e_sc, e_scales, 0)
         load_w(0)
-        load_scales(x_sc, x_scales, 0)
         load_w(1)
-        load_scales(x_sc, x_scales, 1)
+        load_scales(x_sc, x_scales, PASSES)
         load_words(x_wd[0], x_words[0])
         load_words(x_wd[1], x_words[1])
         load_words(e_wd, e_words[0])
@@ -108,14 +107,14 @@ def tile_picked_ylift_lift_p_kernel(tc, x_words, x_scales, w1, e_words, e_scales
         nc.vector.tensor_copy(pos_sc_listed[:], e_sc[:].indirect(pos_t[:]))
         nc.vector.tensor_copy(xg_sc[:], x_sc[:].indirect(offs_t[:]))
         nc.vector.quantize_mx(out=wq0[:].bitcast(FP8X4), scales=ws[0][:], in_=w_bf[0][:])
-        xg0 = [keep.tile([P, S // 2], U32, name=f"xg0_{i}", tag=("w_bf0", "xg0_1")[i], align_bytes=64) for i in range(2)]
+        xg0 = [keep.tile([P, S // 2], U32, name=f"xg0_{i}", align_bytes=64) for i in range(2)]
         for i in range(2):
             picked = entries(offs_t, i * S // 2, (i + 1) * S // 2)
             nc.vector.tensor_copy(xg0[i][:], x_wd[0][:].bitcast(U32).indirect(picked))
         wq1 = keep.tile([P, H], U32, name="wq1", tag="x_wd0", align_bytes=64)
         nc.vector.quantize_mx(out=wq1[:].bitcast(FP8X4), scales=ws[1][:], in_=w_bf[1][:])
         wq = [wq0, wq1]
-        xg1 = [keep.tile([P, S // 2], U32, name=f"xg1_{i}", tag=("w_bf1", "xg1_1")[i], align_bytes=64) for i in range(2)]
+        xg1 = [keep.tile([P, S // 2], U32, name=f"xg1_{i}", align_bytes=64) for i in range(2)]
         for i in range(2):
             picked = entries(offs_t, i * S // 2, (i + 1) * S // 2)
             nc.vector.tensor_copy(xg1[i][:], x_wd[1][:].bitcast(U32).indirect(picked))
@@ -124,9 +123,9 @@ def tile_picked_ylift_lift_p_kernel(tc, x_words, x_scales, w1, e_words, e_scales
             out=pos_sc[:].rearrange("p (d v) -> p d v", d=D),
             in_=pos_sc_listed[:].rearrange("p (v d) -> p d v", d=D),
         )
-        neg_first = keep.tile([P, QUARTER], U32, name="neg_first", tag="neg_first", align_bytes=64)
+        neg_q0 = keep.tile([P, QUARTER], U32, name="neg_q0", align_bytes=64)
         neg_q1 = keep.tile([P, QUARTER], U32, name="neg_q1", align_bytes=64)
-        nc.vector.tensor_copy(neg_first[:], e_wd[:].bitcast(U32).indirect(entries(neg_t, 0, QUARTER)))
+        nc.vector.tensor_copy(neg_q0[:], e_wd[:].bitcast(U32).indirect(entries(neg_t, 0, QUARTER)))
         nc.vector.tensor_copy(neg_q1[:], e_wd[:].bitcast(U32).indirect(entries(neg_t, QUARTER, HALF)))
         shift_rest = keep.tile([P, 1], F32, name="shift_rest", tag="shift_rest", align_bytes=64)
         shift_last = keep.tile([P, 1], F32, name="shift_last", tag="shift_last", align_bytes=64)
@@ -152,9 +151,7 @@ def tile_picked_ylift_lift_p_kernel(tc, x_words, x_scales, w1, e_words, e_scales
                         in_=h_ps[a][:].rearrange("p (t n) -> p n t", t=PACK),
                     )
 
-        neg_q0 = keep.tile([P, QUARTER], U32, name="neg_q0", align_bytes=64)
-        nc.vector.tensor_copy(neg_q0[:].bitcast(I32), neg_first[:].bitcast(I32))
-        hq0 = keep.tile([P, P], U32, name="hq0", tag="neg_first", align_bytes=64)
+        hq0 = keep.tile([P, P], U32, name="hq0", align_bytes=64)
         hs0 = keep.tile([P, P], U8, name="hs0", align_bytes=64)
         nc.vector.quantize_mx(out=hq0[:].bitcast(FP8X4), scales=hs0[:], in_=h_bf0[:])
         hq12 = keep.tile([P, 2 * P], U32, name="hq12", tag="h_bf0", align_bytes=64)

@@ -63,6 +63,8 @@ def tile_picked_ylift_lift_p_kernel(tc, x_words, x_scales, w1, e_words, e_scales
         w_raw = [keep.tile([P, PACK, H], F32, name=f"w_raw{g}", align_bytes=64) for g in range(PASSES)]
         ident = keep.tile([P, P], F32, name="ident")
 
+        nc.vector.memset(e_sc[:, 0:W // 2].bitcast(I32), 0)
+        nc.gpsimd.memset(e_sc[:, W // 2:W].bitcast(I32), 0)
         nc.vector.memset(x_sc[:].bitcast(I32), 0)
         make_identity(nc, ident[:])
 
@@ -70,24 +72,23 @@ def tile_picked_ylift_lift_p_kernel(tc, x_words, x_scales, w1, e_words, e_scales
             rows = w1[g * P * PACK:(g + 1) * P * PACK, :]
             nc.sync.dma_start(out=w_raw[g][:], in_=rows.rearrange("(p j) c -> p j c", j=PACK))
 
-        def load_words(tile, words):
-            nc.sync.dma_start(out=tile[:], in_=words.rearrange("p n t -> p (n t)").bitcast(I32))
+        def load_words(tile, words, c0=0, c1=T):
+            nc.sync.dma_start(out=tile[:, c0:c1], in_=words.rearrange("p n t -> p (n t)").bitcast(I32)[:, c0:c1])
 
-        def load_scales(tile, scales, passes):
-            for q in range(P // QUADRANT):
-                first = QUADRANT * q
-                nc.sync.dma_start(out=tile[first:first + PACK * passes, :].bitcast(I32), in_=scales[:, PACK * q:PACK * (q + 1), :].bitcast(I32))
+        def load_scales(tile, scales, g):
+            for r in range(PACK):
+                nc.sync.dma_start(out=tile[PACK * g + r:P:QUADRANT, :].bitcast(I32), in_=scales[g, r:PACK * PACK:PACK, :].bitcast(I32))
 
         nc.sync.dma_start(neg_t[:], neg)
-        for q in range(P // QUADRANT):
-            rows = e_scales[0, PACK * q:PACK * (q + 1), :].bitcast(I32)
-            nc.sync.dma_start(out=e_sc[QUADRANT * q:QUADRANT * (q + 1), :].bitcast(I32), in_=rows.partition_broadcast(QUADRANT // PACK))
         nc.sync.dma_start(pos_t[:], pos)
-        nc.sync.dma_start(offs_t[:], offs)
+        load_words(x_wd[0], x_words[0], 0, T // 4)
+        load_scales(e_sc, e_scales, 0)
         load_w(0)
+        nc.sync.dma_start(offs_t[:], offs)
+        load_scales(x_sc, x_scales, 0)
         load_w(1)
-        load_scales(x_sc, x_scales, PASSES)
-        load_words(x_wd[0], x_words[0])
+        load_scales(x_sc, x_scales, 1)
+        load_words(x_wd[0], x_words[0], T // 4, T)
         load_words(x_wd[1], x_words[1])
         load_words(e_wd, e_words[0])
 

@@ -75,14 +75,14 @@ def tile_picked_ylift_lift_p_kernel(tc, x_words, x_scales, w1, e_words, e_scales
         def load_words(tile, words, c0=0, c1=T):
             nc.sync.dma_start(out=tile[:, c0:c1], in_=words.rearrange("p n t -> p (n t)").bitcast(I32)[:, c0:c1])
 
-        def load_scales(tile, scales, g):
+        def load_scales(tile, scales, g, queues=(nc.sync,)):
             for r in range(PACK):
-                nc.sync.dma_start(out=tile[PACK * g + r:P:QUADRANT, :].bitcast(I32), in_=scales[g, r:PACK * PACK:PACK, :].bitcast(I32))
+                queues[r % len(queues)].dma_start(out=tile[PACK * g + r:P:QUADRANT, :].bitcast(I32), in_=scales[g, r:PACK * PACK:PACK, :].bitcast(I32))
 
+        load_words(x_wd[0], x_words[0], 0, T // 4)
         nc.sync.dma_start(neg_t[:], neg)
         nc.sync.dma_start(pos_t[:], pos)
-        load_words(x_wd[0], x_words[0], 0, T // 4)
-        load_scales(e_sc, e_scales, 0)
+        load_scales(e_sc, e_scales, 0, (nc.sync, nc.scalar))
         load_w(0)
         nc.sync.dma_start(offs_t[:], offs)
         load_scales(x_sc, x_scales, 0)
@@ -155,10 +155,10 @@ def tile_picked_ylift_lift_p_kernel(tc, x_words, x_scales, w1, e_words, e_scales
         hq0 = keep.tile([P, P], U32, name="hq0", align_bytes=64)
         hs0 = keep.tile([P, P], U8, name="hs0", align_bytes=64)
         nc.vector.quantize_mx(out=hq0[:].bitcast(FP8X4), scales=hs0[:], in_=h_bf0[:])
-        hq12 = keep.tile([P, 2 * P], U32, name="hq12", tag="h_bf0", align_bytes=64)
+        hq12 = keep.tile([P, 2 * P], U32, name="hq12", align_bytes=64)
         hs12 = keep.tile([P, 2 * P], U8, name="hs12", align_bytes=64)
         nc.vector.quantize_mx(out=hq12[:].bitcast(FP8X4), scales=hs12[:], in_=h_bf12[:])
-        hq3 = keep.tile([P, P], U32, name="hq3", tag="h_bf12", align_bytes=64)
+        hq3 = keep.tile([P, P], U32, name="hq3", align_bytes=64)
         hs3 = keep.tile([P, P], U8, name="hs3", align_bytes=64)
         nc.vector.quantize_mx(out=hq3[:].bitcast(FP8X4), scales=hs3[:], in_=h_bf3[:])
         late = keep.tile([P, HALF + U], U32, name="late", tag="h_bf3", align_bytes=64)
@@ -172,12 +172,13 @@ def tile_picked_ylift_lift_p_kernel(tc, x_words, x_scales, w1, e_words, e_scales
         hs = [hs0[:], hs12[:, 0:P], hs12[:, P:2 * P], hs3[:]]
         neg_parts = [[(neg_q0[:], 0, QUARTER), (neg_q1[:], QUARTER, HALF)], [(neg_second, 0, HALF)]]
 
-        pos_wd = [keep.tile([P, HALF], U32, name=f"pos_wd{i}", align_bytes=64) for i in range(2)]
-        for i in range(2):
-            nc.vector.tensor_copy(
-                out=pos_wd[i][:].bitcast(I32).rearrange("p (d u w) -> p u d w", d=D // 2, w=LINE),
-                in_=pos_wd_listed.bitcast(I32).rearrange("p (u w d) -> p u d w", d=D, w=LINE)[:, :, i * D // 2:(i + 1) * D // 2, :],
-            )
+        pos_wd = [keep.tile([P, HALF], U32, name=f"pos_wd{m}", align_bytes=64) for m in range(2)]
+        for m in range(2):
+            for i in range(2):
+                nc.vector.tensor_copy(
+                    out=pos_wd[m][:].bitcast(I32).rearrange("p (d i u w) -> p i u d w", d=D // 2, i=2, w=LINE)[:, i],
+                    in_=pos_wd_listed[:, i * HALF:(i + 1) * HALF].bitcast(I32).rearrange("p (u w d) -> p u d w", d=D, w=LINE)[:, :, m * D // 2:(m + 1) * D // 2, :],
+                )
 
         steps = [(a, i) for i in range(2) for a in range(TILES)]
         z_ps = []
@@ -220,7 +221,7 @@ def tile_picked_ylift_lift_p_kernel(tc, x_words, x_scales, w1, e_words, e_scales
         for n in range(4, 7):
             exponentials(n, shift_rest)
         warm_ps = psum.tile([P, HALF], F32, name="warm_ps", tag="bank1")
-        for n in range(3):
+        for n in range(2):
             product(warm_ps[:], hq[0], hs[0], pos_wd_listed[:, 0:HALF], pos_sc_listed[:, 0:HALF], True, True)
         turned = [keep.tile([P, P], F32, name=f"turned{b}", tag=("shift_rest", "shift_last")[b], align_bytes=64) for b in range(2)]
         sums_ps = [psum.tile([P, V], F32, name=f"sums_ps{b}", tag=("bank3", "bank2")[b]) for b in range(2)]
@@ -256,17 +257,19 @@ def tile_picked_ylift_lift_p_kernel(tc, x_words, x_scales, w1, e_words, e_scales
             for i, sums in enumerate((sums_ps[b][:], sums_sb[b][:])):
                 nc.scalar.activation(out=logs[b].rearrange("p (a i v) -> p a i v", a=2, i=2)[:, :, i, :],
                                      in_=sums.rearrange("p (a v) -> p a v", a=2), func=ACT.Ln)
-        for n, (a0, a1) in enumerate(((0, 2), (2, 3), (3, 4))):
-            width = (a1 - a0) * V
-            margin = keep.tile([P, width], F32, name=f"margin{n}")
-            result = keep.tile([P, width], F32, name=f"result{n}")
-            nc.vector.scalar_tensor_tensor(out=margin[:], in0=y_ps[n][:], scalar=-1.0 / D, in1=logs_all[:, a0 * V:a1 * V],
+        pieces = ((0, 2), (2, 3), (3, 4))
+        margin = [keep.tile([P, (a1 - a0) * V], F32, name=f"margin{a0}") for a0, a1 in pieces]
+        result = [keep.tile([P, (a1 - a0) * V], F32, name=f"result{a0}") for a0, a1 in pieces]
+        for n, (a0, a1) in enumerate(pieces):
+            nc.vector.scalar_tensor_tensor(out=margin[n][:], in0=y_ps[n][:], scalar=-1.0 / D, in1=logs_all[:, a0 * V:a1 * V],
                                            op0=ALU.mult, op1=ALU.add)
+        for n, (a0, a1) in enumerate(pieces):
             if n == 0:
-                positive = keep.tile([P, width], F32, name="positive")
-                nc.scalar.activation(out=positive[:], in_=margin[:], func=ACT.Relu)
-                nc.scalar.activation(out=result[:], in_=positive[:], func=ACT.Square)
+                positive = keep.tile([P, (a1 - a0) * V], F32, name="positive")
+                for func, source, target in ((ACT.Relu, margin[n], positive), (ACT.Square, positive, result[n])):
+                    for a in range(a0, a1):
+                        nc.scalar.activation(out=target[:, a * V:(a + 1) * V], in_=source[:, a * V:(a + 1) * V], func=func)
             else:
-                nc.vector.scalar_tensor_tensor(out=result[:], in0=margin[:], scalar=0.0, in1=margin[:], op0=ALU.max, op1=ALU.mult)
+                nc.vector.scalar_tensor_tensor(out=result[n][:], in0=margin[n][:], scalar=0.0, in1=margin[n][:], op0=ALU.max, op1=ALU.mult)
             rows = out[a0 * P:a1 * P, :]
-            nc.sync.dma_start(out=rows.rearrange("(a t) v -> t a v", t=P), in_=result[:].rearrange("p (a v) -> p a v", v=V))
+            nc.sync.dma_start(out=rows.rearrange("(a t) v -> t a v", t=P), in_=result[n][:].rearrange("p (a v) -> p a v", v=V))

@@ -220,9 +220,6 @@ def tile_picked_ylift_lift_p_kernel(tc, x_words, x_scales, w1, e_words, e_scales
                 scores(7)
         for n in range(4, 7):
             exponentials(n, shift_rest)
-        warm_ps = psum.tile([P, HALF], F32, name="warm_ps", tag="bank1")
-        for n in range(2):
-            product(warm_ps[:], hq[0], hs[0], pos_wd_listed[:, 0:HALF], pos_sc_listed[:, 0:HALF], True, True)
         turned = [keep.tile([P, P], F32, name=f"turned{b}", tag=("shift_rest", "shift_last")[b], align_bytes=64) for b in range(2)]
         sums_ps = [psum.tile([P, V], F32, name=f"sums_ps{b}", tag=("bank3", "bank2")[b]) for b in range(2)]
         for b in range(2):

@@ -105,7 +105,7 @@ def tile_picked_ylift_lift_p_kernel(tc, x_words, x_scales, w1, e_words, e_scales
         pos_sc_listed = keep.tile([P, U], U8, name="pos_sc_listed", align_bytes=64)
         xg_sc = keep.tile([P, S], U8, name="xg_sc", align_bytes=64)
         nc.vector.tensor_copy(neg_sc[:], e_sc[:].indirect(neg_t[:]))
-        nc.vector.tensor_copy(pos_sc_listed[:], e_sc[:].indirect(pos_t[:]))
+        nc.vector.tensor_copy(pos_sc_listed[:].rearrange("p (q d r) -> p q r d", d=D, r=PACK), e_sc[:].indirect(pos_t[:]))
         nc.vector.tensor_copy(xg_sc[:], x_sc[:].indirect(offs_t[:]))
         nc.vector.quantize_mx(out=wq0[:].bitcast(FP8X4), scales=ws[0][:], in_=w_bf[0][:])
         xg0 = [keep.tile([P, S // 2], U32, name=f"xg0_{i}", align_bytes=64) for i in range(2)]
@@ -121,8 +121,8 @@ def tile_picked_ylift_lift_p_kernel(tc, x_words, x_scales, w1, e_words, e_scales
             nc.vector.tensor_copy(xg1[i][:], x_wd[1][:].bitcast(U32).indirect(picked))
         pos_sc = keep.tile([P, U], U8, name="pos_sc", tag="x_wd1", align_bytes=64)
         nc.vector.tensor_copy(
-            out=pos_sc[:].rearrange("p (d v) -> p d v", d=D),
-            in_=pos_sc_listed[:].rearrange("p (v d) -> p d v", d=D),
+            out=pos_sc[:].bitcast(I32).rearrange("p (d q) -> p d q", d=D),
+            in_=pos_sc_listed[:].bitcast(I32).rearrange("p (q d) -> p d q", d=D),
         )
         neg_q0 = keep.tile([P, QUARTER], U32, name="neg_q0", align_bytes=64)
         neg_q1 = keep.tile([P, QUARTER], U32, name="neg_q1", align_bytes=64)

@@ -115,10 +115,12 @@ def tile_picked_ylift_lift_p_kernel(tc, x_words, x_scales, w1, e_words, e_scales
         wq1 = keep.tile([P, H], U32, name="wq1", tag="x_wd0", align_bytes=64)
         nc.vector.quantize_mx(out=wq1[:].bitcast(FP8X4), scales=ws[1][:], in_=w_bf[1][:])
         wq = [wq0, wq1]
-        xg1 = [keep.tile([P, S // 2], U32, name=f"xg1_{i}", align_bytes=64) for i in range(2)]
-        for i in range(2):
-            picked = entries(offs_t, i * S // 2, (i + 1) * S // 2)
-            nc.vector.tensor_copy(xg1[i][:], x_wd[1][:].bitcast(U32).indirect(picked))
+        x_parts = ((0, 1), (1, 2), (2, 4))
+        xg1 = []
+        for a0, a1 in x_parts:
+            part = keep.tile([P, (a1 - a0) * P], U32, name=f"xg1_{a0}", align_bytes=64)
+            nc.vector.tensor_copy(part[:], x_wd[1][:].bitcast(U32).indirect(entries(offs_t, a0 * P, a1 * P)))
+            xg1.extend(part[:, (a - a0) * P:(a - a0 + 1) * P] for a in range(a0, a1))
         pos_sc = keep.tile([P, U], U8, name="pos_sc", tag="x_wd1", align_bytes=64)
         nc.vector.tensor_copy(
             out=pos_sc[:].bitcast(I32).rearrange("p (d q) -> p d q", d=D),
@@ -128,9 +130,9 @@ def tile_picked_ylift_lift_p_kernel(tc, x_words, x_scales, w1, e_words, e_scales
         neg_q1 = keep.tile([P, QUARTER], U32, name="neg_q1", align_bytes=64)
         nc.vector.tensor_copy(neg_q0[:], e_wd[:].bitcast(U32).indirect(entries(neg_t, 0, QUARTER)))
         nc.vector.tensor_copy(neg_q1[:], e_wd[:].bitcast(U32).indirect(entries(neg_t, QUARTER, HALF)))
-        shift_rest = keep.tile([P, 1], F32, name="shift_rest", tag="shift_rest", align_bytes=64)
-        shift_last = keep.tile([P, 1], F32, name="shift_last", tag="shift_last", align_bytes=64)
-        nc.gpsimd.memset(shift_rest[:], SHIFT)
+        shift = keep.tile([P, 1], F32, name="shift", tag="shift", align_bytes=64)
+        shift_last = keep.tile([P, 1], F32, name="shift_last")
+        nc.gpsimd.memset(shift[:], SHIFT)
         nc.gpsimd.memset(shift_last[:], SHIFT)
 
         h_bf0 = keep.tile([P, PACK * P], BF16, name="h_bf0", tag="h_bf0", align_bytes=64)
@@ -141,7 +143,7 @@ def tile_picked_ylift_lift_p_kernel(tc, x_words, x_scales, w1, e_words, e_scales
         for g in range(PASSES):
             for a in range(TILES):
                 anchors = slice(a * P, (a + 1) * P)
-                x_codes = [xg0[a // 2][:, (a % 2) * P:(a % 2 + 1) * P], xg1[a // 2][:, (a % 2) * P:(a % 2 + 1) * P]]
+                x_codes = [xg0[a // 2][:, (a % 2) * P:(a % 2 + 1) * P], xg1[a]]
                 for t in range(PACK):
                     channels = slice(t * P, (t + 1) * P)
                     product(h_ps[a][:, channels], wq[g][:, channels], ws[g][:, channels], x_codes[g], xg_sc[PACK * g:P, anchors],
@@ -161,112 +163,118 @@ def tile_picked_ylift_lift_p_kernel(tc, x_words, x_scales, w1, e_words, e_scales
         hq3 = keep.tile([P, P], U32, name="hq3", align_bytes=64)
         hs3 = keep.tile([P, P], U8, name="hs3", align_bytes=64)
         nc.vector.quantize_mx(out=hq3[:].bitcast(FP8X4), scales=hs3[:], in_=h_bf3[:])
+        neg_wd = [neg_q0[:], neg_q1[:]]
+        hq = [hq0[:], hq12[:, 0:P], hq12[:, P:2 * P], hq3[:]]
+        hs = [hs0[:], hs12[:, 0:P], hs12[:, P:2 * P], hs3[:]]
+
+        def scores(bank, blocks):
+            z_ps = psum.tile([P, len(blocks) * QUARTER], F32, name=f"z_ps{blocks[0][0]}{blocks[0][1]}", tag=f"bank{bank}")
+            for n, (a, q) in enumerate(blocks):
+                product(z_ps[:, n * QUARTER:(n + 1) * QUARTER], hq[a], hs[a], neg_wd[q], neg_sc[:, q * QUARTER:(q + 1) * QUARTER], True, True)
+            return z_ps
+
+        ee_first = [keep.tile([P, U], F32, name=f"ee_first{b}", tag=f"ee_first{b}") for b in range(2)]
+        ee_second = [keep.tile([P, U], F32, name=f"ee_second{i}", tag=f"ee_second{i}") for i in range(2)]
+
+        def exp_first(z_ps, a, v0, v1, bias):
+            c0 = (a % 2) * V // 2
+            nc.scalar.activation(
+                out=ee_first[a // 2][:].rearrange("p (d v) -> p d v", d=D)[:, :, c0 + v0:c0 + v1],
+                in_=z_ps[:].rearrange("p (v d) -> p d v", d=D),
+                func=ACT.Exp,
+                bias=bias[:],
+            )
+
+        def exp_flat(z_ps, u):
+            nc.scalar.activation(out=ee_second[0][:].rearrange("p (a u c) -> p a u c", a=2, u=2)[:, :, u, :],
+                                 in_=z_ps[:].rearrange("p (a c) -> p a c", a=2), func=ACT.Exp, bias=shift[:])
+
+        def exp_members(z_ps, u, bias):
+            nc.scalar.activation(out=ee_second[1][:].rearrange("p (d a u v) -> p a d u v", d=D, a=2, u=2)[:, :, :, u, :],
+                                 in_=z_ps[:].rearrange("p (a v d) -> p a d v", a=2, d=D), func=ACT.Exp, bias=bias[:])
+
+        def turn(b, bank):
+            turned_ps = psum.tile([P, P], F32, name=f"turned_ps{b}", tag=f"bank{bank}")
+            for d in range(D):
+                nc.tensor.matmul(turned_ps[:], ee_first[b][:, d * V:(d + 1) * V], ident[:],
+                                 start=(d == 0), stop=(d == D - 1), is_transpose=True)
+            return turned_ps
+
+        def means(y_ps, a, m, start, stop):
+            for e in range(2):
+                d = 2 * m + e
+                product(y_ps, hq[a], hs[a], pos_wd[m][:, e * V:(e + 1) * V], pos_sc[:, d * V:(d + 1) * V],
+                        start and e == 0, stop and e == 1)
+
+        z_00 = scores(4, [(0, 0)])
+        z_01 = scores(5, [(0, 1)])
+        z_first = [scores(bank, [(a, 0), (a, 1)]) for a, bank in ((1, 6), (2, 7), (3, 0))]
+        exp_first(z_00, 0, 0, V // 4, shift)
         late = keep.tile([P, HALF + U], U32, name="late", tag="h_bf3", align_bytes=64)
-        neg_second = late[:, 0:HALF]
+        neg_wd.extend((late[:, 0:QUARTER], late[:, QUARTER:HALF]))
         pos_wd_listed = late[:, HALF:HALF + U]
-        nc.vector.tensor_copy(neg_second, e_wd[:].bitcast(U32).indirect(entries(neg_t, HALF, U)))
+        for q in range(2, 4):
+            nc.vector.tensor_copy(neg_wd[q], e_wd[:].bitcast(U32).indirect(entries(neg_t, q * QUARTER, (q + 1) * QUARTER)))
         for i in range(2):
             nc.vector.tensor_copy(pos_wd_listed[:, i * HALF:(i + 1) * HALF],
                                   e_wd[:].bitcast(U32).indirect(entries(pos_t, i * HALF, (i + 1) * HALF)))
-        hq = [hq0[:], hq12[:, 0:P], hq12[:, P:2 * P], hq3[:]]
-        hs = [hs0[:], hs12[:, 0:P], hs12[:, P:2 * P], hs3[:]]
-        neg_parts = [[(neg_q0[:], 0, QUARTER), (neg_q1[:], QUARTER, HALF)], [(neg_second, 0, HALF)]]
-
-        pos_wd = [keep.tile([P, HALF], U32, name=f"pos_wd{m}", align_bytes=64) for m in range(2)]
-        for m in range(2):
-            for i in range(2):
-                nc.vector.tensor_copy(
-                    out=pos_wd[m][:].bitcast(I32).rearrange("p (d i u w) -> p i u d w", d=D // 2, i=2, w=LINE)[:, i],
-                    in_=pos_wd_listed[:, i * HALF:(i + 1) * HALF].bitcast(I32).rearrange("p (u w d) -> p u d w", d=D, w=LINE)[:, :, m * D // 2:(m + 1) * D // 2, :],
-                )
-
-        steps = [(a, i) for i in range(2) for a in range(TILES)]
-        z_ps = []
-        y_ps = []
-
-        def scores(n):
-            a, i = steps[n]
-            z_ps.append(psum.tile([P, HALF], F32, name=f"z_ps{n}", tag=SCORE_BANKS[n]))
-            for codes, c0, c1 in neg_parts[i]:
-                product(z_ps[n][:, c0:c1], hq[a], hs[a], codes, neg_sc[:, i * HALF + c0:i * HALF + c1], True, True)
-
-        ee_first = [keep.tile([P, U], F32, name=f"ee_first{b}") for b in range(2)]
-        ee_second = [keep.tile([P, U], F32, name=f"ee_second{b}") for b in range(2)]
-
-        def exponentials(n, shift):
-            a, i = steps[n]
-            if i == 0:
-                nc.scalar.activation(
-                    out=ee_first[a // 2][:].rearrange("p (d v) -> p d v", d=D)[:, :, (a % 2) * V // 2:(a % 2 + 1) * V // 2],
-                    in_=z_ps[n][:].rearrange("p (v d) -> p d v", d=D),
-                    func=ACT.Exp,
-                    bias=shift[:],
-                )
-            else:
-                nc.scalar.activation(out=ee_second[a // 2][:, (a % 2) * HALF:(a % 2 + 1) * HALF], in_=z_ps[n][:], func=ACT.Exp, bias=shift[:])
-
-        for n in range(6):
-            scores(n)
-        for n in range(4):
-            exponentials(n, shift_rest)
-
-        turned_ps = [psum.tile([P, P], F32, name=f"turned_ps{b}", tag=f"bank{4 + b}") for b in range(2)]
-        for b in range(2):
-            for d in range(D):
-                nc.tensor.matmul(turned_ps[b][:], ee_first[b][:, d * V:(d + 1) * V], ident[:],
-                                 start=(d == 0), stop=(d == D - 1), is_transpose=True)
-            if b == 0:
-                scores(6)
-                scores(7)
-        for n in range(4, 7):
-            exponentials(n, shift_rest)
-        turned = [keep.tile([P, P], F32, name=f"turned{b}", tag=("shift_rest", "shift_last")[b], align_bytes=64) for b in range(2)]
-        sums_ps = [psum.tile([P, V], F32, name=f"sums_ps{b}", tag=("bank3", "bank2")[b]) for b in range(2)]
-        for b in range(2):
-            nc.scalar.copy(turned[b][:], turned_ps[b][:])
-            nc.tensor.transpose(sums_ps[b][:], turned[b][:], ident[:])
-            if b == 0:
-                exponentials(len(steps) - 1, shift_last)
-            if b == 0:
-                y_pair = psum.tile([P, 2 * V], F32, name="y_pair", tag="bank4")
-                for i in range(2):
-                    for a in range(2):
-                        for d in range(D // 2):
-                            members = slice(d * V, (d + 1) * V)
-                            product(y_pair[:, a * V:(a + 1) * V], hq[a], hs[a], pos_wd[i][:, members],
-                                    pos_sc[:, i * HALF + d * V:i * HALF + (d + 1) * V],
-                                    (i, a, d) == (0, 0, 0), (i, a, d) == (1, 1, D // 2 - 1))
-                y_ps.append(y_pair)
+        pos_wd = [keep.tile([P, 2 * V], U32, name=f"pos_wd{m}", align_bytes=64) for m in range(D // 2)]
+        for m in range(D // 2):
+            nc.vector.tensor_copy(
+                out=pos_wd[m][:].bitcast(I32).rearrange("p (d u w) -> p u d w", d=2, w=LINE),
+                in_=pos_wd_listed.bitcast(I32).rearrange("p (u w d) -> p u d w", d=D, w=LINE)[:, :, 2 * m:2 * m + 2, :],
+            )
+        z_second = [scores(1, [(0, 2), (1, 2)]), scores(2, [(2, 2), (3, 2)])]
+        exp_first(z_01, 0, V // 4, V // 2, shift)
+        for a in range(1, TILES):
+            exp_first(z_first[a - 1], a, 0, V // 2, shift)
+        turned_ps0 = turn(0, 5)
+        z_fourth = [scores(7, [(0, 3), (1, 3)]), scores(0, [(2, 3), (3, 3)])]
+        exp_flat(z_second[0], 0)
+        exp_flat(z_fourth[0], 1)
+        turned0 = keep.tile([P, P], F32, name="turned0")
+        nc.scalar.copy(turned0[:], turned_ps0[:])
+        sums_ps = [psum.tile([P, V], F32, name=f"sums_ps{b}", tag=f"bank{4 - b}") for b in range(2)]
+        nc.tensor.transpose(sums_ps[0][:], turned0[:], ident[:])
+        turned_ps1 = turn(1, 6)
+        exp_members(z_second[1], 0, shift)
+        exp_members(z_fourth[1], 1, shift_last)
+        y_pair = psum.tile([P, 2 * V], F32, name="y_pair", tag="bank1")
+        for m in range(D // 2):
+            for a in range(2):
+                means(y_pair[:, a * V:(a + 1) * V], a, m, (m, a) == (0, 0), (m, a) == (D // 2 - 1, 1))
+        turned1 = keep.tile([P, P], F32, name="turned1")
+        nc.vector.tensor_copy(turned1[:], turned_ps1[:])
+        sums_sb = [keep.tile([P, V], F32, name=f"sums_sb{b}", tag=("ee_first1", "sums_sb1")[b]) for b in range(2)]
+        nc.vector.tensor_reduce(out=sums_sb[0][:], in_=ee_second[0][:].rearrange("p (c d) -> p c d", d=D),
+                                axis=mybir.AxisListType.X, op=ALU.add)
+        nc.tensor.transpose(sums_ps[1][:], turned1[:], ident[:])
+        folded = keep.tile([P, HALF], F32, name="folded", tag="h_bf3", align_bytes=64)
+        nc.gpsimd.tensor_tensor(out=folded[:], in0=ee_second[1][:, 0:HALF], in1=ee_second[1][:, HALF:U], op=ALU.add)
+        nc.vector.tensor_reduce(out=sums_sb[1][:], in_=folded[:].rearrange("p (d c) -> p c d", d=D // 2),
+                                axis=mybir.AxisListType.X, op=ALU.add)
+        y_ps = [y_pair]
         for a in range(2, TILES):
-            y_ps.append(psum.tile([P, V], F32, name=f"y_ps{a}", tag=("bank6", "bank5")[a - 2]))
-            for d in range(D):
-                product(y_ps[-1][:], hq[a], hs[a], pos_wd[d // 4][:, (d % 4) * V:(d % 4 + 1) * V], pos_sc[:, d * V:(d + 1) * V],
-                        d == 0, d == D - 1)
+            y_ps.append(psum.tile([P, V], F32, name=f"y_ps{a}", tag=("bank5", "bank2")[a - 2]))
+            for m in range(D // 2):
+                means(y_ps[-1][:], a, m, m == 0, m == D // 2 - 1)
 
-        sums_sb = [keep.tile([P, V], F32, name=f"sums_sb{b}") for b in range(2)]
-        for b in range(2):
-            nc.vector.tensor_reduce(out=sums_sb[b][:], in_=ee_second[b][:].rearrange("p (v d) -> p v d", d=D),
-                                    axis=mybir.AxisListType.X, op=ALU.add)
-
-        logs_all = keep.tile([P, TILES * V], F32, name="logs_all", tag="shift_rest", align_bytes=64)
+        logs_all = keep.tile([P, TILES * V], F32, name="logs_all", tag="shift", align_bytes=64)
         logs = [logs_all[:, 2 * b * V:2 * (b + 1) * V] for b in range(2)]
         for b in range(2):
-            for i, sums in enumerate((sums_ps[b][:], sums_sb[b][:])):
+            for i, sums in enumerate((sums_ps[b], sums_sb[b])):
                 nc.scalar.activation(out=logs[b].rearrange("p (a i v) -> p a i v", a=2, i=2)[:, :, i, :],
-                                     in_=sums.rearrange("p (a v) -> p a v", a=2), func=ACT.Ln)
+                                     in_=sums[:].rearrange("p (a v) -> p a v", a=2), func=ACT.Ln)
         pieces = ((0, 2), (2, 3), (3, 4))
-        margin = [keep.tile([P, (a1 - a0) * V], F32, name=f"margin{a0}") for a0, a1 in pieces]
-        result = [keep.tile([P, (a1 - a0) * V], F32, name=f"result{a0}") for a0, a1 in pieces]
+        margin = keep.tile([P, TILES * V], F32, name="margin")
+        result = keep.tile([P, TILES * V], F32, name="result")
         for n, (a0, a1) in enumerate(pieces):
-            nc.vector.scalar_tensor_tensor(out=margin[n][:], in0=y_ps[n][:], scalar=-1.0 / D, in1=logs_all[:, a0 * V:a1 * V],
+            nc.vector.scalar_tensor_tensor(out=margin[:, a0 * V:a1 * V], in0=y_ps[n][:], scalar=-1.0 / D, in1=logs_all[:, a0 * V:a1 * V],
                                            op0=ALU.mult, op1=ALU.add)
-        for n, (a0, a1) in enumerate(pieces):
-            if n == 0:
-                positive = keep.tile([P, (a1 - a0) * V], F32, name="positive")
-                for func, source, target in ((ACT.Relu, margin[n], positive), (ACT.Square, positive, result[n])):
-                    for a in range(a0, a1):
-                        nc.scalar.activation(out=target[:, a * V:(a + 1) * V], in_=source[:, a * V:(a + 1) * V], func=func)
-            else:
-                nc.vector.scalar_tensor_tensor(out=result[n][:], in0=margin[n][:], scalar=0.0, in1=margin[n][:], op0=ALU.max, op1=ALU.mult)
-            rows = out[a0 * P:a1 * P, :]
-            nc.sync.dma_start(out=rows.rearrange("(a t) v -> t a v", t=P), in_=result[n][:].rearrange("p (a v) -> p a v", v=V))
+        for a0, a1 in pieces:
+            piece = margin[:, a0 * V:a1 * V]
+            nc.vector.scalar_tensor_tensor(out=result[:, a0 * V:a1 * V], in0=piece, scalar=0.0, in1=piece, op0=ALU.max, op1=ALU.mult)
+        for b in range(2):
+            rows = out[2 * b * P:2 * (b + 1) * P, :]
+            nc.sync.dma_start(out=rows.rearrange("(a t) v -> t a v", t=P),
+                              in_=result[:, 2 * b * V:2 * (b + 1) * V].rearrange("p (a v) -> p a v", v=V))

@@ -28,6 +28,7 @@ LIST_ROWS = 16
 LINE = 4
 TURNED = 2
 SHIFT = 0.5 - 2.5
+E_ROW = 2 * PACK
 SCORE_BANKS = ("bank4", "bank5", "bank6", "bank7", "bank0", "bank1", "bank7", "bank6")
 
 
@@ -75,19 +76,24 @@ def tile_picked_ylift_lift_p_kernel(tc, x_words, x_scales, w1, e_words, e_scales
         def load_words(tile, words, c0=0, c1=T):
             nc.sync.dma_start(out=tile[:, c0:c1], in_=words.rearrange("p n t -> p (n t)").bitcast(I32)[:, c0:c1])
 
-        def load_scales(tile, scales, g, queues=(nc.sync,)):
-            for r in range(PACK):
-                queues[r % len(queues)].dma_start(out=tile[PACK * g + r:P:QUADRANT, :].bitcast(I32), in_=scales[g, r:PACK * PACK:PACK, :].bitcast(I32))
+        def load_scales(tile, first_row, scales, r, queue=nc.sync):
+            queue.dma_start(out=tile[first_row + r:P:QUADRANT, :].bitcast(I32), in_=scales[r:PACK * PACK:PACK, :].bitcast(I32))
+
+        def load_x_scales(rows):
+            for r in rows:
+                for g in range(PASSES):
+                    load_scales(x_sc, PACK * g, x_scales[g], r)
 
         load_words(x_wd[0], x_words[0], 0, T // 4)
         nc.sync.dma_start(neg_t[:], neg)
         nc.sync.dma_start(pos_t[:], pos)
-        load_scales(e_sc, e_scales, 0, (nc.sync, nc.scalar))
+        for r in range(PACK):
+            load_scales(e_sc, E_ROW, e_scales[0], r, (nc.sync, nc.scalar)[r % 2])
         load_w(0)
         nc.sync.dma_start(offs_t[:], offs)
-        load_scales(x_sc, x_scales, 0)
+        load_x_scales((0, 1))
         load_w(1)
-        load_scales(x_sc, x_scales, 1)
+        load_x_scales((2, 3))
         load_words(x_wd[0], x_words[0], T // 4, T)
         load_words(x_wd[1], x_words[1])
         load_words(e_wd, e_words[0])
@@ -160,7 +166,7 @@ def tile_picked_ylift_lift_p_kernel(tc, x_words, x_scales, w1, e_words, e_scales
         hq12 = keep.tile([P, 2 * P], U32, name="hq12", align_bytes=64)
         hs12 = keep.tile([P, 2 * P], U8, name="hs12", align_bytes=64)
         nc.vector.quantize_mx(out=hq12[:].bitcast(FP8X4), scales=hs12[:], in_=h_bf12[:])
-        hq3 = keep.tile([P, P], U32, name="hq3", align_bytes=64)
+        hq3 = keep.tile([P, P], U32, name="hq3", tag="hq3", align_bytes=64)
         hs3 = keep.tile([P, P], U8, name="hs3", align_bytes=64)
         nc.vector.quantize_mx(out=hq3[:].bitcast(FP8X4), scales=hs3[:], in_=h_bf3[:])
         neg_wd = [neg_q0[:], neg_q1[:]]
@@ -170,7 +176,7 @@ def tile_picked_ylift_lift_p_kernel(tc, x_words, x_scales, w1, e_words, e_scales
         def scores(bank, blocks):
             z_ps = psum.tile([P, len(blocks) * QUARTER], F32, name=f"z_ps{blocks[0][0]}{blocks[0][1]}", tag=f"bank{bank}")
             for n, (a, q) in enumerate(blocks):
-                product(z_ps[:, n * QUARTER:(n + 1) * QUARTER], hq[a], hs[a], neg_wd[q], neg_sc[:, q * QUARTER:(q + 1) * QUARTER], True, True)
+                product(z_ps[:, n * QUARTER:(n + 1) * QUARTER], hq[a], hs[a], neg_wd[q], neg_sc[E_ROW:P, q * QUARTER:(q + 1) * QUARTER], True, True)
             return z_ps
 
         ee_first = [keep.tile([P, U], F32, name=f"ee_first{b}", tag=f"ee_first{b}") for b in range(2)]
@@ -193,17 +199,15 @@ def tile_picked_ylift_lift_p_kernel(tc, x_words, x_scales, w1, e_words, e_scales
             nc.scalar.activation(out=ee_second[1][:].rearrange("p (d a u v) -> p a d u v", d=D, a=2, u=2)[:, :, :, u, :],
                                  in_=z_ps[:].rearrange("p (a v d) -> p a d v", a=2, d=D), func=ACT.Exp, bias=bias[:])
 
-        def turn(b, bank):
-            turned_ps = psum.tile([P, P], F32, name=f"turned_ps{b}", tag=f"bank{bank}")
+        def turn(turned_ps, b):
             for d in range(D):
-                nc.tensor.matmul(turned_ps[:], ee_first[b][:, d * V:(d + 1) * V], ident[:],
+                nc.tensor.matmul(turned_ps[:, b * P:(b + 1) * P], ee_first[b][:, d * V:(d + 1) * V], ident[:],
                                  start=(d == 0), stop=(d == D - 1), is_transpose=True)
-            return turned_ps
 
         def means(y_ps, a, m, start, stop):
             for e in range(2):
                 d = 2 * m + e
-                product(y_ps, hq[a], hs[a], pos_wd[m][:, e * V:(e + 1) * V], pos_sc[:, d * V:(d + 1) * V],
+                product(y_ps, hq[a], hs[a], pos_wd[d], pos_sc[E_ROW:P, d * V:(d + 1) * V],
                         start and e == 0, stop and e == 1)
 
         z_00 = scores(4, [(0, 0)])
@@ -215,66 +219,69 @@ def tile_picked_ylift_lift_p_kernel(tc, x_words, x_scales, w1, e_words, e_scales
         pos_wd_listed = late[:, HALF:HALF + U]
         for q in range(2, 4):
             nc.vector.tensor_copy(neg_wd[q], e_wd[:].bitcast(U32).indirect(entries(neg_t, q * QUARTER, (q + 1) * QUARTER)))
-        for i in range(2):
-            nc.vector.tensor_copy(pos_wd_listed[:, i * HALF:(i + 1) * HALF],
-                                  e_wd[:].bitcast(U32).indirect(entries(pos_t, i * HALF, (i + 1) * HALF)))
-        pos_wd = [keep.tile([P, 2 * V], U32, name=f"pos_wd{m}", align_bytes=64) for m in range(D // 2)]
-        for m in range(D // 2):
+        nc.vector.tensor_copy(pos_wd_listed, e_wd[:].bitcast(U32).indirect(pos_t[:]))
+        pos_wd = []
+        for d0, d1 in ((0, 2), (2, 4), (4, D)):
+            part = keep.tile([P, (d1 - d0) * V], U32, name=f"pos_wd{d0}", align_bytes=64)
             nc.vector.tensor_copy(
-                out=pos_wd[m][:].bitcast(I32).rearrange("p (d u w) -> p u d w", d=2, w=LINE),
-                in_=pos_wd_listed.bitcast(I32).rearrange("p (u w d) -> p u d w", d=D, w=LINE)[:, :, 2 * m:2 * m + 2, :],
+                out=part[:].bitcast(I32).rearrange("p (d u w) -> p u d w", d=d1 - d0, w=LINE),
+                in_=pos_wd_listed.bitcast(I32).rearrange("p (u w d) -> p u d w", d=D, w=LINE)[:, :, d0:d1, :],
             )
+            pos_wd.extend(part[:, (d - d0) * V:(d - d0 + 1) * V] for d in range(d0, d1))
         z_second = [scores(1, [(0, 2), (1, 2)]), scores(2, [(2, 2), (3, 2)])]
         exp_first(z_01, 0, V // 4, V // 2, shift)
         for a in range(1, TILES):
             exp_first(z_first[a - 1], a, 0, V // 2, shift)
-        turned_ps0 = turn(0, 5)
+        turned_ps = psum.tile([P, 2 * P], F32, name="turned_ps", tag="bank5")
+        turn(turned_ps, 0)
         z_fourth = [scores(7, [(0, 3), (1, 3)]), scores(0, [(2, 3), (3, 3)])]
         exp_flat(z_second[0], 0)
         exp_flat(z_fourth[0], 1)
-        turned0 = keep.tile([P, P], F32, name="turned0")
-        nc.scalar.copy(turned0[:], turned_ps0[:])
-        sums_ps = [psum.tile([P, V], F32, name=f"sums_ps{b}", tag=f"bank{4 - b}") for b in range(2)]
-        nc.tensor.transpose(sums_ps[0][:], turned0[:], ident[:])
-        turned_ps1 = turn(1, 6)
+        turn(turned_ps, 1)
         exp_members(z_second[1], 0, shift)
         exp_members(z_fourth[1], 1, shift_last)
         y_pair = psum.tile([P, 2 * V], F32, name="y_pair", tag="bank1")
         for m in range(D // 2):
             for a in range(2):
                 means(y_pair[:, a * V:(a + 1) * V], a, m, (m, a) == (0, 0), (m, a) == (D // 2 - 1, 1))
-        turned1 = keep.tile([P, P], F32, name="turned1")
-        nc.vector.tensor_copy(turned1[:], turned_ps1[:])
+        turned = keep.tile([P, 2 * P], F32, name="turned")
+        nc.vector.tensor_copy(turned[:], turned_ps[:])
         sums_sb = [keep.tile([P, V], F32, name=f"sums_sb{b}", tag=("ee_first1", "sums_sb1")[b]) for b in range(2)]
         nc.vector.tensor_reduce(out=sums_sb[0][:], in_=ee_second[0][:].rearrange("p (c d) -> p c d", d=D),
                                 axis=mybir.AxisListType.X, op=ALU.add)
-        nc.tensor.transpose(sums_ps[1][:], turned1[:], ident[:])
+        sums_ps = psum.tile([P, 2 * V], F32, name="sums_ps", tag="bank4")
+        for b in range(2):
+            nc.tensor.transpose(sums_ps[:, b * V:(b + 1) * V], turned[:, b * P:(b + 1) * P], ident[:])
         folded = keep.tile([P, HALF], F32, name="folded", tag="h_bf3", align_bytes=64)
         nc.gpsimd.tensor_tensor(out=folded[:], in0=ee_second[1][:, 0:HALF], in1=ee_second[1][:, HALF:U], op=ALU.add)
         nc.vector.tensor_reduce(out=sums_sb[1][:], in_=folded[:].rearrange("p (d c) -> p c d", d=D // 2),
                                 axis=mybir.AxisListType.X, op=ALU.add)
         y_ps = [y_pair]
         for a in range(2, TILES):
-            y_ps.append(psum.tile([P, V], F32, name=f"y_ps{a}", tag=("bank5", "bank2")[a - 2]))
+            y_ps.append(psum.tile([P, V], F32, name=f"y_ps{a}", tag=("bank6", "bank2")[a - 2]))
             for m in range(D // 2):
                 means(y_ps[-1][:], a, m, m == 0, m == D // 2 - 1)
 
         logs_all = keep.tile([P, TILES * V], F32, name="logs_all", tag="shift", align_bytes=64)
         logs = [logs_all[:, 2 * b * V:2 * (b + 1) * V] for b in range(2)]
         for b in range(2):
-            for i, sums in enumerate((sums_ps[b], sums_sb[b])):
+            for i, sums in enumerate((sums_ps[:, b * V:(b + 1) * V], sums_sb[b][:])):
                 nc.scalar.activation(out=logs[b].rearrange("p (a i v) -> p a i v", a=2, i=2)[:, :, i, :],
-                                     in_=sums[:].rearrange("p (a v) -> p a v", a=2), func=ACT.Ln)
+                                     in_=sums.rearrange("p (a v) -> p a v", a=2), func=ACT.Ln)
         pieces = ((0, 2), (2, 3), (3, 4))
         margin = keep.tile([P, TILES * V], F32, name="margin")
-        result = keep.tile([P, TILES * V], F32, name="result")
+        result = [keep.tile([P, 2 * V], F32, name=f"result{b}", tag=("result0", "hq3")[b], align_bytes=64) for b in range(2)]
         for n, (a0, a1) in enumerate(pieces):
             nc.vector.scalar_tensor_tensor(out=margin[:, a0 * V:a1 * V], in0=y_ps[n][:], scalar=-1.0 / D, in1=logs_all[:, a0 * V:a1 * V],
                                            op0=ALU.mult, op1=ALU.add)
-        for a0, a1 in pieces:
+        positive = keep.tile([P, 2 * V], F32, name="positive")
+        for func, source, target in ((ACT.Relu, margin, positive), (ACT.Square, positive, result[0])):
+            for a in range(2):
+                nc.scalar.activation(out=target[:, a * V:(a + 1) * V], in_=source[:, a * V:(a + 1) * V], func=func)
+        for a0, a1 in pieces[1:]:
             piece = margin[:, a0 * V:a1 * V]
-            nc.vector.scalar_tensor_tensor(out=result[:, a0 * V:a1 * V], in0=piece, scalar=0.0, in1=piece, op0=ALU.max, op1=ALU.mult)
+            nc.vector.scalar_tensor_tensor(out=result[1][:, (a0 - 2) * V:(a1 - 2) * V], in0=piece, scalar=0.0, in1=piece, op0=ALU.max, op1=ALU.mult)
         for b in range(2):
             rows = out[2 * b * P:2 * (b + 1) * P, :]
-            nc.sync.dma_start(out=rows.rearrange("(a t) v -> t a v", t=P),
-                              in_=result[:, 2 * b * V:2 * (b + 1) * V].rearrange("p (a v) -> p a v", v=V))
+            (nc.scalar, nc.sync)[b].dma_start(out=rows.rearrange("(a t) v -> t a v", t=P),
+                              in_=result[b][:].rearrange("p (a v) -> p a v", v=V))

@@ -28,7 +28,6 @@ LIST_ROWS = 16
 LINE = 4
 TURNED = 2
 SHIFT = 0.5 - 2.5
-E_ROW = 2 * PACK
 SCORE_BANKS = ("bank4", "bank5", "bank6", "bank7", "bank0", "bank1", "bank7", "bank6")
 
 
@@ -76,24 +75,19 @@ def tile_picked_ylift_lift_p_kernel(tc, x_words, x_scales, w1, e_words, e_scales
         def load_words(tile, words, c0=0, c1=T):
             nc.sync.dma_start(out=tile[:, c0:c1], in_=words.rearrange("p n t -> p (n t)").bitcast(I32)[:, c0:c1])
 
-        def load_scales(tile, first_row, scales, r, queue=nc.sync):
-            queue.dma_start(out=tile[first_row + r:P:QUADRANT, :].bitcast(I32), in_=scales[r:PACK * PACK:PACK, :].bitcast(I32))
-
-        def load_x_scales(rows):
-            for r in rows:
-                for g in range(PASSES):
-                    load_scales(x_sc, PACK * g, x_scales[g], r)
+        def load_scales(tile, scales, g, queues=(nc.sync,)):
+            for r in range(PACK):
+                queues[r % len(queues)].dma_start(out=tile[PACK * g + r:P:QUADRANT, :].bitcast(I32), in_=scales[g, r:PACK * PACK:PACK, :].bitcast(I32))
 
         load_words(x_wd[0], x_words[0], 0, T // 4)
         nc.sync.dma_start(neg_t[:], neg)
         nc.sync.dma_start(pos_t[:], pos)
-        for r in range(PACK):
-            load_scales(e_sc, E_ROW, e_scales[0], r, (nc.sync, nc.scalar)[r % 2])
+        load_scales(e_sc, e_scales, 0, (nc.sync, nc.scalar))
         load_w(0)
         nc.sync.dma_start(offs_t[:], offs)
-        load_x_scales((0, 1))
+        load_scales(x_sc, x_scales, 0)
         load_w(1)
-        load_x_scales((2, 3))
+        load_scales(x_sc, x_scales, 1)
         load_words(x_wd[0], x_words[0], T // 4, T)
         load_words(x_wd[1], x_words[1])
         load_words(e_wd, e_words[0])
@@ -176,7 +170,7 @@ def tile_picked_ylift_lift_p_kernel(tc, x_words, x_scales, w1, e_words, e_scales
         def scores(bank, blocks):
             z_ps = psum.tile([P, len(blocks) * QUARTER], F32, name=f"z_ps{blocks[0][0]}{blocks[0][1]}", tag=f"bank{bank}")
             for n, (a, q) in enumerate(blocks):
-                product(z_ps[:, n * QUARTER:(n + 1) * QUARTER], hq[a], hs[a], neg_wd[q], neg_sc[E_ROW:P, q * QUARTER:(q + 1) * QUARTER], True, True)
+                product(z_ps[:, n * QUARTER:(n + 1) * QUARTER], hq[a], hs[a], neg_wd[q], neg_sc[:, q * QUARTER:(q + 1) * QUARTER], True, True)
             return z_ps
 
         ee_first = [keep.tile([P, U], F32, name=f"ee_first{b}", tag=f"ee_first{b}") for b in range(2)]
@@ -191,13 +185,9 @@ def tile_picked_ylift_lift_p_kernel(tc, x_words, x_scales, w1, e_words, e_scales
                 bias=bias[:],
             )
 
-        def exp_flat(z_ps, u):
-            nc.scalar.activation(out=ee_second[0][:].rearrange("p (a u c) -> p a u c", a=2, u=2)[:, :, u, :],
-                                 in_=z_ps[:].rearrange("p (a c) -> p a c", a=2), func=ACT.Exp, bias=shift[:])
-
-        def exp_members(z_ps, u, bias):
-            nc.scalar.activation(out=ee_second[1][:].rearrange("p (d a u v) -> p a d u v", d=D, a=2, u=2)[:, :, :, u, :],
-                                 in_=z_ps[:].rearrange("p (a v d) -> p a d v", a=2, d=D), func=ACT.Exp, bias=bias[:])
+        def exp_second(z_ps, b, u, bias):
+            nc.scalar.activation(out=ee_second[b][:].rearrange("p (a u c) -> p a u c", a=2, u=2)[:, :, u, :],
+                                 in_=z_ps[:].rearrange("p (a c) -> p a c", a=2), func=ACT.Exp, bias=bias[:])
 
         def turn(turned_ps, b):
             for d in range(D):
@@ -207,7 +197,7 @@ def tile_picked_ylift_lift_p_kernel(tc, x_words, x_scales, w1, e_words, e_scales
         def means(y_ps, a, m, start, stop):
             for e in range(2):
                 d = 2 * m + e
-                product(y_ps, hq[a], hs[a], pos_wd[d], pos_sc[E_ROW:P, d * V:(d + 1) * V],
+                product(y_ps, hq[a], hs[a], pos_wd[d], pos_sc[:, d * V:(d + 1) * V],
                         start and e == 0, stop and e == 1)
 
         z_00 = scores(4, [(0, 0)])
@@ -235,11 +225,11 @@ def tile_picked_ylift_lift_p_kernel(tc, x_words, x_scales, w1, e_words, e_scales
         turned_ps = psum.tile([P, 2 * P], F32, name="turned_ps", tag="bank5")
         turn(turned_ps, 0)
         z_fourth = [scores(7, [(0, 3), (1, 3)]), scores(0, [(2, 3), (3, 3)])]
-        exp_flat(z_second[0], 0)
-        exp_flat(z_fourth[0], 1)
+        exp_second(z_second[0], 0, 0, shift)
+        exp_second(z_fourth[0], 0, 1, shift)
         turn(turned_ps, 1)
-        exp_members(z_second[1], 0, shift)
-        exp_members(z_fourth[1], 1, shift_last)
+        exp_second(z_second[1], 1, 0, shift)
+        exp_second(z_fourth[1], 1, 1, shift_last)
         y_pair = psum.tile([P, 2 * V], F32, name="y_pair", tag="bank1")
         for m in range(D // 2):
             for a in range(2):
@@ -252,9 +242,7 @@ def tile_picked_ylift_lift_p_kernel(tc, x_words, x_scales, w1, e_words, e_scales
         sums_ps = psum.tile([P, 2 * V], F32, name="sums_ps", tag="bank4")
         for b in range(2):
             nc.tensor.transpose(sums_ps[:, b * V:(b + 1) * V], turned[:, b * P:(b + 1) * P], ident[:])
-        folded = keep.tile([P, HALF], F32, name="folded", tag="h_bf3", align_bytes=64)
-        nc.gpsimd.tensor_tensor(out=folded[:], in0=ee_second[1][:, 0:HALF], in1=ee_second[1][:, HALF:U], op=ALU.add)
-        nc.vector.tensor_reduce(out=sums_sb[1][:], in_=folded[:].rearrange("p (d c) -> p c d", d=D // 2),
+        nc.vector.tensor_reduce(out=sums_sb[1][:], in_=ee_second[1][:].rearrange("p (c d) -> p c d", d=D),
                                 axis=mybir.AxisListType.X, op=ALU.add)
         y_ps = [y_pair]
         for a in range(2, TILES):
@@ -283,5 +271,5 @@ def tile_picked_ylift_lift_p_kernel(tc, x_words, x_scales, w1, e_words, e_scales
             nc.vector.scalar_tensor_tensor(out=result[1][:, (a0 - 2) * V:(a1 - 2) * V], in0=piece, scalar=0.0, in1=piece, op0=ALU.max, op1=ALU.mult)
         for b in range(2):
             rows = out[2 * b * P:2 * (b + 1) * P, :]
-            (nc.scalar, nc.sync)[b].dma_start(out=rows.rearrange("(a t) v -> t a v", t=P),
+            nc.sync.dma_start(out=rows.rearrange("(a t) v -> t a v", t=P),
                               in_=result[b][:].rearrange("p (a v) -> p a v", v=V))

@@ -27,6 +27,7 @@ QUARTER = U // 4
 LIST_ROWS = 16
 LINE = 4
 TURNED = 2
+E_ROW = 2 * PACK
 SHIFT = 0.5 - 2.5
 SCORE_BANKS = ("bank4", "bank5", "bank6", "bank7", "bank0", "bank1", "bank7", "bank6")
 
@@ -75,19 +76,19 @@ def tile_picked_ylift_lift_p_kernel(tc, x_words, x_scales, w1, e_words, e_scales
         def load_words(tile, words, c0=0, c1=T):
             nc.sync.dma_start(out=tile[:, c0:c1], in_=words.rearrange("p n t -> p (n t)").bitcast(I32)[:, c0:c1])
 
-        def load_scales(tile, scales, g, queues=(nc.sync,)):
+        def load_scales(tile, scales, g, row, queues=(nc.sync,)):
             for r in range(PACK):
-                queues[r % len(queues)].dma_start(out=tile[PACK * g + r:P:QUADRANT, :].bitcast(I32), in_=scales[g, r:PACK * PACK:PACK, :].bitcast(I32))
+                queues[r % len(queues)].dma_start(out=tile[row + r:P:QUADRANT, :].bitcast(I32), in_=scales[g, r:PACK * PACK:PACK, :].bitcast(I32))
 
         load_words(x_wd[0], x_words[0], 0, T // 4)
         nc.sync.dma_start(neg_t[:], neg)
         nc.sync.dma_start(pos_t[:], pos)
-        load_scales(e_sc, e_scales, 0, (nc.sync, nc.scalar))
+        load_scales(e_sc, e_scales, 0, E_ROW, (nc.sync, nc.scalar))
         load_w(0)
         nc.sync.dma_start(offs_t[:], offs)
-        load_scales(x_sc, x_scales, 0)
+        load_scales(x_sc, x_scales, 0, 0)
         load_w(1)
-        load_scales(x_sc, x_scales, 1)
+        load_scales(x_sc, x_scales, 1, PACK)
         load_words(x_wd[0], x_words[0], T // 4, T)
         load_words(x_wd[1], x_words[1])
         load_words(e_wd, e_words[0])
@@ -170,7 +171,7 @@ def tile_picked_ylift_lift_p_kernel(tc, x_words, x_scales, w1, e_words, e_scales
         def scores(bank, blocks):
             z_ps = psum.tile([P, len(blocks) * QUARTER], F32, name=f"z_ps{blocks[0][0]}{blocks[0][1]}", tag=f"bank{bank}")
             for n, (a, q) in enumerate(blocks):
-                product(z_ps[:, n * QUARTER:(n + 1) * QUARTER], hq[a], hs[a], neg_wd[q], neg_sc[:, q * QUARTER:(q + 1) * QUARTER], True, True)
+                product(z_ps[:, n * QUARTER:(n + 1) * QUARTER], hq[a], hs[a], neg_wd[q], neg_sc[E_ROW:P, q * QUARTER:(q + 1) * QUARTER], True, True)
             return z_ps
 
         ee_first = [keep.tile([P, U], F32, name=f"ee_first{b}", tag=f"ee_first{b}") for b in range(2)]
@@ -197,7 +198,7 @@ def tile_picked_ylift_lift_p_kernel(tc, x_words, x_scales, w1, e_words, e_scales
         def means(y_ps, a, m, start, stop):
             for e in range(2):
                 d = 2 * m + e
-                product(y_ps, hq[a], hs[a], pos_wd[d], pos_sc[:, d * V:(d + 1) * V],
+                product(y_ps, hq[a], hs[a], pos_wd[d], pos_sc[E_ROW:P, d * V:(d + 1) * V],
                         start and e == 0, stop and e == 1)
 
         z_00 = scores(4, [(0, 0)])

@@ -109,6 +109,9 @@ def tile_picked_ylift_lift_p_kernel(tc, x_words, x_scales, w1, e_words, e_scales
         nc.vector.tensor_copy(pos_sc_listed[:].rearrange("p (q d r) -> p q r d", d=D, r=PACK), e_sc[:].indirect(pos_t[:]))
         nc.vector.tensor_copy(xg_sc[:], x_sc[:].indirect(offs_t[:]))
         nc.vector.quantize_mx(out=wq0[:].bitcast(FP8X4), scales=ws[0][:], in_=w_bf[0][:])
+        warm_ps = psum.tile([P, H], F32, name="warm_ps", tag="bank7")
+        for n in range(2):
+            product(warm_ps[:], wq0[:, 0:P], ws[0][:, 0:P], wq0[:], ws[0][:], True, True)
         xg0 = [keep.tile([P, S // 2], U32, name=f"xg0_{i}", align_bytes=64) for i in range(2)]
         for i in range(2):
             picked = entries(offs_t, i * S // 2, (i + 1) * S // 2)

@@ -15,6 +15,7 @@ U8 = mybir.dt.uint8
 FP8X4 = mybir.dt.float8_e4m3fn_x4
 ACT = mybir.ActivationFunctionType
 ALU = mybir.AluOpType
+AXIS_X = mybir.AxisListType.X
 
 P = 128
 PACK = 4
@@ -24,12 +25,12 @@ TILES = S // P
 V = U // D
 HALF = U // 2
 QUARTER = U // 4
+VQ = QUARTER // D
+BANK = 2 * QUARTER
 LIST_ROWS = 16
 LINE = 4
-TURNED = 2
 E_ROW = 2 * PACK
 SHIFT = 0.5 - 2.5
-SCORE_BANKS = ("bank4", "bank5", "bank6", "bank7", "bank0", "bank1", "bank7", "bank6")
 
 
 def tile_picked_ylift_lift_p_kernel(tc, x_words, x_scales, w1, e_words, e_scales, offs, pos, neg, out):
@@ -130,17 +131,11 @@ def tile_picked_ylift_lift_p_kernel(tc, x_words, x_scales, w1, e_words, e_scales
             out=pos_sc[:].bitcast(I32).rearrange("p (d q) -> p d q", d=D),
             in_=pos_sc_listed[:].bitcast(I32).rearrange("p (q d) -> p d q", d=D),
         )
-        neg_q0 = keep.tile([P, QUARTER], U32, name="neg_q0", align_bytes=64)
-        neg_q1 = keep.tile([P, QUARTER], U32, name="neg_q1", align_bytes=64)
-        nc.vector.tensor_copy(neg_q0[:], e_wd[:].bitcast(U32).indirect(entries(neg_t, 0, QUARTER)))
-        nc.vector.tensor_copy(neg_q1[:], e_wd[:].bitcast(U32).indirect(entries(neg_t, QUARTER, HALF)))
         shift = keep.tile([P, 1], F32, name="shift", tag="shift", align_bytes=64)
-        shift_last = keep.tile([P, 1], F32, name="shift_last")
         nc.gpsimd.memset(shift[:], SHIFT)
-        nc.gpsimd.memset(shift_last[:], SHIFT)
 
-        h_bf0 = keep.tile([P, PACK * P], BF16, name="h_bf0", tag="h_bf0", align_bytes=64)
-        h_bf12 = keep.tile([P, 2 * PACK * P], BF16, name="h_bf12", tag="h_bf12", align_bytes=64)
+        h_bf0 = keep.tile([P, PACK * P], BF16, name="h_bf0", align_bytes=64)
+        h_bf12 = keep.tile([P, 2 * PACK * P], BF16, name="h_bf12", align_bytes=64)
         h_bf3 = keep.tile([P, PACK * P], BF16, name="h_bf3", tag="h_bf3", align_bytes=64)
         h_bf = [h_bf0[:], h_bf12[:, 0:PACK * P], h_bf12[:, PACK * P:2 * PACK * P], h_bf3[:]]
         h_ps = [psum.tile([P, PACK * P], F32, name=f"h_ps{a}", tag=f"bank{a}") for a in range(TILES)]
@@ -158,113 +153,113 @@ def tile_picked_ylift_lift_p_kernel(tc, x_words, x_scales, w1, e_words, e_scales
                         in_=h_ps[a][:].rearrange("p (t n) -> p n t", t=PACK),
                     )
 
-        hq0 = keep.tile([P, P], U32, name="hq0", align_bytes=64)
-        hs0 = keep.tile([P, P], U8, name="hs0", align_bytes=64)
-        nc.vector.quantize_mx(out=hq0[:].bitcast(FP8X4), scales=hs0[:], in_=h_bf0[:])
-        hq12 = keep.tile([P, 2 * P], U32, name="hq12", align_bytes=64)
-        hs12 = keep.tile([P, 2 * P], U8, name="hs12", align_bytes=64)
-        nc.vector.quantize_mx(out=hq12[:].bitcast(FP8X4), scales=hs12[:], in_=h_bf12[:])
-        hq3 = keep.tile([P, P], U32, name="hq3", tag="hq3", align_bytes=64)
-        hs3 = keep.tile([P, P], U8, name="hs3", align_bytes=64)
-        nc.vector.quantize_mx(out=hq3[:].bitcast(FP8X4), scales=hs3[:], in_=h_bf3[:])
-        neg_wd = [neg_q0[:], neg_q1[:]]
-        hq = [hq0[:], hq12[:, 0:P], hq12[:, P:2 * P], hq3[:]]
-        hs = [hs0[:], hs12[:, 0:P], hs12[:, P:2 * P], hs3[:]]
+        hq, hs = [], []
 
-        def scores(bank, blocks):
-            z_ps = psum.tile([P, len(blocks) * QUARTER], F32, name=f"z_ps{blocks[0][0]}{blocks[0][1]}", tag=f"bank{bank}")
-            for n, (a, q) in enumerate(blocks):
-                product(z_ps[:, n * QUARTER:(n + 1) * QUARTER], hq[a], hs[a], neg_wd[q], neg_sc[E_ROW:P, q * QUARTER:(q + 1) * QUARTER], True, True)
-            return z_ps
+        def quantise_h(source, tiles):
+            codes = keep.tile([P, tiles * P], U32, name=f"hq{len(hq)}", tag=f"hq{len(hq)}", align_bytes=64)
+            scales = keep.tile([P, tiles * P], U8, name=f"hs{len(hq)}", align_bytes=64)
+            nc.vector.quantize_mx(out=codes[:].bitcast(FP8X4), scales=scales[:], in_=source[:])
+            hq.extend(codes[:, a * P:(a + 1) * P] for a in range(tiles))
+            hs.extend(scales[:, a * P:(a + 1) * P] for a in range(tiles))
 
-        ee_first = [keep.tile([P, U], F32, name=f"ee_first{b}", tag=f"ee_first{b}") for b in range(2)]
-        ee_second = [keep.tile([P, U], F32, name=f"ee_second{i}", tag=f"ee_second{i}") for i in range(2)]
+        def gather_words(target, picked):
+            nc.vector.tensor_copy(target, e_wd[:].bitcast(U32).indirect(picked))
 
-        def exp_first(z_ps, a, v0, v1, bias):
-            c0 = (a % 2) * V // 2
-            nc.scalar.activation(
-                out=ee_first[a // 2][:].rearrange("p (d v) -> p d v", d=D)[:, :, c0 + v0:c0 + v1],
-                in_=z_ps[:].rearrange("p (v d) -> p d v", d=D),
-                func=ACT.Exp,
-                bias=bias[:],
-            )
-
-        def exp_second(z_ps, b, u, bias):
-            nc.scalar.activation(out=ee_second[b][:].rearrange("p (a u c) -> p a u c", a=2, u=2)[:, :, u, :],
-                                 in_=z_ps[:].rearrange("p (a c) -> p a c", a=2), func=ACT.Exp, bias=bias[:])
-
-        def turn(turned_ps, b):
-            for d in range(D):
-                nc.tensor.matmul(turned_ps[:, b * P:(b + 1) * P], ee_first[b][:, d * V:(d + 1) * V], ident[:],
-                                 start=(d == 0), stop=(d == D - 1), is_transpose=True)
-
-        def means(y_ps, a, m, start, stop):
-            for e in range(2):
-                d = 2 * m + e
-                product(y_ps, hq[a], hs[a], pos_wd[d], pos_sc[E_ROW:P, d * V:(d + 1) * V],
-                        start and e == 0, stop and e == 1)
-
-        z_00 = scores(4, [(0, 0)])
-        z_01 = scores(5, [(0, 1)])
-        z_first = [scores(bank, [(a, 0), (a, 1)]) for a, bank in ((1, 6), (2, 7), (3, 0))]
-        exp_first(z_00, 0, 0, V // 4, shift)
+        neg_wd = []
+        for q in range(2):
+            neg_early = keep.tile([P, QUARTER], U32, name=f"neg_early{q}", align_bytes=64)
+            gather_words(neg_early[:], entries(neg_t, q * QUARTER, (q + 1) * QUARTER))
+            neg_wd.append(neg_early[:])
+        quantise_h(h_bf0, 1)
+        quantise_h(h_bf12, 2)
+        quantise_h(h_bf3, 1)
         late = keep.tile([P, HALF + U], U32, name="late", tag="h_bf3", align_bytes=64)
         neg_wd.extend((late[:, 0:QUARTER], late[:, QUARTER:HALF]))
         pos_wd_listed = late[:, HALF:HALF + U]
         for q in range(2, 4):
-            nc.vector.tensor_copy(neg_wd[q], e_wd[:].bitcast(U32).indirect(entries(neg_t, q * QUARTER, (q + 1) * QUARTER)))
-        nc.vector.tensor_copy(pos_wd_listed, e_wd[:].bitcast(U32).indirect(pos_t[:]))
-        pos_wd = []
+            gather_words(neg_wd[q], entries(neg_t, q * QUARTER, (q + 1) * QUARTER))
+        gather_words(pos_wd_listed, pos_t[:])
+
+        def exponentials(bank, blocks, target, walk, bias, **sizes):
+            z_ps = psum.tile([P, len(blocks) * QUARTER], F32, name=f"z_ps{blocks[0][0]}{blocks[0][1]}", tag=f"bank{bank}")
+            for n, (a, q) in enumerate(blocks):
+                product(z_ps[:, n * QUARTER:(n + 1) * QUARTER], hq[a], hs[a], neg_wd[q], neg_sc[E_ROW:P, q * QUARTER:(q + 1) * QUARTER], True, True)
+            nc.scalar.activation(out=target, in_=z_ps[:].rearrange(walk, d=D, **sizes), func=ACT.Exp, bias=bias)
+
+        ee_turn = keep.tile([P, U], F32, name="ee_turn", tag="ee_turn", align_bytes=64)
+        turn_view = ee_turn[:].rearrange("p (d a v) -> p a d v", d=D, a=2)
+        for q in range(2):
+            exponentials(4 + q, [(0, q)], turn_view[:, 0, :, q * VQ:(q + 1) * VQ], "p (v d) -> p d v", SHIFT)
+        exponentials(6, [(1, 0), (1, 1)], turn_view[:, 1], "p (v d) -> p d v", SHIFT)
+
+        fold4 = keep.tile([P, BANK], F32, name="fold4")
+        for i, bank in enumerate((7, 0)):
+            ee_fold = keep.tile([P, BANK], F32, name=f"ee_fold{i}")
+            exponentials(bank, [(2 + i, 0), (2 + i, 1)], ee_fold[:].rearrange("p (d v) -> p d v", d=D), "p (v d) -> p d v", SHIFT)
+            nc.gpsimd.tensor_tensor(out=fold4[:, i * QUARTER:(i + 1) * QUARTER], in0=ee_fold[:, 0:QUARTER], in1=ee_fold[:, QUARTER:BANK], op=ALU.add)
+        fold2 = keep.tile([P, QUARTER], F32, name="fold2")
+        fold4_view = fold4[:].rearrange("p (a e c) -> p a e c", a=2, e=2)
+        nc.gpsimd.tensor_tensor(out=fold2[:].rearrange("p (a c) -> p a c", a=2), in0=fold4_view[:, :, 0, :], in1=fold4_view[:, :, 1, :], op=ALU.add)
+        ee_late = [keep.tile([P, U], F32, name="ee_late0")]
+        ee_last = [keep.tile([P, BANK], F32, name=f"ee_last{i}") for i in range(2)]
+
+        def late_exponentials(bank, b, u, bias):
+            exponentials(bank, [(2 * b, 2 + u), (2 * b + 1, 2 + u)], ee_late[b][:].rearrange("p (a u c) -> p u a c", a=2, u=2)[:, u].rearrange("p a (v d) -> p a v d", d=D),
+                         "p (a v d) -> p a v d", bias, a=2)
+
+        late_exponentials(1, 0, 0, SHIFT)
+        late_exponentials(2, 0, 1, SHIFT)
+        turned_ps = psum.tile([P, P], F32, name="turned_ps", tag="bank3")
+        for d in range(D):
+            nc.tensor.matmul(turned_ps[:], ee_turn[:, d * P:(d + 1) * P], ident[:], start=(d == 0), stop=(d == D - 1), is_transpose=True)
+        exponentials(4, [(2, 2), (2, 3)], ee_last[0][:].rearrange("p (v d) -> p v d", d=D), "p (v d) -> p v d", shift[:])
+        exponentials(0, [(3, 2), (3, 3)], ee_last[1][:].rearrange("p (v d) -> p v d", d=D), "p (v d) -> p v d", SHIFT)
+        turned = keep.tile([P, P], F32, name="turned")
+        nc.vector.tensor_copy(turned[:], turned_ps[:])
+        back_ps = psum.tile([P, P], F32, name="back_ps", tag="bank5")
+        nc.tensor.transpose(back_ps[:], turned[:], ident[:])
+
+        woven = keep.tile([P, U], U32, name="woven", tag="ee_turn", align_bytes=64)
         for d0, d1 in ((0, 2), (2, 4), (4, D)):
-            part = keep.tile([P, (d1 - d0) * V], U32, name=f"pos_wd{d0}", align_bytes=64)
             nc.vector.tensor_copy(
-                out=part[:].bitcast(I32).rearrange("p (d u w) -> p u d w", d=d1 - d0, w=LINE),
+                out=woven[:, d0 * V:d1 * V].bitcast(I32).rearrange("p (d u w) -> p u d w", d=d1 - d0, w=LINE),
                 in_=pos_wd_listed.bitcast(I32).rearrange("p (u w d) -> p u d w", d=D, w=LINE)[:, :, d0:d1, :],
             )
-            pos_wd.extend(part[:, (d - d0) * V:(d - d0 + 1) * V] for d in range(d0, d1))
-        z_second = [scores(1, [(0, 2), (1, 2)]), scores(2, [(2, 2), (3, 2)])]
-        exp_first(z_01, 0, V // 4, V // 2, shift)
-        for a in range(1, TILES):
-            exp_first(z_first[a - 1], a, 0, V // 2, shift)
-        turned_ps = psum.tile([P, 2 * P], F32, name="turned_ps", tag="bank5")
-        turn(turned_ps, 0)
-        z_fourth = [scores(7, [(0, 3), (1, 3)]), scores(0, [(2, 3), (3, 3)])]
-        exp_second(z_second[0], 0, 0, shift)
-        exp_second(z_fourth[0], 0, 1, shift)
-        turn(turned_ps, 1)
-        exp_second(z_second[1], 1, 0, shift)
-        exp_second(z_fourth[1], 1, 1, shift_last)
-        y_pair = psum.tile([P, 2 * V], F32, name="y_pair", tag="bank1")
+
+        def means(y_ps, a, d, start, stop):
+            product(y_ps, hq[a], hs[a], woven[:, d * V:(d + 1) * V], pos_sc[E_ROW:P, d * V:(d + 1) * V], start, stop)
+
+        y_pair = psum.tile([P, 2 * V], F32, name="y_pair", tag="bank6")
         for m in range(D // 2):
             for a in range(2):
-                means(y_pair[:, a * V:(a + 1) * V], a, m, (m, a) == (0, 0), (m, a) == (D // 2 - 1, 1))
-        turned = keep.tile([P, 2 * P], F32, name="turned")
-        nc.vector.tensor_copy(turned[:], turned_ps[:])
-        sums_sb = [keep.tile([P, V], F32, name=f"sums_sb{b}", tag=("ee_first1", "sums_sb1")[b]) for b in range(2)]
-        nc.vector.tensor_reduce(out=sums_sb[0][:], in_=ee_second[0][:].rearrange("p (c d) -> p c d", d=D),
-                                axis=mybir.AxisListType.X, op=ALU.add)
-        sums_ps = psum.tile([P, 2 * V], F32, name="sums_ps", tag="bank4")
-        for b in range(2):
-            nc.tensor.transpose(sums_ps[:, b * V:(b + 1) * V], turned[:, b * P:(b + 1) * P], ident[:])
-        nc.vector.tensor_reduce(out=sums_sb[1][:], in_=ee_second[1][:].rearrange("p (c d) -> p c d", d=D),
-                                axis=mybir.AxisListType.X, op=ALU.add)
+                for e in range(2):
+                    means(y_pair[:, a * V:(a + 1) * V], a, 2 * m + e, (m, a, e) == (0, 0, 0), (m, a, e) == (D // 2 - 1, 1, 1))
         y_ps = [y_pair]
         for a in range(2, TILES):
-            y_ps.append(psum.tile([P, V], F32, name=f"y_ps{a}", tag=("bank6", "bank2")[a - 2]))
-            for m in range(D // 2):
-                means(y_ps[-1][:], a, m, m == 0, m == D // 2 - 1)
+            y_ps.append(psum.tile([P, V], F32, name=f"y_ps{a}", tag=("bank7", "bank1")[a - 2]))
+            for d in range(D):
+                means(y_ps[-1][:], a, d, d == 0, d == D - 1)
 
-        logs_all = keep.tile([P, TILES * V], F32, name="logs_all", tag="shift", align_bytes=64)
-        logs = [logs_all[:, 2 * b * V:2 * (b + 1) * V] for b in range(2)]
-        for b in range(2):
-            for i, sums in enumerate((sums_ps[:, b * V:(b + 1) * V], sums_sb[b][:])):
-                nc.scalar.activation(out=logs[b].rearrange("p (a i v) -> p a i v", a=2, i=2)[:, :, i, :],
-                                     in_=sums.rearrange("p (a v) -> p a v", a=2), func=ACT.Ln)
+        sums23 = keep.tile([P, 2 * V], F32, name="sums23", tag="h_bf3", align_bytes=64)
+        sums23_view = sums23[:].rearrange("p (a h v) -> p a h v", a=2, h=2)
+        fold2_view = fold2[:].rearrange("p (a e v) -> p a e v", a=2, e=2)
+        nc.gpsimd.tensor_tensor(out=sums23_view[:, :, 0, :], in0=fold2_view[:, :, 0, :], in1=fold2_view[:, :, 1, :], op=ALU.add)
+        sums01 = keep.tile([P, V], F32, name="sums01")
+        nc.vector.tensor_reduce(out=sums01[:], in_=ee_late[0][:].rearrange("p (c d) -> p c d", d=D), axis=AXIS_X, op=ALU.add)
+        for i in range(2):
+            nc.vector.tensor_reduce(out=sums23_view[:, i, 1, :], in_=ee_last[i][:].rearrange("p (v d) -> p v d", d=D), axis=AXIS_X, op=ALU.add)
+
+        logs = keep.tile([P, TILES * V], F32, name="logs", tag="shift", align_bytes=64)
+        for i, sums in enumerate((back_ps[:], sums01[:])):
+            nc.scalar.activation(out=logs[:, 0:2 * V].rearrange("p (a i v) -> p a i v", a=2, i=2)[:, :, i, :],
+                                 in_=sums.rearrange("p (a v) -> p a v", a=2), func=ACT.Ln)
+        for i in range(2):
+            nc.scalar.activation(out=logs[:, (2 + i) * V:(3 + i) * V], in_=sums23[:, i * V:(i + 1) * V], func=ACT.Ln)
         pieces = ((0, 2), (2, 3), (3, 4))
         margin = keep.tile([P, TILES * V], F32, name="margin")
         result = [keep.tile([P, 2 * V], F32, name=f"result{b}", tag=("result0", "hq3")[b], align_bytes=64) for b in range(2)]
         for n, (a0, a1) in enumerate(pieces):
-            nc.vector.scalar_tensor_tensor(out=margin[:, a0 * V:a1 * V], in0=y_ps[n][:], scalar=-1.0 / D, in1=logs_all[:, a0 * V:a1 * V],
+            nc.vector.scalar_tensor_tensor(out=margin[:, a0 * V:a1 * V], in0=y_ps[n][:], scalar=-1.0 / D, in1=logs[:, a0 * V:a1 * V],
                                            op0=ALU.mult, op1=ALU.add)
         positive = keep.tile([P, 2 * V], F32, name="positive")
         for func, source, target in ((ACT.Relu, margin, positive), (ACT.Square, positive, result[0])):

@@ -135,7 +135,7 @@ def tile_picked_ylift_lift_p_kernel(tc, x_words, x_scales, w1, e_words, e_scales
         nc.gpsimd.memset(shift[:], SHIFT)
 
         h_bf0 = keep.tile([P, PACK * P], BF16, name="h_bf0", align_bytes=64)
-        h_bf12 = keep.tile([P, 2 * PACK * P], BF16, name="h_bf12", align_bytes=64)
+        h_bf12 = keep.tile([P, 2 * PACK * P], BF16, name="h_bf12", tag="h_bf12", align_bytes=64)
         h_bf3 = keep.tile([P, PACK * P], BF16, name="h_bf3", tag="h_bf3", align_bytes=64)
         h_bf = [h_bf0[:], h_bf12[:, 0:PACK * P], h_bf12[:, PACK * P:2 * PACK * P], h_bf3[:]]
         h_ps = [psum.tile([P, PACK * P], F32, name=f"h_ps{a}", tag=f"bank{a}") for a in range(TILES)]
@@ -173,7 +173,7 @@ def tile_picked_ylift_lift_p_kernel(tc, x_words, x_scales, w1, e_words, e_scales
         quantise_h(h_bf0, 1)
         quantise_h(h_bf12, 2)
         quantise_h(h_bf3, 1)
-        late = keep.tile([P, HALF + U], U32, name="late", tag="h_bf3", align_bytes=64)
+        late = keep.tile([P, HALF + U], U32, name="late", tag="h_bf12", align_bytes=64)
         neg_wd.extend((late[:, 0:QUARTER], late[:, QUARTER:HALF]))
         pos_wd_listed = late[:, HALF:HALF + U]
         for q in range(2, 4):
@@ -197,9 +197,6 @@ def tile_picked_ylift_lift_p_kernel(tc, x_words, x_scales, w1, e_words, e_scales
             ee_fold = keep.tile([P, BANK], F32, name=f"ee_fold{i}")
             exponentials(bank, [(2 + i, 0), (2 + i, 1)], ee_fold[:].rearrange("p (d v) -> p d v", d=D), "p (v d) -> p d v", SHIFT)
             nc.gpsimd.tensor_tensor(out=fold4[:, i * QUARTER:(i + 1) * QUARTER], in0=ee_fold[:, 0:QUARTER], in1=ee_fold[:, QUARTER:BANK], op=ALU.add)
-        fold2 = keep.tile([P, QUARTER], F32, name="fold2")
-        fold4_view = fold4[:].rearrange("p (a e c) -> p a e c", a=2, e=2)
-        nc.gpsimd.tensor_tensor(out=fold2[:].rearrange("p (a c) -> p a c", a=2), in0=fold4_view[:, :, 0, :], in1=fold4_view[:, :, 1, :], op=ALU.add)
         ee_late = [keep.tile([P, U], F32, name="ee_late0")]
         ee_last = [keep.tile([P, BANK], F32, name=f"ee_last{i}") for i in range(2)]
 
@@ -240,7 +237,10 @@ def tile_picked_ylift_lift_p_kernel(tc, x_words, x_scales, w1, e_words, e_scales
             for d in range(D):
                 means(y_ps[-1][:], a, d, d == 0, d == D - 1)
 
-        sums23 = keep.tile([P, 2 * V], F32, name="sums23", tag="h_bf3", align_bytes=64)
+        fold2 = keep.tile([P, QUARTER], F32, name="fold2", tag="h_bf12", align_bytes=64)
+        fold4_view = fold4[:].rearrange("p (a e c) -> p a e c", a=2, e=2)
+        nc.gpsimd.tensor_tensor(out=fold2[:].rearrange("p (a c) -> p a c", a=2), in0=fold4_view[:, :, 0, :], in1=fold4_view[:, :, 1, :], op=ALU.add)
+        sums23 = keep.tile([P, 2 * V], F32, name="sums23")
         sums23_view = sums23[:].rearrange("p (a h v) -> p a h v", a=2, h=2)
         fold2_view = fold2[:].rearrange("p (a e v) -> p a e v", a=2, e=2)
         nc.gpsimd.tensor_tensor(out=sums23_view[:, :, 0, :], in0=fold2_view[:, :, 0, :], in1=fold2_view[:, :, 1, :], op=ALU.add)

@@ -250,16 +250,17 @@ def tile_picked_ylift_lift_p_kernel(tc, x_words, x_scales, w1, e_words, e_scales
             nc.vector.tensor_reduce(out=sums23_view[:, i, 1, :], in_=ee_last[i][:].rearrange("p (v d) -> p v d", d=D), axis=AXIS_X, op=ALU.add)
 
         logs = keep.tile([P, TILES * V], F32, name="logs", tag="shift", align_bytes=64)
-        for i, sums in enumerate((back_ps[:], sums01[:])):
-            nc.scalar.activation(out=logs[:, 0:2 * V].rearrange("p (a i v) -> p a i v", a=2, i=2)[:, :, i, :],
-                                 in_=sums.rearrange("p (a v) -> p a v", a=2), func=ACT.Ln)
+        logs01 = logs[:, 0:2 * V].rearrange("p (a h v) -> p a h v", a=2, h=2)
+        nc.scalar.activation(out=logs01[:, :, 0, :], in_=back_ps[:].rearrange("p (a v) -> p a v", a=2), func=ACT.Ln)
+        for i in range(2):
+            nc.scalar.activation(out=logs01[:, i, 1, :], in_=sums01[:, i * V // 2:(i + 1) * V // 2], func=ACT.Ln)
         for i in range(2):
             nc.scalar.activation(out=logs[:, (2 + i) * V:(3 + i) * V], in_=sums23[:, i * V:(i + 1) * V], func=ACT.Ln)
         pieces = ((0, 2), (2, 3), (3, 4))
         margin = keep.tile([P, TILES * V], F32, name="margin")
         result = [keep.tile([P, 2 * V], F32, name=f"result{b}", tag=("result0", "hq3")[b], align_bytes=64) for b in range(2)]
-        for n, (a0, a1) in enumerate(pieces):
-            nc.vector.scalar_tensor_tensor(out=margin[:, a0 * V:a1 * V], in0=y_ps[n][:], scalar=-1.0 / D, in1=logs[:, a0 * V:a1 * V],
+        for a, y_tile in enumerate((y_pair[:, 0:V], y_pair[:, V:2 * V], y_ps[1][:], y_ps[2][:])):
+            nc.vector.scalar_tensor_tensor(out=margin[:, a * V:(a + 1) * V], in0=y_tile, scalar=-1.0 / D, in1=logs[:, a * V:(a + 1) * V],
                                            op0=ALU.mult, op1=ALU.add)
         positive = keep.tile([P, 2 * V], F32, name="positive")
         for func, source, target in ((ACT.Relu, margin, positive), (ACT.Square, positive, result[0])):

@@ -68,29 +68,33 @@ def tile_picked_ylift_lift_p_kernel(tc, x_words, x_scales, w1, e_words, e_scales
         nc.vector.memset(e_sc[:, 0:W // 2].bitcast(I32), 0)
         nc.gpsimd.memset(e_sc[:, W // 2:W].bitcast(I32), 0)
         nc.vector.memset(x_sc[:].bitcast(I32), 0)
+        shift_set = keep.tile([P, 1], F32, name="shift_set")
+        nc.gpsimd.memset(shift_set[:], SHIFT)
+        shift = keep.tile([P, 1], F32, name="shift", tag="shift", align_bytes=64)
+        nc.scalar.activation(out=shift[:], in_=shift_set[:], func=ACT.Copy)
         make_identity(nc, ident[:])
 
-        def load_w(g):
+        def load_w(g, j0=0, j1=PACK):
             rows = w1[g * P * PACK:(g + 1) * P * PACK, :]
-            nc.sync.dma_start(out=w_raw[g][:], in_=rows.rearrange("(p j) c -> p j c", j=PACK))
+            nc.sync.dma_start(out=w_raw[g][:, j0:j1, :], in_=rows.rearrange("(p j) c -> p j c", j=PACK)[:, j0:j1, :])
 
-        def load_words(tile, words, c0=0, c1=T):
-            nc.sync.dma_start(out=tile[:, c0:c1], in_=words.rearrange("p n t -> p (n t)").bitcast(I32)[:, c0:c1])
+        def load_words(tile, words):
+            nc.sync.dma_start(out=tile[:], in_=words.rearrange("p n t -> p (n t)").bitcast(I32))
 
         def load_scales(tile, scales, g, row, queues=(nc.sync,)):
             for r in range(PACK):
                 queues[r % len(queues)].dma_start(out=tile[row + r:P:QUADRANT, :].bitcast(I32), in_=scales[g, r:PACK * PACK:PACK, :].bitcast(I32))
 
-        load_words(x_wd[0], x_words[0], 0, T // 4)
+        load_w(0, 0, 1)
         nc.sync.dma_start(neg_t[:], neg)
         nc.sync.dma_start(pos_t[:], pos)
         load_scales(e_sc, e_scales, 0, E_ROW, (nc.sync, nc.scalar))
-        load_w(0)
+        load_w(0, 1, PACK)
         nc.sync.dma_start(offs_t[:], offs)
         load_scales(x_sc, x_scales, 0, 0)
         load_w(1)
         load_scales(x_sc, x_scales, 1, PACK)
-        load_words(x_wd[0], x_words[0], T // 4, T)
+        load_words(x_wd[0], x_words[0])
         load_words(x_wd[1], x_words[1])
         load_words(e_wd, e_words[0])
 
@@ -131,8 +135,6 @@ def tile_picked_ylift_lift_p_kernel(tc, x_words, x_scales, w1, e_words, e_scales
             out=pos_sc[:].bitcast(I32).rearrange("p (d q) -> p d q", d=D),
             in_=pos_sc_listed[:].bitcast(I32).rearrange("p (q d) -> p d q", d=D),
         )
-        shift = keep.tile([P, 1], F32, name="shift", tag="shift", align_bytes=64)
-        nc.gpsimd.memset(shift[:], SHIFT)
 
         h_bf0 = keep.tile([P, PACK * P], BF16, name="h_bf0", align_bytes=64)
         h_bf12 = keep.tile([P, 2 * PACK * P], BF16, name="h_bf12", tag="h_bf12", align_bytes=64)

@@ -30,6 +30,7 @@ BANK = 2 * QUARTER
 LIST_ROWS = 16
 LINE = 4
 E_ROW = 2 * PACK
+SCALAR_SHARE = 3 * P // 4
 SHIFT = 0.5 - 2.5
 
 
@@ -101,11 +102,15 @@ def tile_picked_ylift_lift_p_kernel(tc, x_words, x_scales, w1, e_words, e_scales
         w_bf = [keep.tile([P, PACK * H], BF16, name=f"w_bf{g}", tag=f"w_bf{g}", align_bytes=64) for g in range(PASSES)]
         wq0 = keep.tile([P, H], U32, name="wq0", align_bytes=64)
         ws = [keep.tile([P, H], U8, name=f"ws{g}", align_bytes=64) for g in range(PASSES)]
-        for g in range(PASSES):
+        for g, m1 in enumerate((SCALAR_SHARE, P)):
             nc.scalar.copy(
-                out=w_bf[g][:].rearrange("p (t m j) -> p m j t", t=PACK, j=PACK),
-                in_=w_raw[g][:].rearrange("p j (m t) -> p m j t", t=PACK),
+                out=w_bf[g][:].rearrange("p (t m j) -> p m j t", t=PACK, j=PACK)[:, 0:m1],
+                in_=w_raw[g][:].rearrange("p j (m t) -> p m j t", t=PACK)[:, 0:m1],
             )
+        nc.gpsimd.tensor_copy(
+            out=w_bf[0][:].rearrange("p (t m j) -> p m t j", t=PACK, j=PACK)[:, SCALAR_SHARE:P],
+            in_=w_raw[0][:].rearrange("p j (m t) -> p m t j", t=PACK)[:, SCALAR_SHARE:P],
+        )
 
         neg_sc = keep.tile([P, U], U8, name="neg_sc", align_bytes=64)
         pos_sc_listed = keep.tile([P, U], U8, name="pos_sc_listed", align_bytes=64)
@@ -258,19 +263,14 @@ def tile_picked_ylift_lift_p_kernel(tc, x_words, x_scales, w1, e_words, e_scales
             nc.scalar.activation(out=logs01[:, i, 1, :], in_=sums01[:, i * V // 2:(i + 1) * V // 2], func=ACT.Ln)
         for i in range(2):
             nc.scalar.activation(out=logs[:, (2 + i) * V:(3 + i) * V], in_=sums23[:, i * V:(i + 1) * V], func=ACT.Ln)
-        pieces = ((0, 2), (2, 3), (3, 4))
         margin = keep.tile([P, TILES * V], F32, name="margin")
         result = [keep.tile([P, 2 * V], F32, name=f"result{b}", tag=("result0", "hq3")[b], align_bytes=64) for b in range(2)]
         for a, y_tile in enumerate((y_pair[:, 0:V], y_pair[:, V:2 * V], y_ps[1][:], y_ps[2][:])):
             nc.vector.scalar_tensor_tensor(out=margin[:, a * V:(a + 1) * V], in0=y_tile, scalar=-1.0 / D, in1=logs[:, a * V:(a + 1) * V],
                                            op0=ALU.mult, op1=ALU.add)
-        positive = keep.tile([P, 2 * V], F32, name="positive")
-        for func, source, target in ((ACT.Relu, margin, positive), (ACT.Square, positive, result[0])):
-            for a in range(2):
-                nc.scalar.activation(out=target[:, a * V:(a + 1) * V], in_=source[:, a * V:(a + 1) * V], func=func)
-        for a0, a1 in pieces[1:]:
-            piece = margin[:, a0 * V:a1 * V]
-            nc.vector.scalar_tensor_tensor(out=result[1][:, (a0 - 2) * V:(a1 - 2) * V], in0=piece, scalar=0.0, in1=piece, op0=ALU.max, op1=ALU.mult)
+        for a in range(TILES):
+            piece = margin[:, a * V:(a + 1) * V]
+            nc.vector.scalar_tensor_tensor(out=result[a // 2][:, (a % 2) * V:(a % 2 + 1) * V], in0=piece, scalar=0.0, in1=piece, op0=ALU.max, op1=ALU.mult)
         for b in range(2):
             rows = out[2 * b * P:2 * (b + 1) * P, :]
             nc.sync.dma_start(out=rows.rearrange("(a t) v -> t a v", t=P),

@@ -66,8 +66,8 @@ def tile_picked_ylift_lift_p_kernel(tc, x_words, x_scales, w1, e_words, e_scales
         w_raw = [keep.tile([P, PACK, H], F32, name=f"w_raw{g}", align_bytes=64) for g in range(PASSES)]
         ident = keep.tile([P, P], F32, name="ident")
 
-        nc.vector.memset(e_sc[:, 0:W // 2].bitcast(I32), 0)
-        nc.gpsimd.memset(e_sc[:, W // 2:W].bitcast(I32), 0)
+        nc.vector.memset(e_sc[:, 0:W // 4].bitcast(I32), 0)
+        nc.gpsimd.memset(e_sc[:, W // 4:W].bitcast(I32), 0)
         nc.vector.memset(x_sc[:].bitcast(I32), 0)
         shift_set = keep.tile([P, 1], F32, name="shift_set")
         nc.gpsimd.memset(shift_set[:], SHIFT)
@@ -271,7 +271,6 @@ def tile_picked_ylift_lift_p_kernel(tc, x_words, x_scales, w1, e_words, e_scales
         for a in range(TILES):
             piece = margin[:, a * V:(a + 1) * V]
             nc.vector.scalar_tensor_tensor(out=result[a // 2][:, (a % 2) * V:(a % 2 + 1) * V], in0=piece, scalar=0.0, in1=piece, op0=ALU.max, op1=ALU.mult)
-        for b in range(2):
-            rows = out[2 * b * P:2 * (b + 1) * P, :]
-            nc.sync.dma_start(out=rows.rearrange("(a t) v -> t a v", t=P),
-                              in_=result[b][:].rearrange("p (a v) -> p a v", v=V))
+        nc.sync.dma_start(out=out[0:2 * P, :].rearrange("(a t) v -> t a v", t=P), in_=result[0][:].rearrange("p (a v) -> p a v", v=V))
+        for a in range(2, TILES):
+            nc.sync.dma_start(out=out[a * P:(a + 1) * P, :], in_=result[1][:, (a - 2) * V:(a - 1) * V])

from contextlib import ExitStack

import concourse.mybir as mybir
from concourse.masks import make_identity

K, T, S, H, D, W, U = 1024, 2048, 512, 512, 8, 2048, 1024
FLOPS = 2 * K * H * S + 2 * 2 * H * S * U

F32 = mybir.dt.float32
BF16 = mybir.dt.bfloat16
I32 = mybir.dt.int32
U32 = mybir.dt.uint32
U16 = mybir.dt.uint16
U8 = mybir.dt.uint8
FP8X4 = mybir.dt.float8_e4m3fn_x4
ACT = mybir.ActivationFunctionType
ALU = mybir.AluOpType
AXIS_X = mybir.AxisListType.X

P = 128
PACK = 4
QUADRANT = 32
PASSES = K // (P * PACK)
TILES = S // P
V = U // D
HALF = U // 2
QUARTER = U // 4
VQ = QUARTER // D
BANK = 2 * QUARTER
LIST_ROWS = 16
LINE = 4
E_ROW = 2 * PACK
SCALAR_SHARE = 3 * P // 4
SHIFT = 0.5 - 2.5


def tile_picked_ylift_lift_p_kernel(tc, x_words, x_scales, w1, e_words, e_scales, offs, pos, neg, out):
    nc = tc.nc
    with ExitStack() as ctx:
        lists = ctx.enter_context(tc.tile_pool(name="lists", bufs=1))
        keep = ctx.enter_context(tc.tile_pool(name="keep", bufs=1))
        psum = ctx.enter_context(tc.psum_pool(name="psum", bufs=1))

        def entries(list_tile, first, end):
            return list_tile[:, first // LIST_ROWS:end // LIST_ROWS]

        def product(acc, stationary, stationary_scales, moving, moving_scales, start, stop):
            nc.tensor.matmul_mx(
                out=acc,
                lhsT=stationary.bitcast(FP8X4),
                lhsT_scale=stationary_scales,
                rhs=moving.bitcast(FP8X4),
                rhs_scale=moving_scales,
                start=start,
                stop=stop,
            )

        offs_t = lists.tile([P, S // LIST_ROWS], U16, name="offs_t")
        pos_t = lists.tile([P, U // LIST_ROWS], U16, name="pos_t")
        neg_t = lists.tile([P, U // LIST_ROWS], U16, name="neg_t")

        e_sc = keep.tile([P, W], U8, name="e_sc", align_bytes=64)
        x_sc = keep.tile([P, T], U8, name="x_sc", align_bytes=64)
        e_wd = keep.tile([P, W], I32, name="e_wd", align_bytes=64)
        x_wd = [keep.tile([P, T], I32, name=f"x_wd{g}", tag=f"x_wd{g}", align_bytes=64) for g in range(PASSES)]
        w_raw = [keep.tile([P, PACK, H], F32, name=f"w_raw{g}", align_bytes=64) for g in range(PASSES)]
        ident = keep.tile([P, P], F32, name="ident")

        nc.vector.memset(e_sc[:, 0:W // 4].bitcast(I32), 0)
        nc.gpsimd.memset(e_sc[:, W // 4:W].bitcast(I32), 0)
        nc.vector.memset(x_sc[:].bitcast(I32), 0)
        shift_set = keep.tile([P, 1], F32, name="shift_set")
        nc.gpsimd.memset(shift_set[:], SHIFT)
        shift = keep.tile([P, 1], F32, name="shift", tag="shift", align_bytes=64)
        nc.scalar.activation(out=shift[:], in_=shift_set[:], func=ACT.Copy)
        make_identity(nc, ident[:])

        def load_w(g, j0=0, j1=PACK):
            rows = w1[g * P * PACK:(g + 1) * P * PACK, :]
            nc.sync.dma_start(out=w_raw[g][:, j0:j1, :], in_=rows.rearrange("(p j) c -> p j c", j=PACK)[:, j0:j1, :])

        def load_words(tile, words):
            nc.sync.dma_start(out=tile[:], in_=words.rearrange("p n t -> p (n t)").bitcast(I32))

        def load_scales(tile, scales, g, row, queues=(nc.sync,)):
            for r in range(PACK):
                queues[r % len(queues)].dma_start(out=tile[row + r:P:QUADRANT, :].bitcast(I32), in_=scales[g, r:PACK * PACK:PACK, :].bitcast(I32))

        load_w(0, 0, 1)
        nc.sync.dma_start(neg_t[:], neg)
        nc.sync.dma_start(pos_t[:], pos)
        load_scales(e_sc, e_scales, 0, E_ROW, (nc.sync, nc.scalar))
        load_w(0, 1, PACK)
        nc.sync.dma_start(offs_t[:], offs)
        load_scales(x_sc, x_scales, 0, 0)
        load_w(1)
        load_scales(x_sc, x_scales, 1, PACK)
        load_words(x_wd[0], x_words[0])
        load_words(x_wd[1], x_words[1])
        load_words(e_wd, e_words[0])

        w_bf = [keep.tile([P, PACK * H], BF16, name=f"w_bf{g}", tag=f"w_bf{g}", align_bytes=64) for g in range(PASSES)]
        wq0 = keep.tile([P, H], U32, name="wq0", align_bytes=64)
        ws = [keep.tile([P, H], U8, name=f"ws{g}", align_bytes=64) for g in range(PASSES)]
        for g, m1 in enumerate((SCALAR_SHARE, P)):
            nc.scalar.copy(
                out=w_bf[g][:].rearrange("p (t m j) -> p m j t", t=PACK, j=PACK)[:, 0:m1],
                in_=w_raw[g][:].rearrange("p j (m t) -> p m j t", t=PACK)[:, 0:m1],
            )
        nc.gpsimd.tensor_copy(
            out=w_bf[0][:].rearrange("p (t m j) -> p m t j", t=PACK, j=PACK)[:, SCALAR_SHARE:P],
            in_=w_raw[0][:].rearrange("p j (m t) -> p m t j", t=PACK)[:, SCALAR_SHARE:P],
        )

        neg_sc = keep.tile([P, U], U8, name="neg_sc", align_bytes=64)
        pos_sc_listed = keep.tile([P, U], U8, name="pos_sc_listed", align_bytes=64)
        xg_sc = keep.tile([P, S], U8, name="xg_sc", align_bytes=64)
        nc.vector.tensor_copy(neg_sc[:], e_sc[:].indirect(neg_t[:]))
        nc.vector.tensor_copy(pos_sc_listed[:].rearrange("p (q d r) -> p q r d", d=D, r=PACK), e_sc[:].indirect(pos_t[:]))
        nc.vector.tensor_copy(xg_sc[:], x_sc[:].indirect(offs_t[:]))
        nc.vector.quantize_mx(out=wq0[:].bitcast(FP8X4), scales=ws[0][:], in_=w_bf[0][:])
        warm_ps = psum.tile([P, H], F32, name="warm_ps", tag="bank7")
        for n in range(2):
            product(warm_ps[:], wq0[:, 0:P], ws[0][:, 0:P], wq0[:], ws[0][:], True, True)
        xg0 = [keep.tile([P, S // 2], U32, name=f"xg0_{i}", align_bytes=64) for i in range(2)]
        for i in range(2):
            picked = entries(offs_t, i * S // 2, (i + 1) * S // 2)
            nc.vector.tensor_copy(xg0[i][:], x_wd[0][:].bitcast(U32).indirect(picked))
        wq1 = keep.tile([P, H], U32, name="wq1", tag="x_wd0", align_bytes=64)
        nc.vector.quantize_mx(out=wq1[:].bitcast(FP8X4), scales=ws[1][:], in_=w_bf[1][:])
        wq = [wq0, wq1]
        x_parts = ((0, 1), (1, 2), (2, 4))
        xg1 = []
        for a0, a1 in x_parts:
            part = keep.tile([P, (a1 - a0) * P], U32, name=f"xg1_{a0}", align_bytes=64)
            nc.vector.tensor_copy(part[:], x_wd[1][:].bitcast(U32).indirect(entries(offs_t, a0 * P, a1 * P)))
            xg1.extend(part[:, (a - a0) * P:(a - a0 + 1) * P] for a in range(a0, a1))
        pos_sc = keep.tile([P, U], U8, name="pos_sc", tag="x_wd1", align_bytes=64)
        nc.vector.tensor_copy(
            out=pos_sc[:].bitcast(I32).rearrange("p (d q) -> p d q", d=D),
            in_=pos_sc_listed[:].bitcast(I32).rearrange("p (q d) -> p d q", d=D),
        )

        h_bf0 = keep.tile([P, PACK * P], BF16, name="h_bf0", align_bytes=64)
        h_bf12 = keep.tile([P, 2 * PACK * P], BF16, name="h_bf12", tag="h_bf12", align_bytes=64)
        h_bf3 = keep.tile([P, PACK * P], BF16, name="h_bf3", tag="h_bf3", align_bytes=64)
        h_bf = [h_bf0[:], h_bf12[:, 0:PACK * P], h_bf12[:, PACK * P:2 * PACK * P], h_bf3[:]]
        h_ps = [psum.tile([P, PACK * P], F32, name=f"h_ps{a}", tag=f"bank{a}") for a in range(TILES)]
        for g in range(PASSES):
            for a in range(TILES):
                anchors = slice(a * P, (a + 1) * P)
                x_codes = [xg0[a // 2][:, (a % 2) * P:(a % 2 + 1) * P], xg1[a]]
                for t in range(PACK):
                    channels = slice(t * P, (t + 1) * P)
                    product(h_ps[a][:, channels], wq[g][:, channels], ws[g][:, channels], x_codes[g], xg_sc[PACK * g:P, anchors],
                            g == 0 and t == 0, g == PASSES - 1 and t == PACK - 1)
                if g == PASSES - 1:
                    nc.scalar.copy(
                        out=h_bf[a].rearrange("p (n t) -> p n t", t=PACK),
                        in_=h_ps[a][:].rearrange("p (t n) -> p n t", t=PACK),
                    )

        hq, hs = [], []

        def quantise_h(source, tiles):
            codes = keep.tile([P, tiles * P], U32, name=f"hq{len(hq)}", tag=f"hq{len(hq)}", align_bytes=64)
            scales = keep.tile([P, tiles * P], U8, name=f"hs{len(hq)}", align_bytes=64)
            nc.vector.quantize_mx(out=codes[:].bitcast(FP8X4), scales=scales[:], in_=source[:])
            hq.extend(codes[:, a * P:(a + 1) * P] for a in range(tiles))
            hs.extend(scales[:, a * P:(a + 1) * P] for a in range(tiles))

        def gather_words(target, picked):
            nc.vector.tensor_copy(target, e_wd[:].bitcast(U32).indirect(picked))

        neg_wd = []
        for q in range(2):
            neg_early = keep.tile([P, QUARTER], U32, name=f"neg_early{q}", align_bytes=64)
            gather_words(neg_early[:], entries(neg_t, q * QUARTER, (q + 1) * QUARTER))
            neg_wd.append(neg_early[:])
        quantise_h(h_bf0, 1)
        quantise_h(h_bf12, 2)
        quantise_h(h_bf3, 1)
        late = keep.tile([P, HALF + U], U32, name="late", tag="h_bf12", align_bytes=64)
        neg_wd.extend((late[:, 0:QUARTER], late[:, QUARTER:HALF]))
        pos_wd_listed = late[:, HALF:HALF + U]
        for q in range(2, 4):
            gather_words(neg_wd[q], entries(neg_t, q * QUARTER, (q + 1) * QUARTER))
        gather_words(pos_wd_listed, pos_t[:])

        def exponentials(bank, blocks, target, walk, bias, **sizes):
            z_ps = psum.tile([P, len(blocks) * QUARTER], F32, name=f"z_ps{blocks[0][0]}{blocks[0][1]}", tag=f"bank{bank}")
            for n, (a, q) in enumerate(blocks):
                product(z_ps[:, n * QUARTER:(n + 1) * QUARTER], hq[a], hs[a], neg_wd[q], neg_sc[E_ROW:P, q * QUARTER:(q + 1) * QUARTER], True, True)
            nc.scalar.activation(out=target, in_=z_ps[:].rearrange(walk, d=D, **sizes), func=ACT.Exp, bias=bias)

        ee_turn = keep.tile([P, U], F32, name="ee_turn", tag="ee_turn", align_bytes=64)
        turn_view = ee_turn[:].rearrange("p (d a v) -> p a d v", d=D, a=2)
        for q in range(2):
            exponentials(4 + q, [(0, q)], turn_view[:, 0, :, q * VQ:(q + 1) * VQ], "p (v d) -> p d v", SHIFT)
        exponentials(6, [(1, 0), (1, 1)], turn_view[:, 1], "p (v d) -> p d v", SHIFT)

        fold4 = keep.tile([P, BANK], F32, name="fold4")
        for i, bank in enumerate((7, 0)):
            ee_fold = keep.tile([P, BANK], F32, name=f"ee_fold{i}")
            exponentials(bank, [(2 + i, 0), (2 + i, 1)], ee_fold[:].rearrange("p (d v) -> p d v", d=D), "p (v d) -> p d v", SHIFT)
            nc.gpsimd.tensor_tensor(out=fold4[:, i * QUARTER:(i + 1) * QUARTER], in0=ee_fold[:, 0:QUARTER], in1=ee_fold[:, QUARTER:BANK], op=ALU.add)
        ee_late = [keep.tile([P, U], F32, name="ee_late0")]
        ee_last = [keep.tile([P, BANK], F32, name=f"ee_last{i}") for i in range(2)]

        def late_exponentials(bank, b, u, bias):
            exponentials(bank, [(2 * b, 2 + u), (2 * b + 1, 2 + u)], ee_late[b][:].rearrange("p (a u c) -> p u a c", a=2, u=2)[:, u].rearrange("p a (v d) -> p a v d", d=D),
                         "p (a v d) -> p a v d", bias, a=2)

        late_exponentials(1, 0, 0, SHIFT)
        late_exponentials(2, 0, 1, SHIFT)
        turned_ps = psum.tile([P, P], F32, name="turned_ps", tag="bank3")
        for d in range(D):
            nc.tensor.matmul(turned_ps[:], ee_turn[:, d * P:(d + 1) * P], ident[:], start=(d == 0), stop=(d == D - 1), is_transpose=True)
        exponentials(4, [(2, 2), (2, 3)], ee_last[0][:].rearrange("p (v d) -> p v d", d=D), "p (v d) -> p v d", shift[:])
        exponentials(0, [(3, 2), (3, 3)], ee_last[1][:].rearrange("p (v d) -> p v d", d=D), "p (v d) -> p v d", SHIFT)
        turned = keep.tile([P, P], F32, name="turned")
        nc.vector.tensor_copy(turned[:], turned_ps[:])
        back_ps = psum.tile([P, P], F32, name="back_ps", tag="bank5")
        nc.tensor.transpose(back_ps[:], turned[:], ident[:])

        woven = keep.tile([P, U], U32, name="woven", tag="ee_turn", align_bytes=64)
        for d0, d1 in ((0, 2), (2, 4), (4, D)):
            nc.vector.tensor_copy(
                out=woven[:, d0 * V:d1 * V].bitcast(I32).rearrange("p (d u w) -> p u d w", d=d1 - d0, w=LINE),
                in_=pos_wd_listed.bitcast(I32).rearrange("p (u w d) -> p u d w", d=D, w=LINE)[:, :, d0:d1, :],
            )

        def means(y_ps, a, d, start, stop):
            product(y_ps, hq[a], hs[a], woven[:, d * V:(d + 1) * V], pos_sc[E_ROW:P, d * V:(d + 1) * V], start, stop)

        y_pair = psum.tile([P, 2 * V], F32, name="y_pair", tag="bank6")
        for m in range(D // 2):
            for a in range(2):
                for e in range(2):
                    means(y_pair[:, a * V:(a + 1) * V], a, 2 * m + e, (m, a, e) == (0, 0, 0), (m, a, e) == (D // 2 - 1, 1, 1))
        y_ps = [y_pair]
        for a in range(2, TILES):
            y_ps.append(psum.tile([P, V], F32, name=f"y_ps{a}", tag=("bank7", "bank1")[a - 2]))
            for d in range(D):
                means(y_ps[-1][:], a, d, d == 0, d == D - 1)

        fold2 = keep.tile([P, QUARTER], F32, name="fold2", tag="h_bf12", align_bytes=64)
        fold4_view = fold4[:].rearrange("p (a e c) -> p a e c", a=2, e=2)
        nc.gpsimd.tensor_tensor(out=fold2[:].rearrange("p (a c) -> p a c", a=2), in0=fold4_view[:, :, 0, :], in1=fold4_view[:, :, 1, :], op=ALU.add)
        sums23 = keep.tile([P, 2 * V], F32, name="sums23")
        sums23_view = sums23[:].rearrange("p (a h v) -> p a h v", a=2, h=2)
        fold2_view = fold2[:].rearrange("p (a e v) -> p a e v", a=2, e=2)
        nc.gpsimd.tensor_tensor(out=sums23_view[:, :, 0, :], in0=fold2_view[:, :, 0, :], in1=fold2_view[:, :, 1, :], op=ALU.add)
        sums01 = keep.tile([P, V], F32, name="sums01")
        nc.vector.tensor_reduce(out=sums01[:], in_=ee_late[0][:].rearrange("p (c d) -> p c d", d=D), axis=AXIS_X, op=ALU.add)
        for i in range(2):
            nc.vector.tensor_reduce(out=sums23_view[:, i, 1, :], in_=ee_last[i][:].rearrange("p (v d) -> p v d", d=D), axis=AXIS_X, op=ALU.add)

        logs = keep.tile([P, TILES * V], F32, name="logs", tag="shift", align_bytes=64)
        logs01 = logs[:, 0:2 * V].rearrange("p (a h v) -> p a h v", a=2, h=2)
        nc.scalar.activation(out=logs01[:, :, 0, :], in_=back_ps[:].rearrange("p (a v) -> p a v", a=2), func=ACT.Ln)
        for i in range(2):
            nc.scalar.activation(out=logs01[:, i, 1, :], in_=sums01[:, i * V // 2:(i + 1) * V // 2], func=ACT.Ln)
        for i in range(2):
            nc.scalar.activation(out=logs[:, (2 + i) * V:(3 + i) * V], in_=sums23[:, i * V:(i + 1) * V], func=ACT.Ln)
        margin = keep.tile([P, TILES * V], F32, name="margin")
        result = [keep.tile([P, 2 * V], F32, name=f"result{b}", tag=("result0", "hq3")[b], align_bytes=64) for b in range(2)]
        for a, y_tile in enumerate((y_pair[:, 0:V], y_pair[:, V:2 * V], y_ps[1][:], y_ps[2][:])):
            nc.vector.scalar_tensor_tensor(out=margin[:, a * V:(a + 1) * V], in0=y_tile, scalar=-1.0 / D, in1=logs[:, a * V:(a + 1) * V],
                                           op0=ALU.mult, op1=ALU.add)
        for a in range(TILES):
            piece = margin[:, a * V:(a + 1) * V]
            nc.vector.scalar_tensor_tensor(out=result[a // 2][:, (a % 2) * V:(a % 2 + 1) * V], in0=piece, scalar=0.0, in1=piece, op0=ALU.max, op1=ALU.mult)
        nc.sync.dma_start(out=out[0:2 * P, :].rearrange("(a t) v -> t a v", t=P), in_=result[0][:].rearrange("p (a v) -> p a v", v=V))
        for a in range(2, TILES):
            nc.sync.dma_start(out=out[a * P:(a + 1) * P, :], in_=result[1][:, (a - 2) * V:(a - 1) * V])
